import numpy as np, ml_dtypes
CORES = [5,29,101,125,133,157,229,253]
N = 8
import mx_ref
BF = ml_dtypes.bfloat16
def cols(t, e):
    v = np.concatenate([t.reshape(128, -1, 4), np.zeros((128, 1, 4), BF)], axis=1)
    return np.ascontiguousarray(v[:, e]).reshape(128, -1)
def pick(q, e):
    c = np.concatenate([q[0].reshape(128, -1, 4), np.zeros((128, 1, 4), np.uint8)], axis=1); s = np.concatenate([q[1], np.ones((16, 1), np.uint8)], axis=1)
    return (np.ascontiguousarray(c[:, e].reshape(128, -1)), np.ascontiguousarray(s[:, e]))
def join(*qs):
    return (np.concatenate([q[0] for q in qs], axis=1), np.concatenate([q[1] for q in qs], axis=1))
def put(q, e, v):
    c, s = q[0].reshape(128, -1, 4).copy(), q[1].copy(); c[:, e] = v[0].reshape(128, -1, 4); s[:, e] = v[1]
    return (c.reshape(128, -1), s)
def pk(c, s):
    return (np.ascontiguousarray(c), mx_ref.live(s))
def emit(q):
    return q[0], q[1]
def decode(q):
    o = []
    for b in range(4):
        e = np.zeros((128, 128, 4), np.float32); e[np.arange(128), np.arange(128), b] = 1
        o.append(mx_ref.matmul(mx_ref.quantize(e.reshape(128, 512).astype(BF)), q))
    return np.stack(o, axis=2).reshape(128, -1)
def f(rng, *shape):
    return mx_ref.flush((rng.standard_normal(shape, dtype=np.float32) * np.exp2(rng.integers(-2, 3, shape[:-1] + (1,)))).astype(BF))
def wide(rng, *shape, cols=0):
    v = rng.standard_normal(shape, dtype=np.float32) * np.exp2(rng.integers(-12, 13, shape)).astype(np.float32)
    if cols: v *= np.repeat(np.exp2(rng.integers(-cols, cols + 1, shape[:-2] + (1, shape[-1] // 4))) * (rng.random(shape[:-2] + (1, shape[-1] // 4)) > 0.0625), 4, axis=-1).astype(np.float32)
    return mx_ref.flush(v.astype(BF))
P, K, O = 96, 32, 1
def big(v):
    v = np.array(v.astype(np.float32))
    v[np.abs(v) < np.float32(2.0 ** -16)] = 0
    return v.astype(BF)
def sized(t, a):
    return big(t.astype(np.float32) * np.repeat(np.asarray(a, np.float32), 4, axis=-1))
def query(rng):
    v = np.zeros((N, 128, 512), BF)
    v[:, :, :4] = f(rng, 1, 128, 4)
    return v
def plain(rng):
    return {"lv": big(f(rng, N, 128, 4 * P)), "dm": big(f(rng, N, 128, 4 * P)), "nz": big(f(rng, N, 128, 4 * P)), "u": query(rng), "z": query(rng), "w": f(rng, N, 128, 512 * O)}
def positive(d):
    return {k: v if k == "w" else np.abs(v.astype(np.float32)).astype(BF) for k, v in d.items()}
def onto(t, e, rng):
    at, far = np.arange(N * P), e[e >= P]
    free = rng.permutation(np.setdiff1d(np.arange(P), e))[:far.size]
    at[free], at[far] = far, free
    return np.stack(np.split(cols(np.concatenate(t, axis=1), at), N, axis=1))
def setup_inputs(rng):
    return plain(rng)
def setup_inputs_ties(rng):
    d = plain(rng)
    for k in ("lv", "dm", "nz"):
        v = big((1 + rng.random((128, 48))) * 2.0 ** 27)
        d[k] = np.stack([big(cols(v, rng.permutation(np.arange(P) % 12)).astype(np.float32) * np.repeat(1 - 2 * rng.integers(0, 2, P), 4)) for r in range(N)])
    for k in ("u", "z"): d[k][:, :, :4] = big((1 + rng.random((1, 128, 4))) * 2.0 ** 29)
    return d
def setup_inputs_one(rng):
    d = positive(plain(rng))
    a, b = rng.permutation(N)[:2]
    g, h = np.ones((N, P)), np.ones((N, P))
    g[a, rng.permutation(P)[:K]] = 2.0 ** -8
    g[b, rng.permutation(P)[:K]] = 2.0 ** -4
    h[b, rng.permutation(P)[:K]] = 2.0 ** 8
    h[a, rng.permutation(P)[:K]] = 2.0 ** 4
    d["lv"], d["dm"] = sized(d["lv"], g[:, None]), sized(d["dm"], h[:, None])
    return d
def setup_inputs_again(rng):
    d = positive(plain(rng))
    n, top = K // N, (np.arange(128) < 64)[None, :, None]
    lt, lb, dt, db, nt = np.ones((5, N, P))
    for r in range(N):
        at, to = rng.permutation(P), rng.permutation(P)
        lt[r, at[:n]], lt[r, at[n:2 * n]] = 2.0 ** -6, 2.0 ** -3
        lb[r, at[:n:2]] = 2.0 ** 8
        nt[r, at[:n // 2]], nt[r, at[n // 2:n]] = 2.0 ** -8, 2.0 ** 4
        dt[r, to[:n]] = 2.0 ** -8
        db[r, to[:n]], db[r, to[n:2 * n]] = 2.0 ** 6, 2.0 ** 3
    d["lv"] = sized(d["lv"], np.where(top, lt[:, None], lb[:, None]))
    d["dm"] = sized(d["dm"], np.where(top, dt[:, None], db[:, None]))
    d["nz"] = sized(d["nz"], np.where(top, nt[:, None], 1.0))
    d["u"], d["z"] = big(d["u"].astype(np.float32) * top), big(d["z"].astype(np.float32) * ~top)
    return d
def setup_inputs_zero(rng):
    d = plain(rng)
    g, h, e = np.ones((3, N, P))
    for r in range(N):
        g[r, rng.permutation(P)[:3 * K // (2 * N)]] = 0
        h[r, rng.permutation(P)[K // (2 * N):]] = 0
        e[r, rng.permutation(P)[:P // 2]] = 0
    d["lv"], d["dm"], d["nz"] = sized(d["lv"], g[:, None]), sized(d["dm"], h[:, None]), sized(d["nz"], e[:, None])
    return d
def setup_inputs_spread(rng):
    d = plain(rng)
    d["lv"] = sized(wide(rng, N, 128, 4 * P), 32 * np.exp2(rng.integers(-6, 7, (N, 1, P))))
    for k in ("dm", "nz"): d[k] = sized(wide(rng, N, 128, 4 * P, cols=6), np.full((1, 1, P), 32.0))
    for k in ("u", "z"): d[k] = sized(d[k], np.full((1, 1, 128), 2.0 ** 24))
    low = np.concatenate([score(d["u"][r], mx_ref.quantize(np.ascontiguousarray(d["lv"][r]))) for r in range(N)])
    high = np.concatenate([score(d["z"][r], mx_ref.quantize(np.ascontiguousarray(d["dm"][r]))) for r in range(N)])
    d["lv"] = onto(d["lv"], np.argsort(low, kind="stable")[:K], rng)
    d["dm"] = onto(d["dm"], np.argsort(-high, kind="stable")[:K], rng)
    return d
def check_inputs(d):
    b = []
    for k, lo, hi in (("lv", -16, 28), ("dm", -16, 28), ("nz", -16, 28), ("u", -30, 30), ("z", -30, 30), ("w", -30, 30)):
        v = np.abs(d[k].astype(np.float32))
        if not (np.isfinite(v).all() and ((v == 0) | (v >= 2.0 ** lo) & (v <= 2.0 ** hi)).all()): b.append("a value of " + k)
    for k in ("u", "z"):
        v = d[k].astype(np.float32)
        if (v[:, :, 4:] != 0).any(): b.append(k + " has numbers behind its column 0")
        if (v != v[:1]).any(): b.append(k + " isn't the same on all ranks")
    return b
def score(t, q):
    return np.abs(mx_ref.matmul(mx_ref.quantize(np.ascontiguousarray(t)), q)[0]) + np.float32(0)
def reference(lv, dm, nz, u, z, w):
    L = [mx_ref.quantize(np.ascontiguousarray(lv[r])) for r in range(N)]
    X = [mx_ref.quantize(np.ascontiguousarray(dm[r])) for r in range(N)]
    noise = join(*[mx_ref.quantize(np.ascontiguousarray(nz[r])) for r in range(N)])
    oc, osc = np.zeros((N, 128, 8 * P), np.uint8), np.zeros((N, 16, 2 * P), np.uint8)
    sw, lw, y = np.zeros((N, 2, K), np.float32), np.zeros((N, 2, K), np.float32), np.zeros((N, 128, O * P), np.float32)
    for t in range(2):
        low = np.argsort(np.concatenate([score(u[r], L[r]) for r in range(N)]), kind="stable")[:K]
        high = np.argsort(-np.concatenate([score(z[r], X[r]) for r in range(N)]), kind="stable")[:K]
        lw[:, t], sw[:, t] = low, high
        gone, come = pick(join(*L), low), pick(join(*X), high)
        v = decode(come) * np.float32(0.5) + decode(pick(noise, low)) * np.float32(0.5)
        new = mx_ref.quantize(np.ascontiguousarray(v.astype(BF)))
        for r in range(N):
            a, b = np.flatnonzero(low // P == r), np.flatnonzero(high // P == r)
            L[r] = put(L[r], low[a] - P * r, pick(new, a))
            X[r] = put(X[r], high[b] - P * r, pick(gone, b))
    for r in range(N):
        oc[r], osc[r] = emit(join(L[r], X[r]))
        for o in range(O):
            y[r, :, P * o:P * o + P] = mx_ref.matmul(mx_ref.quantize(np.ascontiguousarray(w[r][:, 512 * o:512 * o + 512])), L[r])
    return {"oc": oc, "osc": osc, "sw": sw, "lw": lw, "y": y}

@@ -1,0 +1,661 @@
+import numpy as np
+from concourse.bass import DstId, RemoteDMATransfer
+from concourse.mybir import dt, AluOpType, AxisListType, ActivationFunctionType
+
+O = AluOpType
+AF = ActivationFunctionType
+P = 96
+F32, BF, I32, U16 = "float32", "bfloat16", "int32", "uint16"
+SCRATCH = {
+    "BT": ("sbuf", [128, 1152], BF), "WT": ("sbuf", [128, 512], BF), "UZ": ("sbuf", [128, 8], BF),
+    "UT": ("sbuf", [128, 512], BF), "ZT": ("sbuf", [128, 512], BF), "ONB": ("sbuf", [128, 128], BF),
+    "HAF": ("sbuf", [128, 128], BF), "DG": ("sbuf", [128, 128], BF), "ET": ("sbuf", [128, 2048], BF),
+    "NT0": ("sbuf", [128, 512], BF), "NT1": ("sbuf", [128, 512], BF),
+    "PI": ("sbuf", [128, 1], I32), "PJ": ("sbuf", [128, 3], I32), "MI": ("sbuf", [128, 3], I32),
+    "DPo": ("sbuf", [128, 2], U16), "LPo": ("sbuf", [128, 2], U16), "Mo": ("sbuf", [128, 6], U16),
+    "X2o": ("sbuf", [128, 6], U16), "B2o": ("sbuf", [128, 2], U16), "N2o": ("sbuf", [128, 2], U16),
+    "FLo": ("sbuf", [128, 8], U16), "FDo": ("sbuf", [128, 6], U16), "GI": ("sbuf", [128, 4], I32), "GJ": ("sbuf", [128, 4], I32),
+    "GK": ("sbuf", [128, 4], I32),
+}
+for _n, _w in {"QT": 544, "UQ": 128, "ZQ": 128, "EQ": 512, "WQ": 128, "SL1": 32, "LD1": 32, "MG1": 16, "UD": 128, "SL2": 96,
+               "LD2": 96, "MG2": 16, "LD3": 32, "MG3": 16, "DW": 224, "NP1": 128, "BP2": 128, "NP2": 128, "LF": 128, "DF": 96}.items():
+    SCRATCH[_n] = ("sbuf", [128, _w], "float8_e4m3fn_x4")
+    SCRATCH[_n + "s"] = ("sbuf", [128, _w], "uint8")
+for _x, _n in ((1, 4), (2, 12), (3, 4)):
+    SCRATCH["RC%d" % _x] = ("sbuf", [128, 4 * _n], "float8_e4m3fn_x4")
+    SCRATCH["RC%ds" % _x] = ("sbuf", [128, 4 * _n], "uint8")
+    SCRATCH["RW%d" % _x] = ("sbuf", [128, _n], "float8_e4m3fn_x4")
+    SCRATCH["RW%ds" % _x] = ("sbuf", [128, _n], "uint8")
+_F = {"RS1": 3, "RS2": 1, "SD": 32, "NK": 32, "ON": 32, "ROW": 192, "R96": 96, "PC": 8, "LC": 1, "TL": 32, "CT": 416,
+      "FT": 96, "FK": 96, "S8": 8, "JB": 6, "PT": 192, "K0": 192, "KK": 192, "TT": 192, "KF": 96, "TF": 96, "CL": 288, "RB": 4,
+      "HL": 288, "HT": 288, "EA": 256, "RA": 256, "CA": 1792, "CN": 8, "H1": 64, "H1t": 64, "OL": 2,
+      "SWK": 8, "EB": 256, "RBW": 256, "CB": 1792, "CBN": 8, "CF": 8, "VO": 2, "H2": 192, "H2t": 192, "OX": 6, "XO": 24, "XP": 18,
+      "GID": 8, "OW": 4, "HB": 1024, "SB": 1024, "LB": 4, "XB": 16, "SX": 8, "MM": 96, "MW": 384, "MV": 384, "OM": 6,
+      "SC": 32, "NS": 4, "FM": 12, "FH": 768, "FR": 24, "FL": 6, "FD": 6, "Y": 96, "G4": 8, "G4t": 64, "NB": 1,
+      "FT0": 192, "FT1": 192, "FT2": 192, "FT3": 192}
+for _n, _w in (("EP", 128), ("EQr", 128), ("MK", 128), ("MG", 192), ("MT", 512), ("MH", 640), ("ML", 16)):
+    _F[_n] = _F[_n + "b"] = _w
+_AT, _o = {}, 0
+for _n, _w in _F.items():
+    if _n in ("RS1", "RS2", "SD", "NK", "Y", "G4t"):
+        SCRATCH["f" + _n] = ("sbuf", [128, _w], F32)
+    else:
+        _AT["f" + _n] = (_o, _w)
+        _o += -(-_w // 32) * 32
+SCRATCH["fW"] = ("sbuf", [128, _o], F32)
+for _i in range(8):
+    SCRATCH["p%d" % _i] = ("psum", [128, 512], F32)
+SEMAPHORES = ["vs", "ac", "te", "gp", "ls", "sa1", "sa2", "sr1", "sr2"]
+for _x in (1, 2, 3):
+    SEMAPHORES += ["a%d" % _x, "b%d" % _x, "qc%d" % _x, "qs%d" % _x, "wc%d" % _x, "ws%d" % _x]
+SEMAPHORES += ["d%d" % _i for _i in range(60)]
+NX = {1: 4, 2: 12, 3: 4}
+LAND = {1: ("UD", 0), 2: ("DW", 96), 3: ("DW", 192)}
+
+
+def _layout(T, topo):
+    ranks = T.cores
+    a = [r for r in range(8) if r == 0 or topo.same_plane(ranks[0], ranks[r])]
+    b = [r for r in range(8) if r not in a]
+    return a, b
+
+
+def _helpers(home, far, topo):
+    h = [c for c in topo.cores_of(home) if c != home and topo.may_write(c, far)]
+    return sorted(h, key=lambda c: (topo.die(c) != topo.die(home), c))
+
+
+def _remote(g, T, topo, core, moves, sem):
+    tr = []
+    for src, dsts, eng in moves:
+        ids = []
+        for c, _ in dsts:
+            rid, pid = topo.addr(c, core)
+            ids.append(DstId(rid=rid, pnc=pid))
+        m = 0
+        for e in eng:
+            m |= 1 << e
+        tr.append(RemoteDMATransfer(dst_ids=ids, dma_engine_mask=m, remote_sem=T.sem[sem], srcs=[src], dsts=[d for _, d in dsts]))
+    g.remote_dma_fused(tr, local_sem=T.sem.ls)
+    return sum(len(e) for _, _, e in moves)
+
+
+def _codes(T, name, a, b):
+    return T[name][:, a:b].bitcast(dt.uint8)
+
+
+def _hand_on(g, core, T, topo, rank, far):
+    home = T.cores[rank]
+    hs = _helpers(home, T.cores[far[0]], topo)
+    if core not in hs:
+        return
+    me, ls = hs.index(core), 0
+    eng = topo.engines(core, T.cores[far[0]])
+    n_on = len(topo.engines(home, core)) - len(eng)
+    a, b = _layout(T, topo)
+    pos = (a + b).index(rank)
+
+    def scores(k, w):
+        g.wait_ge(T.sem["sr%d" % k], n_on)
+        dst = "fSD" if k == 1 else "fNK"
+        return _remote(g, T, topo, core, [(T["fRS%d" % k][:], [(T.cores[r], T[dst][:, 4 * rank:4 * rank + w]) for r in far], eng)], "sa%d" % k)
+
+    def first(x, codes):
+        n = NX[x]
+        g.wait_ge(T.sem[("qc%d" if codes else "qs%d") % x], n_on)
+        mv = []
+        for i, r in enumerate(far):
+            e = eng[2 * i:2 * i + 2]
+            if codes:
+                mv.append((_codes(T, "RC%d" % x, n * i, n * i + n), [(T.cores[r], _codes(T, "LD%d" % x, n * rank, n * rank + n))], e))
+            else:
+                mv.append((T["RC%ds" % x][:, n * i:n * i + n], [(T.cores[r], T["LD%ds" % x][:, n * rank:n * rank + n])], e))
+        return _remote(g, T, topo, core, mv, "a%d" % x)
+
+    def second(x, codes):
+        n = NX[x]
+        nm, base = LAND[x]
+        base += n * pos
+        g.wait_ge(T.sem[("wc%d" if codes else "ws%d") % x], n_on)
+        if codes:
+            mv = [(_codes(T, "RW%d" % x, 0, n), [(T.cores[r], _codes(T, nm, base, base + n)) for r in far], eng)]
+        else:
+            mv = [(T["RW%ds" % x][:], [(T.cores[r], T[nm + "s"][:, base:base + n]) for r in far], eng)]
+        return _remote(g, T, topo, core, mv, "b%d" % x)
+
+    if me == 0:
+        ls += scores(1, 3) + scores(2, 1)
+    elif me in (1, 2):
+        for x in (1, 3):
+            ls += first(x, me == 1)
+            ls += second(x, me == 1)
+    else:
+        for f in (first, second):
+            ls += f(2, True)
+            ls += f(2, False)
+    g.wait_ge(T.sem.ls, ls)
+
+
+def rank_program(g, core, T, topo):
+    rank = T.rank_of(core)
+    pa, pb = _layout(T, topo)
+    if rank is None:
+        for r in range(8):
+            if core in topo.cores_of(T.cores[r]):
+                _hand_on(g, core, T, topo, r, pb if r in pa else pa)
+        return
+    far = pb if rank in pa else pa
+    near = [r for r in (pa if rank in pa else pb) if r != rank]
+    order = pa + pb
+    m = order.index(rank)
+    m0 = order.index(far[0])
+    hs = _helpers(core, T.cores[far[0]], topo)
+    e_off = topo.engines(core, T.cores[near[0]])
+    e_on = [e for e in topo.engines(core, hs[0]) if e not in e_off]
+    me = rank
+
+    Q = {"v": g.vector, "a": g.scalar, "t": g.tensor, "g": g, "y": g.sync}
+    SEM = {"v": "vs", "a": "ac", "t": "te", "g": "gp"}
+    acc, waited, know, cnt = {}, {q: {} for q in Q}, {}, {}
+    nd = [0]
+
+    def X(name, c0=0, c1=None, r0=0, r1=128, st=1):
+        o, w = _AT[name] if name in _AT else (0, SCRATCH[name][1][1])
+        return ("fW" if name in _AT else name, o + c0, o + (w if c1 is None else c1), r0, r1, st)
+
+    def ap(v):
+        n, c0, c1, r0, r1, st = v
+        if (r0, r1) == (0, 128):
+            return T[n][:, c0:c1] if st == 1 else T[n][:, c0:c1:st]
+        return T[n][r0:r1, c0:c1] if st == 1 else T[n][r0:r1, c0:c1:st]
+
+    def hit(a, b):
+        if a[4] <= b[3] or b[4] <= a[3] or a[2] <= b[1] or b[2] <= a[1]:
+            return False
+        return not (a[5] == b[5] > 1 and (a[1] - b[1]) % a[5])
+
+    def norm(v):
+        return (v[0], 0, 512, 0, 128, 1) if SCRATCH[v[0]][0] == "psum" else v
+
+    def pre(q, reads, writes):
+        need = {}
+        for vs, w in ((reads, False), (writes, True)):
+            for v in vs:
+                ps = SCRATCH[v[0]][0] == "psum"
+                for r, iw, ev, eq in acc.get(v[0], []):
+                    if (iw or w or (ps and eq != q)) and hit(r, norm(v)):
+                        if ps and q == "t" and eq == "t" and w:
+                            continue
+                        need[ev[0]] = max(need.get(ev[0], 0), ev[1])
+        for s in sorted(need, key=lambda s: (s in ("vs", "ac", "te"), s)):
+            if waited[q].get(s, 0) < need[s]:
+                Q[q].wait_ge(T.sem[s], need[s])
+                for s2, n2 in know.get((s, need[s]), {}).items():
+                    waited[q][s2] = max(waited[q].get(s2, 0), n2)
+                waited[q][s] = need[s]
+
+    def post(q, reads, writes, ev):
+        know[ev] = dict(waited[q])
+        for v in writes:
+            nv = norm(v)
+            acc[v[0]] = [e for e in acc.get(v[0], []) if not (nv[1] <= e[0][1] and e[0][2] <= nv[2] and nv[3] <= e[0][3] and e[0][4] <= nv[4] and nv[5] == 1)]
+            acc[v[0]].append((nv, True, ev, q))
+        for v in reads:
+            acc.setdefault(v[0], []).append((norm(v), False, ev, q))
+
+    def op(q, call, reads, writes):
+        pre(q, reads, writes)
+        s = SEM[q]
+        if q == "g" and waited[q].get(s, 0) < cnt.get(s, 0):
+            g.wait_ge(T.sem[s], cnt[s])
+            waited[q][s] = cnt[s]
+        i = call()
+        cnt[s] = cnt.get(s, 0) + 1
+        i.then_inc(T.sem[s], 1)
+        post(q, reads, writes, (s, cnt[s]))
+
+    def dma(q, out, in_, reads=(), writes=()):
+        pre(q, reads, writes)
+        s = "d%d" % nd[0]
+        nd[0] += 1
+        Q[q].dma_start(out, in_).then_inc(T.sem[s], 16)
+        cnt[s] = 16
+        post(q, reads, writes, (s, 16))
+
+    def dcol(q, dst, d0, src, s0, n):
+        dma(q, _codes(T, dst, d0, d0 + n), _codes(T, src, s0, s0 + n), [X(src, s0, s0 + n)], [X(dst, d0, d0 + n)])
+        dma(q, T[dst + "s"][:, d0:d0 + n], T[src + "s"][:, s0:s0 + n], [X(src + "s", s0, s0 + n)], [X(dst + "s", d0, d0 + n)])
+
+    def arrive(views, sem, total):
+        cnt[sem] = total
+        for v in views:
+            acc.setdefault(v[0], []).append((v, True, (sem, total), "r"))
+
+    def sc(s):
+        return (ap(s), [s]) if isinstance(s, tuple) else (s, [])
+
+    def ts(out, a, s1, op0, s2=None, op1=None):
+        p1, r1 = sc(s1)
+        p2, r2 = sc(s2)
+        if op1 is None:
+            op("v", lambda: g.vector.tensor_scalar(ap(out), ap(a), p1, None, op0), [a] + r1, [out])
+        else:
+            op("v", lambda: g.vector.tensor_scalar(ap(out), ap(a), p1, p2, op0, op1), [a] + r1 + r2, [out])
+
+    def tt(out, a, b, o):
+        op("v", lambda: g.vector.tensor_tensor(ap(out), ap(a), ap(b), o), [a, b], [out])
+
+    def cp(out, a):
+        op("v", lambda: g.vector.tensor_copy(ap(out), ap(a)), [a], [out])
+
+    def red(out, a, o=O.add, neg=False, ab=False):
+        op("v", lambda: g.vector.tensor_reduce(ap(out), ap(a), AxisListType.X, o, negate=neg, apply_absolute_value=ab), [a], [out])
+
+    def tr(out, a):
+        op("v", lambda: g.vector.transpose(ap(out), ap(a)), [a], [out])
+
+    def ms(out, c):
+        op("v", lambda: g.vector.memset(ap(out), c), [], [out])
+
+    def act(out, a, func=AF.Copy, scale=1.0):
+        p, r = sc(scale)
+        op("a", lambda: g.scalar.activation(ap(out), ap(a), func, scale=p), [a] + r, [out])
+
+    def accum(out, a):
+        op("a", lambda: g.scalar.activation(ap(a), ap(a), AF.Copy, accum_out=ap(out)), [a], [a, out])
+
+    def iota(out, pat, base, cm=0):
+        if SCRATCH[out[0]][2] == I32:
+            op("g", lambda: g.iota(ap(out), pat, base, cm), [], [out])
+        else:
+            op("g", lambda: g.iota(ap(out), pat, base, cm, allow_small_or_imprecise_dtypes=True), [], [out])
+
+    def quant(dst, d0, d1, src, s0, s1):
+        op("v", lambda: g.vector.quantize_mx(T[dst][:, d0:d1], T[dst + "s"][:, d0:d1], T[src][:, s0:s1]), [X(src, s0, s1)], [X(dst, d0, d1), X(dst + "s", d0, d1)])
+
+    def mm(bank, n, l, l0, r, r0, start=True, stop=True):
+        op("t", lambda: g.tensor.matmul_mx(T[bank][:, 0:n], T[l][:, l0:l0 + 128], T[l + "s"][:, l0:l0 + 128], T[r][:, r0:r0 + n], T[r + "s"][:, r0:r0 + n], start, stop),
+           [X(l, l0, l0 + 128), X(l + "s", l0, l0 + 128), X(r, r0, r0 + n), X(r + "s", r0, r0 + n)], [X(bank, 0, n)])
+
+    def pick(dst, n, win, a, b, off):
+        ov = X(off[0], off[1], off[1] + n // 16)
+        op("a", lambda: g.scalar.activation(T[dst + "s"][:, 0:n], T[win + "s"][:, a:b].indirect(ap(ov)), AF.Copy), [X(win + "s", a, b), ov], [X(dst + "s", 0, n)])
+        op("v", lambda: g.vector.tensor_copy(T[dst][:, 0:n].bitcast(dt.uint32), T[win][:, a:b].bitcast(dt.uint32).indirect(ap(ov))), [X(win, a, b), ov], [X(dst, 0, n)])
+
+    ls = [0]
+
+    def send(moves, sem, reads):
+        pre("g", reads, [])
+        ls[0] += _remote(g, T, topo, core, moves, sem)
+
+    def send1(x, src, s0):
+        n = NX[x]
+        p, ps = s0 + n * m0, src + "s"
+        send([(_codes(T, src, p, p + 4 * n), [(hs[3 if x == 2 else 1], _codes(T, "RC%d" % x, 0, 4 * n))], e_on)], "qc%d" % x, [X(src, p, p + 4 * n)])
+        send([(T[ps][:, p:p + 4 * n], [(hs[3 if x == 2 else 2], T["RC%ds" % x][:])], e_on)], "qs%d" % x, [X(ps, p, p + 4 * n)])
+        mc, mp, rd, rp = [], [], [], []
+        for i, r in enumerate(near):
+            c = s0 + n * order.index(r)
+            e = e_off[2 * i:2 * i + 2]
+            mc.append((_codes(T, src, c, c + n), [(T.cores[r], _codes(T, "LD%d" % x, n * me, n * me + n))], e))
+            mp.append((T[ps][:, c:c + n], [(T.cores[r], T["LD%ds" % x][:, n * me:n * me + n])], e))
+            rd.append(X(src, c, c + n))
+            rp.append(X(ps, c, c + n))
+        send(mc, "a%d" % x, rd)
+        send(mp, "a%d" % x, rp)
+        dcol("y", "LD%d" % x, n * me, src, s0 + n * m, n)
+        oth = [X(k, n * r, n * r + n) for k in ("LD%d" % x, "LD%ds" % x) for r in range(8) if r != me]
+        arrive(oth, "a%d" % x, 4 * 7)
+
+    def send2(x):
+        n = NX[x]
+        nm, base = LAND[x]
+        c = base + n * m
+        src = "MG%d" % x
+        for s, hc, h, k in ((src, "RW%d" % x, hs[3 if x == 2 else 1], "wc%d"), (src + "s", "RW%ds" % x, hs[3 if x == 2 else 2], "ws%d")):
+            pre("g", [X(s, 0, n)], [])
+            code = s == src
+            sap = _codes(T, s, 0, n) if code else T[s][:, 0:n]
+            dap = _codes(T, nm, c, c + n) if code else T[nm + "s"][:, c:c + n]
+            hap = _codes(T, hc, 0, n) if code else T[hc][:]
+            for mv, sem in ([(sap, [(h, hap)], e_on)], k % x), ([(sap, [(T.cores[r], dap) for r in near], e_off)], "b%d" % x):
+                ls[0] += _remote(g, T, topo, core, mv, sem)
+        dcol("y", nm, c, src, 0, n)
+        oth = [X(k, base + n * order.index(r), base + n * order.index(r) + n) for k in (nm, nm + "s") for r in range(8) if r != me]
+        arrive(oth, "b%d" % x, 7 * 2 * len(e_off))
+
+    def send_scores(k, src, c0, w):
+        sap = T[src][:, c0:c0 + w]
+        pre("g", [X(src, c0, c0 + w)], [])
+        ls[0] += _remote(g, T, topo, core, [(sap, [(hs[0], T["fRS%d" % k][:])], e_on)], "sr%d" % k)
+        ls[0] += _remote(g, T, topo, core, [(sap, [(T.cores[r], T[src][:, c0:c0 + w]) for r in near], e_off)], "sa%d" % k)
+        arrive([X(src, 4 * r, 4 * r + w) for r in range(8) if r != me], "sa%d" % k, 7 * len(e_off))
+
+    def load(q, buf, c0, c1, ext):
+        dma(q, T[buf][:, c0:c1], ext, [], [X(buf, c0, c1)])
+
+    load("y", "BT", 384, 768, T.dm[:])
+    load("a", "BT", 0, 384, T.lv[:])
+    load("y", "UZ", 4, 8, T.z[:, 0:4])
+    load("a", "UZ", 0, 4, T.u[:, 0:4])
+    load("y", "BT", 768, 1152, T.nz[:])
+    load("a", "WT", 0, 512, T.w[:])
+    iota(X("PI"), [[1, 1]], 0, 1)
+    iota(X("fR96"), [[0, 3], [1, 32]], 0)
+    iota(X("fROW"), [[16, 6], [0, 2], [1, 16]], 0)
+    CT = lambda a, b, r0=0, r1=128: X("fCT", a, b, r0, r1)
+    iota(CT(96, 128), [[0, 8], [1, 4]], 4 * m)
+    iota(X("fS8"), [[128, 8]], 0)
+    iota(X("fJB"), [[16, 6]], 0)
+    ms(X("ONB"), 1.0)
+    ms(X("fON"), 1.0)
+    ms(X("HAF"), 0.5)
+    ms(CT(192, 320, 0, 64), -1000.0)
+    ms(CT(320, 384, 64, 128), -1000.0)
+    op("g", lambda: g.affine_select(T.DG[:], T.HAF[:], [[-1, 128]], O.is_equal, 0.0, 0, 1), [X("HAF")], [X("DG")])
+    for i, k in enumerate((31, 15, 3)):
+        op("v", lambda k=k, i=i: g.vector.tensor_scalar(T.PJ[:, i:i + 1], T.PI[:], k, None, O.bitwise_and), [X("PI")], [X("PJ", i, i + 1)])
+    cp(X("fPC", 0, 3), X("PJ"))
+    P32, P16, P4 = X("fPC", 0, 1), X("fPC", 1, 2), X("fPC", 2, 3)
+    for a in range(4):
+        ts(X("fLC", 0, 1, 32 * a, 32 * a + 32), X("fPC", 0, 1, 32 * a, 32 * a + 32), 32.0 * (a % 2), O.add)
+    ts(X("fTL"), X("fR96", 0, 32), X("fLC"), O.add, P32, O.subtract)
+    step = 2.0 ** -24
+    ms(X("fFT", 0, 96, 64, 128), 1.0)
+    ms(X("fFK", 0, 96, 0, 64), 1.0)
+    for n, r0 in (("fFT", 0), ("fFK", 64)):
+        v = X(n, 0, 96, r0, r0 + 64)
+        ts(v, X("fR96", 0, 96, r0, r0 + 64), X("fPC", 0, 1, r0, r0 + 64), O.is_lt, -step, O.mult)
+        ts(v, v, 1.0, O.add)
+    for b in range(3):
+        ts(X("fPC", 3 + b, 4 + b), P32, 32.0 * b, O.add)
+    for nm, c, q in (("ZT", 4, "ZQ"), ("UT", 0, "UQ")):
+        for t in range(4):
+            ts(X(nm, t, 512, 0, 128, 4), X("ONB"), X("UZ", c + t, c + t + 1), O.mult)
+        quant(q, 0, 128, nm, 0, 512)
+    quant("QT", 0, 288, "BT", 0, 1152)
+    mm("p0", 192, "ZQ", 0, "QT", 0)
+    mm("p1", 128, "UQ", 0, "QT", 0)
+    act(X("fK0", 0, 96, 0, 64), X("p0", 96, 192, 0, 64), AF.Abs)
+    act(X("fK0", 0, 96, 64, 128), X("p1", 0, 96, 64, 128), AF.Abs)
+    act(X("fK0", 96, 192), X("p0", 0, 96), AF.Abs)
+    low = 2.0 ** -110
+    ts(X("fKK", 0, 96, 0, 64), X("fK0", 0, 96, 0, 64), low, O.max)
+    ts(X("fKK", 0, 96, 64, 128), X("fK0", 0, 96, 64, 128), -1.0, O.mult, -low, O.min)
+    ts(X("fKK", 96, 192), X("fK0", 96, 192), low, O.max)
+    tr(X("fTT"), X("fKK"))
+    tt(X("fKF"), X("fKK", 0, 96), X("fFK"), O.mult)
+    tt(X("fTF"), X("fTT", 0, 96), X("fFT"), O.mult)
+    for b in range(3):
+        s = X("fTT", 32 * b, 32 * b + 1)
+        if b:
+            ts(X("fCL", 96 * b, 96 * b + 32 * b), X("fKK", 0, 32 * b), s, O.is_ge)
+        if b < 2:
+            ts(X("fCL", 96 * b + 32 * b + 32, 96 * b + 96), X("fKK", 32 * b + 32, 96), s, O.is_gt)
+        tt(X("fCL", 128 * b, 128 * b + 32), X("fKF", 32 * b, 32 * b + 32), X("fTF", 32 * b, 32 * b + 32), O.is_gt)
+    for b in range(3):
+        red(X("fRB", b, b + 1), X("fCL", 96 * b, 96 * b + 96))
+    for i, val in enumerate((lambda b: X("fTT", 32 * b, 32 * b + 1), lambda b: X("fPC", 3 + b, 4 + b), lambda b: X("fTT", 96 + 32 * b, 97 + 32 * b))):
+        for b in range(3):
+            ts(X("fHL", 96 * i + 32 * b, 96 * i + 32 * b + 32), X("fTL"), X("fRB", b, b + 1), O.is_equal, val(b), O.mult)
+    tr(X("fHT"), X("fHL"))
+    for i in range(3):
+        red(X("fSD", 4 * me + i, 4 * me + i + 1), X("fHT", 96 * i, 96 * i + 96))
+    send_scores(1, "fSD", 4 * me, 3)
+
+    LCv = X("fLC")
+    ts(CT(0, 64), X("fROW", 0, 64), LCv, O.subtract)
+    ts(CT(64, 96), X("fR96", 0, 32), LCv, O.subtract)
+    ts(CT(128, 160), X("fR96", 0, 32), LCv, O.subtract, 32.0, O.add)
+    ts(CT(96, 128), CT(96, 128), P32, O.is_equal)
+    ts(CT(384, 416), X("fROW", 0, 32), 12.0, O.is_ge, -1000.0, O.mult)
+    tt(CT(160, 192), CT(384, 416), X("fROW", 0, 32), O.add)
+    for i in range(3):
+        ts(X("fMM", 32 * i, 32 * i + 32), CT(160, 192), 12.0 * m - 32.0 * i, O.add, P32, O.is_equal)
+    ts(CT(192, 320, 64, 128), X("fROW", 0, 128, 64, 128), X("fLC", 0, 1, 64, 128), O.subtract)
+    ts(CT(320, 384, 0, 64), X("fROW", 0, 64, 0, 64), X("fLC", 0, 1, 0, 64), O.subtract, 32.0, O.add)
+    ts(X("fPT"), X("fROW"), 128.0 * me, O.add)
+    ts(X("fJB"), X("fJB"), P16, O.add)
+    ms(X("fVO", 0, 1, 0, 64), 96.0)
+    ms(X("fVO", 0, 1, 64, 128), 0.0)
+    ms(X("ET"), 0.0)
+    for b in range(4):
+        cp(X("ET", 513 * b, 512 * b + 512, 0, 128, 4), X("DG"))
+    quant("EQ", 0, 512, "ET", 0, 2048)
+    quant("WQ", 0, 128, "WT", 0, 512)
+    ms(X("FLo", 6, 8), 0)
+    for d in ("UD", "NP1", "BP2", "NP2"):
+        dcol("y", d, 32, "QT", 0, 96)
+    dcol("y", "DW", 0, "QT", 96, 96)
+
+    def key(s):
+        return X("fSD", 4 * s, 4 * s + 1)
+
+    def expand(e, col, rows):
+        for s in range(8):
+            if s % 2:
+                act(X(e, 32 * s, 32 * s + 32), X("fON"), AF.Copy, col(s))
+            else:
+                ts(X(e, 32 * s, 32 * s + 32), X("fON"), col(s), O.mult)
+        tr(X(rows), X(e))
+
+    def compare(buf, rows, s):
+        if s:
+            ts(X(buf, 224 * s, 224 * s + 32 * s), X(rows, 0, 32 * s), key(s), O.is_ge)
+        if s < 7:
+            ts(X(buf, 224 * s + 32 * s, 224 * s + 224), X(rows, 32 * s + 32, 256), key(s), O.is_gt)
+        return X(buf, 224 * s, 224 * s + 224)
+
+    def rows4(v, a):
+        return (v[0], v[1], v[2], 32 * a, 32 * a + 32, v[5])
+
+    def to_all(out, src, a):
+        for d in range(4):
+            if d % 2 and SCRATCH[out[0]][2] == F32:
+                act(rows4(out, d), rows4(src, a))
+            else:
+                cp(rows4(out, d), rows4(src, a))
+
+    expand("fEA", key, "fRA")
+    red(X("fCN", me, me + 1), compare("fCA", "fRA", me))
+    ts(X("fH1"), CT(0, 64), X("fCN", me, me + 1), O.is_equal, X("fSD", 4 * me + 1, 4 * me + 2), O.mult)
+    tr(X("fH1t"), X("fH1"))
+    red(X("fOL", 0, 1), X("fH1t", 0, 32))
+    red(X("fOL", 1, 2), X("fH1t", 32, 64))
+    to_all(X("DPo"), X("fOL"), 0)
+    pick("SL1", 32, "QT", 96, 192, ("DPo", 0))
+    send1(1, "SL1", 0)
+
+    others = [s for s in range(8) if s != me]
+    for s in others:
+        accum(X("fCN", s, s + 1), compare("fCA", "fRA", s))
+
+    def listed(k, tgt, cn, val, out):
+        for s in range(8):
+            ts(X("fHB", 256 * k + 32 * s, 256 * k + 32 * s + 32), tgt, X(cn, s, s + 1), O.is_equal, val(s), O.mult)
+        tr(X("fSB", 256 * k, 256 * k + 256), X("fHB", 256 * k, 256 * k + 256))
+        accum(out, X("fSB", 256 * k, 256 * k + 256))
+
+    def owners(parts, mul, add, i):
+        n = len(parts)
+        for j, (mask, col) in enumerate(parts):
+            ts(X("fMW", 128 * i + 32 * j, 128 * i + 32 * j + 32), mask, col, O.mult)
+        tr(X("fMV", 128 * i, 128 * i + 32 * n), X("fMW", 128 * i, 128 * i + 32 * n))
+        red(X("fOM", 2 * i, 2 * i + 1), X("fMV", 128 * i, 128 * i + 32 * n))
+        ts(X("fOM", 2 * i + 1, 2 * i + 2), X("fOM", 2 * i, 2 * i + 1), 63.5, O.subtract, 1.0 / 128, O.mult)
+        cp(X("MI", i, i + 1), X("fOM", 2 * i + 1, 2 * i + 2))
+        ts(X("Mo", 2 * i, 2 * i + 1), X("MI", i, i + 1), float(mul), O.mult, add, O.add)
+
+    tt(X("fGID"), ("fSD", 1, 32, 0, 128, 4), X("fS8"), O.add)
+    gid = lambda s: X("fGID", s, s + 1)
+    listed(0, CT(64, 96), "fCN", gid, X("fG4", 4, 5))
+    L1g, L2g, D1g, H2g = (X("fG4", i, i + 1) for i in range(4))
+    to_all(D1g, X("fG4", 4, 5), 0)
+    owners([(CT(96, 128), D1g)], 4, P4, 0)
+
+    for a in range(4):
+        src = ("fSD", 0, 32, 32 * (a ^ 1), 32 * (a ^ 1) + 32, 4)
+        (act if a % 2 else cp)(X("fSWK", 0, 8, 32 * a, 32 * a + 32), src)
+    expand("fEB", lambda s: X("fSWK", s, s + 1), "fRBW")
+    red(X("fCBN", me, me + 1), compare("fCB", "fRBW", me))
+    tt(X("fCF", me, me + 1), X("fCN", me, me + 1), X("fCBN", me, me + 1), O.add)
+    tt(X("fVO", 1, 2), X("fVO", 0, 1), X("fSD", 4 * me + 1, 4 * me + 2), O.add)
+    ts(X("fH2"), CT(192, 384), X("fCF", me, me + 1), O.is_equal, X("fVO", 1, 2), O.mult)
+    tr(X("fH2t"), X("fH2"))
+    for c in range(6):
+        (accum if c % 2 else red)(X("fOX", c, c + 1), X("fH2t", 32 * c, 32 * c + 32))
+    pick("MG1", 16, "LD1", 0, 32, ("Mo", 0))
+    send2(1)
+    for a in range(4):
+        to_all(X("fXO", 6 * a, 6 * a + 6), X("fOX"), a)
+    tt(X("fXP", 0, 12), X("fXO", 0, 12), X("fXO", 12, 24), O.add)
+    tt(X("fXP", 12, 18), X("fXP", 0, 6), X("fXP", 6, 12), O.add)
+    cp(X("X2o"), X("fXP", 12, 18))
+    pick("SL2", 96, "QT", 0, 192, ("X2o", 0))
+    send1(2, "SL2", 0)
+
+    to_all(X("LPo"), X("fOL"), 2)
+    pick("NP1", 32, "QT", 192, 288, ("LPo", 0))
+    for b in range(4):
+        mm("p%d" % (2 + b), 128, "EQ", 128 * b, "NP1", 0, True, False)
+    to_all(L1g, X("fG4", 4, 5), 2)
+    ts(X("fOW", 0, 1), L1g, 128.0 * me, O.is_ge)
+    ts(X("fOW", 1, 2), L1g, 128.0 * me + 128, O.is_lt)
+    tt(X("fOW", 2, 3), X("fOW", 0, 1), X("fOW", 1, 2), O.mult)
+    for s in others:
+        accum(X("fCBN", s, s + 1), compare("fCB", "fRBW", s))
+    tt(X("fCF"), X("fCN"), X("fCBN"), O.add)
+    listed(1, CT(128, 160), "fCF", gid, X("fLB", 0, 1))
+    listed(2, CT(128, 160), "fCF", key, X("fLB", 1, 2))
+    listed(3, CT(64, 96), "fCF", lambda s: X("fSD", 4 * s + 2, 4 * s + 3), X("fLB", 2, 3))
+    for a in range(4):
+        to_all(X("fXB", 4 * a, 4 * a + 3), X("fLB", 0, 3), a)
+    tt(X("fSX", 0, 3), X("fXB", 0, 3), X("fXB", 4, 7), O.add)
+    tt(X("fSX", 4, 7), X("fXB", 8, 11), X("fXB", 12, 15), O.add)
+    c2g, c2k, o2g, o2k, z1 = X("fSX", 0, 1), X("fSX", 1, 2), X("fSX", 4, 5), X("fSX", 5, 6), X("fSX", 6, 7)
+    owners([(X("fMM", 32 * i, 32 * i + 32), c) for i, c in enumerate((L1g, o2g, c2g)) if 12 * m < 32 * i + 32 and 12 * m + 12 > 32 * i], 12, P16, 2)
+    owners([(CT(96, 128), L1g)], 4, P4, 1)
+
+    def new(nt, q0):
+        for b in range(4):
+            o = X(nt, b, 512, 0, 128, 4)
+            if b < 2:
+                cp(o, X("p%d" % (2 + b), 0, 128))
+            else:
+                act(o, X("p%d" % (2 + b), 0, 128))
+        quant("QT", q0, q0 + 128, nt, 0, 512)
+
+    for b in range(4):
+        mm("p%d" % (2 + b), 128, "EQ", 128 * b, "UD", 0, False, True)
+    new("NT0", 288)
+    mm("p6", 128, "UQ", 0, "QT", 288)
+    tr(X("fSC"), X("p6", 0, 32))
+    red(X("fNS", 0, 1), X("fSC", 0, 1), O.add, True, True)
+    tt(X("fNK", 4 * me, 4 * me + 1), X("fNS", 0, 1), X("fOW", 2, 3), O.mult)
+    send_scores(2, "fNK", 4 * me, 1)
+    send1(3, "QT", 288)
+    pick("MG2", 16, "LD2", 0, 96, ("Mo", 4))
+    send2(2)
+
+    tiles = {"": ("fEP", "fEQr", "fMK", "fMG", "fMT", "fMH", "fML")}
+    tiles["b"] = tuple(n + "b" for n in tiles[""])
+
+    def prep(w, ak, ag, bg):
+        e, r, k, gl = tiles[w][:4]
+        for i, c in enumerate((ak, ag, bg)):
+            ts(X(e, 32 * i, 32 * i + 32), X("fON"), c, O.mult)
+        tr(X(k, 0, 32), X(e, 0, 32))
+        tr(X(r, 0, 64), X(e, 32, 96))
+        ts(X(gl, 0, 32), X(r, 32, 64), ag, O.is_lt)
+        ts(X(gl, 32, 96), X(r, 0, 64), bg, O.is_lt)
+
+    def ranks(w, ak, bk):
+        e, r, k, gl, t, h, ml = tiles[w]
+        ts(X(e, 96, 128), X("fON"), bk, O.mult)
+        tr(X(k, 32, 64), X(e, 96, 128))
+        ts(X(t, 256, 288), X(k, 32, 64), ak, O.is_equal)
+        ts(X(t, 288, 352), X(k, 0, 64), bk, O.is_equal)
+        ts(X(t, 0, 32), X(k, 32, 64), ak, O.is_gt)
+        ts(X(t, 64, 128), X(k, 0, 64), bk, O.is_gt)
+        tt(X(t, 32, 64), X(t, 256, 288), X(gl, 0, 32), O.mult)
+        tt(X(t, 128, 192), X(t, 288, 352), X(gl, 32, 96), O.mult)
+        red(X(ml, 0, 1), X(t, 0, 64))
+        red(X(ml, 1, 2), X(t, 64, 192))
+        ts(X(ml, 2, 3), X(ml, 0, 1), P32, O.add)
+
+    def hot(w, at, row, n, va, vb, outs):
+        e, r, k, gl, t, h, ml = tiles[w]
+        ts(X(h, at, at + n), row, X(ml, 2, 3), O.is_equal, va, O.mult)
+        ts(X(h, at + n, at + 2 * n), row, X(ml, 1, 2), O.is_equal, vb, O.mult)
+        tt(X(h, at + 2 * n, at + 3 * n), X(h, at, at + n), X(h, at + n, at + 2 * n), O.add)
+        tr(X(h, at + 3 * n, at + 4 * n), X(h, at + 2 * n, at + 3 * n))
+        for i, o in enumerate(outs):
+            red(o, X(h, at + 3 * n + 32 * i, at + 3 * n + 32 * i + 32))
+
+    def pc(i, v):
+        ts(X("fFM", i, i + 1), P32, float(v), O.add)
+        return X("fFM", i, i + 1)
+
+    def final(i, gcol, acol, out):
+        ts(X("fFH", 192 * i, 192 * i + 192), X("fPT"), gcol, O.is_equal, acol, O.mult)
+        tr(X("fFT%d" % i), X("fFH", 192 * i, 192 * i + 192))
+        for c in range(6):
+            (red if i > 1 and c % 2 else accum)(X("fFR", 6 * i + c, 6 * i + c + 1), X("fFT%d" % i, 32 * c, 32 * c + 32))
+        tt(out, X("fFR", 6 * i, 6 * i + 6), out, O.max)
+
+    prep("", c2k, c2g, D1g)
+    ranks("", c2k, z1)
+    hot("", 0, X("fROW", 0, 64), 64, pc(0, 64), P32, [X("fML", 4, 5), X("fML", 5, 6)])
+    cp(X("B2o"), X("fML", 4, 6))
+    prep("b", o2k, o2g, L1g)
+    hot("", 256, X("fR96", 0, 32), 32, c2g, D1g, [H2g])
+    cp(X("fFL"), X("fJB"))
+    cp(X("fFD"), X("fJB"))
+    final(0, L1g, pc(1, 288), X("fFL"))
+    final(1, D1g, pc(2, 96), X("fFD"))
+    a416, a128, a192 = pc(3, 416), pc(4, 128), pc(5, 192)
+
+    red(X("fNB"), ("fNK", 0, 32, 0, 128, 4))
+    ts(X("fNS", 1, 2), X("fNB"), -low, O.min)
+    ranks("b", o2k, X("fNS", 1, 2))
+    hot("b", 0, X("fROW", 0, 64), 64, o2g, L1g, [X("fMLb", 4, 5), X("fMLb", 5, 6)])
+    ts(X("N2o"), X("fMLb", 4, 6), 128.0 * me, O.subtract, 95.0, O.min)
+    pick("NP2", 32, "QT", 192, 288, ("N2o", 0))
+    for b in range(4):
+        mm("p%d" % (2 + b), 128, "EQ", 128 * b, "NP2", 0, True, False)
+    pick("BP2", 32, "DW", 96, 192, ("B2o", 0))
+    for b in range(4):
+        mm("p%d" % (2 + b), 128, "EQ", 128 * b, "BP2", 0, False, True)
+    pick("MG3", 16, "LD3", 0, 32, ("Mo", 2))
+    send2(3)
+    hot("b", 256, X("fR96", 0, 32), 32, o2g, L1g, [L2g])
+    final(2, L2g, a416, X("fFL"))
+    cp(X("FLo", 0, 6), X("fFL"))
+    new("NT1", 416)
+    pick("LF", 128, "QT", 0, 544, ("FLo", 0))
+    mm("p7", 128, "WQ", 0, "LF", 0)
+    dma("y", T.oc[:, 0:384], _codes(T, "LF", 0, 96), [X("LF", 0, 96)], [])
+    for k in range(4):
+        dma("y", T.osc[4 * k:4 * k + 4, 0:96], T.LFs[32 * k:32 * k + 4, 0:96], [X("LFs", 0, 96)], [])
+    act(X("fY"), X("p7", 0, 96))
+    dma("a", T.y[:], T.fY[:], [X("fY")], [])
+
+    hot("b", 384, X("fR96", 0, 32), 32, a128, a192, [X("fMLb", 6, 7)])
+    final(3, H2g, X("fMLb", 6, 7), X("fFD"))
+    cp(X("FDo"), X("fFD"))
+    pick("DF", 96, "DW", 0, 224, ("FDo", 0))
+    dma("y", T.oc[:, 384:768], _codes(T, "DF", 0, 96), [X("DF", 0, 96)], [])
+    for k in range(4):
+        dma("a" if k % 2 else "y", T.osc[4 * k:4 * k + 4, 96:192], T.DFs[32 * k:32 * k + 4, 0:96], [X("DFs", 0, 96)], [])
+    cp(X("GI"), X("fG4", 0, 4))
+    op("v", lambda: g.vector.tensor_scalar(T.GJ[:], T.GI[:], 7, None, O.arith_shift_right), [X("GI")], [X("GJ")])
+    ts(X("GK"), X("GJ"), -32, O.mult)
+    ms(X("fG4t", 0, 32), 0.0)
+    tt(X("fG4t", 0, 4), X("GI"), X("GK"), O.add)
+    tr(X("fG4t", 32, 64), X("fG4t", 0, 32))
+    dma("a", T.lw[:], T.fG4t[0:2, 32:64], [X("fG4t", 32, 64)], [])
+    dma("a", T.sw[:], T.fG4t[2:4, 32:64], [X("fG4t", 32, 64)], [])
+    cnt["ls"] = ls[0]
+    for s in sorted(cnt):
+        if waited["g"].get(s, 0) < cnt[s]:
+            g.wait_ge(T.sem[s], cnt[s])

@@ -26,7 +26,7 @@ for _x, _n in ((1, 4), (2, 12), (3, 4)):
     SCRATCH["RC%ds" % _x] = ("sbuf", [128, 4 * _n], "uint8")
     SCRATCH["RW%d" % _x] = ("sbuf", [128, _n], "float8_e4m3fn_x4")
     SCRATCH["RW%ds" % _x] = ("sbuf", [128, _n], "uint8")
-_F = {"RS1": 3, "RS2": 1, "SD": 32, "NK": 32, "ON": 32, "ROW": 192, "R96": 96, "PC": 8, "LC": 1, "TL": 32, "CT": 416,
+_F = {"RS1": 3, "RS2": 1, "SD": 32, "NK": 32, "ON": 32, "ROW": 192, "R96": 96, "PC": 8, "LC": 1, "TL": 32, "CT": 416, "UZ": 8,
       "FT": 96, "FK": 96, "S8": 8, "JB": 6, "PT": 192, "K0": 192, "KK": 192, "TT": 192, "KF": 96, "TF": 96, "CL": 288, "RB": 4,
       "HL": 288, "HT": 288, "EA": 256, "RA": 256, "CA": 1792, "CN": 8, "H1": 64, "H1t": 64, "OL": 2,
       "SWK": 8, "EB": 256, "RBW": 256, "CB": 1792, "CBN": 8, "CF": 8, "VO": 2, "H2": 192, "H2t": 192, "OX": 6, "XO": 24, "XP": 18,
@@ -49,6 +49,7 @@ SEMAPHORES = ["vs", "ac", "te", "gp", "ls", "sa1", "sa2", "sr1", "sr2"]
 for _x in (1, 2, 3):
     SEMAPHORES += ["a%d" % _x, "b%d" % _x, "qc%d" % _x, "qs%d" % _x, "wc%d" % _x, "ws%d" % _x]
 SEMAPHORES += ["d%d" % _i for _i in range(60)]
+WAKE, PIPE, CYCLE, SLACK, FLIGHT = 0.1, 0.06, 0.00083, 0.03, 6.2
 NX = {1: 4, 2: 12, 3: 4}
 LAND = {1: ("UD", 0), 2: ("DW", 96), 3: ("DW", 192)}
 
@@ -157,7 +158,7 @@ def rank_program(g, core, T, topo):
     Q = {"v": g.vector, "a": g.scalar, "t": g.tensor, "g": g, "y": g.sync}
     SEM = {"v": "vs", "a": "ac", "t": "te", "g": "gp"}
     acc, waited, know, cnt = {}, {q: {} for q in Q}, {}, {}
-    nd = [0]
+    nd, ls, sent = [0], [0], []
 
     def X(name, c0=0, c1=None, r0=0, r1=128, st=1):
         o, w = _AT[name] if name in _AT else (0, SCRATCH[name][1][1])
@@ -169,6 +170,9 @@ def rank_program(g, core, T, topo):
             return T[n][:, c0:c1] if st == 1 else T[n][:, c0:c1:st]
         return T[n][r0:r1, c0:c1] if st == 1 else T[n][r0:r1, c0:c1:st]
 
+    def width(v):
+        return -(-(v[2] - v[1]) // v[5])
+
     def hit(a, b):
         if a[4] <= b[3] or b[4] <= a[3] or a[2] <= b[1] or b[2] <= a[1]:
             return False
@@ -176,6 +180,14 @@ def rank_program(g, core, T, topo):
 
     def norm(v):
         return (v[0], 0, 512, 0, 128, 1) if SCRATCH[v[0]][0] == "psum" else v
+
+    def enter(book, reads, writes, tag, q):
+        for v in writes:
+            nv = norm(v)
+            book[v[0]] = [e for e in book.get(v[0], []) if not (nv[1] <= e[0][1] and e[0][2] <= nv[2] and nv[3] <= e[0][3] and e[0][4] <= nv[4] and nv[5] == 1)]
+            book[v[0]].append((nv, True, tag, q))
+        for v in reads:
+            book.setdefault(v[0], []).append((norm(v), False, tag, q))
 
     def pre(q, reads, writes):
         need = {}
@@ -196,14 +208,57 @@ def rank_program(g, core, T, topo):
 
     def post(q, reads, writes, ev):
         know[ev] = dict(waited[q])
-        for v in writes:
-            nv = norm(v)
-            acc[v[0]] = [e for e in acc.get(v[0], []) if not (nv[1] <= e[0][1] and e[0][2] <= nv[2] and nv[3] <= e[0][3] and e[0][4] <= nv[4] and nv[5] == 1)]
-            acc[v[0]].append((nv, True, ev, q))
-        for v in reads:
-            acc.setdefault(v[0], []).append((norm(v), False, ev, q))
+        enter(acc, reads, writes, ev, q)
 
-    def op(q, call, reads, writes):
+    nodes, seen = [], {}
+
+    def note(ways, reads, writes, after=(), late=0.0):
+        k = len(nodes)
+        pr = set(after)
+        q0 = list(ways)[0] if len(ways) == 1 else ""
+        for vs, w in ((reads, False), (writes, True)):
+            for v in vs:
+                ps = SCRATCH[v[0]][0] == "psum"
+                for r, iw, i, q in seen.get(v[0], []):
+                    if i != k and (iw or w or (ps and (q != q0 or not q))) and hit(r, norm(v)):
+                        pr.add(i)
+        enter(seen, reads, writes, k, q0)
+        nodes.append((ways, pr, late))
+        return k
+
+    def schedule():
+        n = len(nodes)
+        succ = [[] for _ in range(n)]
+        for k, (_, pr, _) in enumerate(nodes):
+            for p in pr:
+                succ[p].append(k)
+        dur = [min(c for _, c in w.values()) + late for w, _, late in nodes]
+        path = [0.0] * n
+        for k in range(n - 1, -1, -1):
+            path[k] = dur[k] + max([path[x] + WAKE for x in succ[k]], default=0.0)
+        left = [len(pr) for _, pr, _ in nodes]
+        at = [0.0] * n
+        free = {q: 0.0 for q in Q}
+        ready = {k for k in range(n) if not left[k]}
+        while ready:
+            opt = []
+            for k in ready:
+                q, t = min(((q, max(free.get(q, 0.0), at[k])) for q in nodes[k][0]), key=lambda x: x[1] + nodes[k][0][x[0]][1])
+                opt.append((t, k, q))
+            first = min(opt)[0]
+            t, k, q = max((o for o in opt if o[0] <= first + SLACK), key=lambda o: (path[o[1]], -o[1]))
+            ready.discard(k)
+            issue, c = nodes[k][0][q]
+            issue()
+            if q in free:
+                free[q] = t + c - (PIPE if q in SEM else 0.0)
+            for x in succ[k]:
+                at[x] = max(at[x], t + c + nodes[k][2] + WAKE)
+                left[x] -= 1
+                if not left[x]:
+                    ready.add(x)
+
+    def issue_op(q, call, reads, writes):
         pre(q, reads, writes)
         s = SEM[q]
         if q == "g" and waited[q].get(s, 0) < cnt.get(s, 0):
@@ -214,22 +269,41 @@ def rank_program(g, core, T, topo):
         i.then_inc(T.sem[s], 1)
         post(q, reads, writes, (s, cnt[s]))
 
+    def el(n, f=1.0):
+        return PIPE + max(64, n * f) * CYCLE
+
+    def op(q, call, reads, writes, cost):
+        note({q: (lambda: issue_op(q, call, reads, writes), cost)}, reads, writes)
+
+    def either(v, a, reads, writes, n):
+        note({"v": (lambda: issue_op("v", v, reads, writes), el(n)), "a": (lambda: issue_op("a", a, reads, writes), el(n) + 0.02)}, reads, writes)
+
     def dma(q, out, in_, reads=(), writes=()):
-        pre(q, reads, writes)
-        s = "d%d" % nd[0]
-        nd[0] += 1
-        Q[q].dma_start(out, in_).then_inc(T.sem[s], 16)
-        cnt[s] = 16
-        post(q, reads, writes, (s, 16))
+        def issue():
+            pre(q, reads, writes)
+            s = "d%d" % nd[0]
+            nd[0] += 1
+            Q[q].dma_start(out, in_).then_inc(T.sem[s], 16)
+            cnt[s] = 16
+            post(q, reads, writes, (s, 16))
+        note({q: (issue, 0.06)}, reads, writes, (), 2.0)
+
+    def send(moves, sem, reads):
+        def issue():
+            pre("g", reads, [])
+            ls[0] += _remote(g, T, topo, core, moves, sem)
+        sent.append(note({"g": (issue, 0.4)}, reads, [], sent[-1:]))
+
+    def arrive(views, sem, total, late):
+        def issue():
+            cnt[sem] = total
+            for v in views:
+                acc.setdefault(v[0], []).append((v, True, (sem, total), "r"))
+        note({"r": (issue, 0.0)}, [], views, sent[-1:], late)
 
     def dcol(q, dst, d0, src, s0, n):
         dma(q, _codes(T, dst, d0, d0 + n), _codes(T, src, s0, s0 + n), [X(src, s0, s0 + n)], [X(dst, d0, d0 + n)])
         dma(q, T[dst + "s"][:, d0:d0 + n], T[src + "s"][:, s0:s0 + n], [X(src + "s", s0, s0 + n)], [X(dst + "s", d0, d0 + n)])
-
-    def arrive(views, sem, total):
-        cnt[sem] = total
-        for v in views:
-            acc.setdefault(v[0], []).append((v, True, (sem, total), "r"))
 
     def sc(s):
         return (ap(s), [s]) if isinstance(s, tuple) else (s, [])
@@ -238,57 +312,56 @@ def rank_program(g, core, T, topo):
         p1, r1 = sc(s1)
         p2, r2 = sc(s2)
         if op1 is None:
-            op("v", lambda: g.vector.tensor_scalar(ap(out), ap(a), p1, None, op0), [a] + r1, [out])
+            op("v", lambda: g.vector.tensor_scalar(ap(out), ap(a), p1, None, op0), [a] + r1, [out], el(width(out)))
         else:
-            op("v", lambda: g.vector.tensor_scalar(ap(out), ap(a), p1, p2, op0, op1), [a] + r1 + r2, [out])
+            op("v", lambda: g.vector.tensor_scalar(ap(out), ap(a), p1, p2, op0, op1), [a] + r1 + r2, [out], el(width(out)))
 
     def tt(out, a, b, o):
-        op("v", lambda: g.vector.tensor_tensor(ap(out), ap(a), ap(b), o), [a, b], [out])
+        op("v", lambda: g.vector.tensor_tensor(ap(out), ap(a), ap(b), o), [a, b], [out], el(width(out), 2.0))
 
     def cp(out, a):
-        op("v", lambda: g.vector.tensor_copy(ap(out), ap(a)), [a], [out])
+        v = lambda: g.vector.tensor_copy(ap(out), ap(a))
+        if SCRATCH[out[0]][2] in (F32, BF) and SCRATCH[a[0]][2] in (F32, BF):
+            either(v, lambda: g.scalar.activation(ap(out), ap(a), AF.Copy), [a], [out], width(out))
+        else:
+            op("v", v, [a], [out], el(width(out)))
+
+    def times(out, a, col):
+        either(lambda: g.vector.tensor_scalar(ap(out), ap(a), ap(col), None, O.mult), lambda: g.scalar.activation(ap(out), ap(a), AF.Copy, scale=ap(col)), [a, col], [out], width(out))
 
     def red(out, a, o=O.add, neg=False, ab=False):
-        op("v", lambda: g.vector.tensor_reduce(ap(out), ap(a), AxisListType.X, o, negate=neg, apply_absolute_value=ab), [a], [out])
+        op("v", lambda: g.vector.tensor_reduce(ap(out), ap(a), AxisListType.X, o, negate=neg, apply_absolute_value=ab), [a], [out], el(width(a)))
+
+    def total(out, a):
+        either(lambda: g.vector.tensor_reduce(ap(out), ap(a), AxisListType.X, O.add),
+               lambda: g.scalar.activation(ap(a), ap(a), AF.Copy, accum_out=ap(out)), [a], [a, out], width(a))
 
     def tr(out, a):
-        op("v", lambda: g.vector.transpose(ap(out), ap(a)), [a], [out])
+        op("v", lambda: g.vector.transpose(ap(out), ap(a)), [a], [out], el(width(a)))
 
     def ms(out, c):
-        op("v", lambda: g.vector.memset(ap(out), c), [], [out])
+        op("v", lambda: g.vector.memset(ap(out), c), [], [out], el(width(out)))
 
-    def act(out, a, func=AF.Copy, scale=1.0):
-        p, r = sc(scale)
-        op("a", lambda: g.scalar.activation(ap(out), ap(a), func, scale=p), [a] + r, [out])
-
-    def accum(out, a):
-        op("a", lambda: g.scalar.activation(ap(a), ap(a), AF.Copy, accum_out=ap(out)), [a], [a, out])
+    def act(out, a, func):
+        op("a", lambda: g.scalar.activation(ap(out), ap(a), func), [a], [out], el(width(out)) + 0.02)
 
     def iota(out, pat, base, cm=0):
-        if SCRATCH[out[0]][2] == I32:
-            op("g", lambda: g.iota(ap(out), pat, base, cm), [], [out])
-        else:
-            op("g", lambda: g.iota(ap(out), pat, base, cm, allow_small_or_imprecise_dtypes=True), [], [out])
+        kw = {} if SCRATCH[out[0]][2] == I32 else {"allow_small_or_imprecise_dtypes": True}
+        op("g", lambda: g.iota(ap(out), pat, base, cm, **kw), [], [out], 0.13 + 2 * CYCLE * width(out))
 
     def quant(dst, d0, d1, src, s0, s1):
-        op("v", lambda: g.vector.quantize_mx(T[dst][:, d0:d1], T[dst + "s"][:, d0:d1], T[src][:, s0:s1]), [X(src, s0, s1)], [X(dst, d0, d1), X(dst + "s", d0, d1)])
+        op("v", lambda: g.vector.quantize_mx(T[dst][:, d0:d1], T[dst + "s"][:, d0:d1], T[src][:, s0:s1]), [X(src, s0, s1)], [X(dst, d0, d1), X(dst + "s", d0, d1)], 0.07 + 0.00022 * (s1 - s0))
 
     def mm(bank, n, l, l0, r, r0, start=True, stop=True):
         op("t", lambda: g.tensor.matmul_mx(T[bank][:, 0:n], T[l][:, l0:l0 + 128], T[l + "s"][:, l0:l0 + 128], T[r][:, r0:r0 + n], T[r + "s"][:, r0:r0 + n], start, stop),
-           [X(l, l0, l0 + 128), X(l + "s", l0, l0 + 128), X(r, r0, r0 + n), X(r + "s", r0, r0 + n)], [X(bank, 0, n)])
+           [X(l, l0, l0 + 128), X(l + "s", l0, l0 + 128), X(r, r0, r0 + n), X(r + "s", r0, r0 + n)], [X(bank, 0, n)], PIPE + 0.001 * (n + 16))
 
     def pick(dst, n, win, a, b, off):
         ov = X(off[0], off[1], off[1] + n // 16)
-        op("a", lambda: g.scalar.activation(T[dst + "s"][:, 0:n], T[win + "s"][:, a:b].indirect(ap(ov)), AF.Copy), [X(win + "s", a, b), ov], [X(dst + "s", 0, n)])
-        op("v", lambda: g.vector.tensor_copy(T[dst][:, 0:n].bitcast(dt.uint32), T[win][:, a:b].bitcast(dt.uint32).indirect(ap(ov))), [X(win, a, b), ov], [X(dst, 0, n)])
+        op("a", lambda: g.scalar.activation(T[dst + "s"][:, 0:n], T[win + "s"][:, a:b].indirect(ap(ov)), AF.Copy), [X(win + "s", a, b), ov], [X(dst + "s", 0, n)], el(n, 1.5) + 0.02)
+        op("v", lambda: g.vector.tensor_copy(T[dst][:, 0:n].bitcast(dt.uint32), T[win][:, a:b].bitcast(dt.uint32).indirect(ap(ov))), [X(win, a, b), ov], [X(dst, 0, n)], el(n, 1.5))
 
-    ls = [0]
-
-    def send(moves, sem, reads):
-        pre("g", reads, [])
-        ls[0] += _remote(g, T, topo, core, moves, sem)
-
-    def send1(x, src, s0):
+    def send1(x, src, s0, between=lambda: None):
         n = NX[x]
         p, ps = s0 + n * m0, src + "s"
         send([(_codes(T, src, p, p + 4 * n), [(hs[3 if x == 2 else 1], _codes(T, "RC%d" % x, 0, 4 * n))], e_on)], "qc%d" % x, [X(src, p, p + 4 * n)])
@@ -301,43 +374,46 @@ def rank_program(g, core, T, topo):
             mp.append((T[ps][:, c:c + n], [(T.cores[r], T["LD%ds" % x][:, n * me:n * me + n])], e))
             rd.append(X(src, c, c + n))
             rp.append(X(ps, c, c + n))
+        between()
         send(mc, "a%d" % x, rd)
         send(mp, "a%d" % x, rp)
         dcol("y", "LD%d" % x, n * me, src, s0 + n * m, n)
         oth = [X(k, n * r, n * r + n) for k in ("LD%d" % x, "LD%ds" % x) for r in range(8) if r != me]
-        arrive(oth, "a%d" % x, 4 * 7)
+        arrive(oth, "a%d" % x, 4 * 7, FLIGHT)
 
     def send2(x):
         n = NX[x]
         nm, base = LAND[x]
         c = base + n * m
         src = "MG%d" % x
+        two = []
         for s, hc, h, k in ((src, "RW%d" % x, hs[3 if x == 2 else 1], "wc%d"), (src + "s", "RW%ds" % x, hs[3 if x == 2 else 2], "ws%d")):
-            pre("g", [X(s, 0, n)], [])
             code = s == src
             sap = _codes(T, s, 0, n) if code else T[s][:, 0:n]
             dap = _codes(T, nm, c, c + n) if code else T[nm + "s"][:, c:c + n]
             hap = _codes(T, hc, 0, n) if code else T[hc][:]
-            for mv, sem in ([(sap, [(h, hap)], e_on)], k % x), ([(sap, [(T.cores[r], dap) for r in near], e_off)], "b%d" % x):
-                ls[0] += _remote(g, T, topo, core, mv, sem)
+            send([(sap, [(h, hap)], e_on)], k % x, [X(s, 0, n)])
+            two.append(([(sap, [(T.cores[r], dap) for r in near], e_off)], "b%d" % x, [X(s, 0, n)]))
+        for mv in two:
+            send(*mv)
         dcol("y", nm, c, src, 0, n)
         oth = [X(k, base + n * order.index(r), base + n * order.index(r) + n) for k in (nm, nm + "s") for r in range(8) if r != me]
-        arrive(oth, "b%d" % x, 7 * 2 * len(e_off))
+        arrive(oth, "b%d" % x, 7 * 2 * len(e_off), FLIGHT)
 
     def send_scores(k, src, c0, w):
         sap = T[src][:, c0:c0 + w]
-        pre("g", [X(src, c0, c0 + w)], [])
-        ls[0] += _remote(g, T, topo, core, [(sap, [(hs[0], T["fRS%d" % k][:])], e_on)], "sr%d" % k)
-        ls[0] += _remote(g, T, topo, core, [(sap, [(T.cores[r], T[src][:, c0:c0 + w]) for r in near], e_off)], "sa%d" % k)
-        arrive([X(src, 4 * r, 4 * r + w) for r in range(8) if r != me], "sa%d" % k, 7 * len(e_off))
+        rd = [X(src, c0, c0 + w)]
+        send([(sap, [(hs[0], T["fRS%d" % k][:])], e_on)], "sr%d" % k, rd)
+        send([(sap, [(T.cores[r], T[src][:, c0:c0 + w]) for r in near], e_off)], "sa%d" % k, rd)
+        arrive([X(src, 4 * r, 4 * r + w) for r in range(8) if r != me], "sa%d" % k, 7 * len(e_off), FLIGHT)
 
     def load(q, buf, c0, c1, ext):
         dma(q, T[buf][:, c0:c1], ext, [], [X(buf, c0, c1)])
 
-    load("y", "BT", 384, 768, T.dm[:])
-    load("a", "BT", 0, 384, T.lv[:])
     load("y", "UZ", 4, 8, T.z[:, 0:4])
     load("a", "UZ", 0, 4, T.u[:, 0:4])
+    load("y", "BT", 384, 768, T.dm[:])
+    load("a", "BT", 0, 384, T.lv[:])
     load("y", "BT", 768, 1152, T.nz[:])
     load("a", "WT", 0, 512, T.w[:])
     iota(X("PI"), [[1, 1]], 0, 1)
@@ -352,9 +428,9 @@ def rank_program(g, core, T, topo):
     ms(X("HAF"), 0.5)
     ms(CT(192, 320, 0, 64), -1000.0)
     ms(CT(320, 384, 64, 128), -1000.0)
-    op("g", lambda: g.affine_select(T.DG[:], T.HAF[:], [[-1, 128]], O.is_equal, 0.0, 0, 1), [X("HAF")], [X("DG")])
+    op("g", lambda: g.affine_select(T.DG[:], T.HAF[:], [[-1, 128]], O.is_equal, 0.0, 0, 1), [X("HAF")], [X("DG")], 0.4)
     for i, k in enumerate((31, 15, 3)):
-        op("v", lambda k=k, i=i: g.vector.tensor_scalar(T.PJ[:, i:i + 1], T.PI[:], k, None, O.bitwise_and), [X("PI")], [X("PJ", i, i + 1)])
+        op("v", lambda k=k, i=i: g.vector.tensor_scalar(T.PJ[:, i:i + 1], T.PI[:], k, None, O.bitwise_and), [X("PI")], [X("PJ", i, i + 1)], el(1))
     cp(X("fPC", 0, 3), X("PJ"))
     P32, P16, P4 = X("fPC", 0, 1), X("fPC", 1, 2), X("fPC", 2, 3)
     for a in range(4):
@@ -369,9 +445,10 @@ def rank_program(g, core, T, topo):
         ts(v, v, 1.0, O.add)
     for b in range(3):
         ts(X("fPC", 3 + b, 4 + b), P32, 32.0 * b, O.add)
+    cp(X("fUZ"), X("UZ"))
     for nm, c, q in (("ZT", 4, "ZQ"), ("UT", 0, "UQ")):
         for t in range(4):
-            ts(X(nm, t, 512, 0, 128, 4), X("ONB"), X("UZ", c + t, c + t + 1), O.mult)
+            times(X(nm, t, 512, 0, 128, 4), X("ONB"), X("fUZ", c + t, c + t + 1))
         quant(q, 0, 128, nm, 0, 512)
     quant("QT", 0, 288, "BT", 0, 1152)
     mm("p0", 192, "ZQ", 0, "QT", 0)
@@ -394,7 +471,7 @@ def rank_program(g, core, T, topo):
             ts(X("fCL", 96 * b + 32 * b + 32, 96 * b + 96), X("fKK", 32 * b + 32, 96), s, O.is_gt)
         tt(X("fCL", 128 * b, 128 * b + 32), X("fKF", 32 * b, 32 * b + 32), X("fTF", 32 * b, 32 * b + 32), O.is_gt)
     for b in range(3):
-        red(X("fRB", b, b + 1), X("fCL", 96 * b, 96 * b + 96))
+        total(X("fRB", b, b + 1), X("fCL", 96 * b, 96 * b + 96))
     for i, val in enumerate((lambda b: X("fTT", 32 * b, 32 * b + 1), lambda b: X("fPC", 3 + b, 4 + b), lambda b: X("fTT", 96 + 32 * b, 97 + 32 * b))):
         for b in range(3):
             ts(X("fHL", 96 * i + 32 * b, 96 * i + 32 * b + 32), X("fTL"), X("fRB", b, b + 1), O.is_equal, val(b), O.mult)
@@ -418,10 +495,12 @@ def rank_program(g, core, T, topo):
     ts(X("fJB"), X("fJB"), P16, O.add)
     ms(X("fVO", 0, 1, 0, 64), 96.0)
     ms(X("fVO", 0, 1, 64, 128), 0.0)
-    ms(X("ET"), 0.0)
+    for b in range(8):
+        ms(X("ET", 256 * b, 256 * b + 256), 0.0)
     for b in range(4):
         cp(X("ET", 513 * b, 512 * b + 512, 0, 128, 4), X("DG"))
-    quant("EQ", 0, 512, "ET", 0, 2048)
+    for b in range(4):
+        quant("EQ", 128 * b, 128 * b + 128, "ET", 512 * b, 512 * b + 512)
     quant("WQ", 0, 128, "WT", 0, 512)
     ms(X("FLo", 6, 8), 0)
     for d in ("UD", "NP1", "BP2", "NP2"):
@@ -433,10 +512,7 @@ def rank_program(g, core, T, topo):
 
     def expand(e, col, rows):
         for s in range(8):
-            if s % 2:
-                act(X(e, 32 * s, 32 * s + 32), X("fON"), AF.Copy, col(s))
-            else:
-                ts(X(e, 32 * s, 32 * s + 32), X("fON"), col(s), O.mult)
+            times(X(e, 32 * s, 32 * s + 32), X("fON"), col(s))
         tr(X(rows), X(e))
 
     def compare(buf, rows, s):
@@ -451,30 +527,27 @@ def rank_program(g, core, T, topo):
 
     def to_all(out, src, a):
         for d in range(4):
-            if d % 2 and SCRATCH[out[0]][2] == F32:
-                act(rows4(out, d), rows4(src, a))
-            else:
-                cp(rows4(out, d), rows4(src, a))
+            cp(rows4(out, d), rows4(src, a))
 
     expand("fEA", key, "fRA")
-    red(X("fCN", me, me + 1), compare("fCA", "fRA", me))
+    total(X("fCN", me, me + 1), compare("fCA", "fRA", me))
     ts(X("fH1"), CT(0, 64), X("fCN", me, me + 1), O.is_equal, X("fSD", 4 * me + 1, 4 * me + 2), O.mult)
     tr(X("fH1t"), X("fH1"))
-    red(X("fOL", 0, 1), X("fH1t", 0, 32))
-    red(X("fOL", 1, 2), X("fH1t", 32, 64))
+    total(X("fOL", 0, 1), X("fH1t", 0, 32))
+    total(X("fOL", 1, 2), X("fH1t", 32, 64))
     to_all(X("DPo"), X("fOL"), 0)
     pick("SL1", 32, "QT", 96, 192, ("DPo", 0))
     send1(1, "SL1", 0)
 
     others = [s for s in range(8) if s != me]
     for s in others:
-        accum(X("fCN", s, s + 1), compare("fCA", "fRA", s))
+        total(X("fCN", s, s + 1), compare("fCA", "fRA", s))
 
     def listed(k, tgt, cn, val, out):
         for s in range(8):
             ts(X("fHB", 256 * k + 32 * s, 256 * k + 32 * s + 32), tgt, X(cn, s, s + 1), O.is_equal, val(s), O.mult)
         tr(X("fSB", 256 * k, 256 * k + 256), X("fHB", 256 * k, 256 * k + 256))
-        accum(out, X("fSB", 256 * k, 256 * k + 256))
+        total(out, X("fSB", 256 * k, 256 * k + 256))
 
     def owners(parts, mul, add, i):
         n = len(parts)
@@ -492,20 +565,19 @@ def rank_program(g, core, T, topo):
     L1g, L2g, D1g, H2g = (X("fG4", i, i + 1) for i in range(4))
     to_all(D1g, X("fG4", 4, 5), 0)
     owners([(CT(96, 128), D1g)], 4, P4, 0)
+    pick("MG1", 16, "LD1", 0, 32, ("Mo", 0))
+    send2(1)
 
     for a in range(4):
-        src = ("fSD", 0, 32, 32 * (a ^ 1), 32 * (a ^ 1) + 32, 4)
-        (act if a % 2 else cp)(X("fSWK", 0, 8, 32 * a, 32 * a + 32), src)
+        cp(X("fSWK", 0, 8, 32 * a, 32 * a + 32), ("fSD", 0, 32, 32 * (a ^ 1), 32 * (a ^ 1) + 32, 4))
     expand("fEB", lambda s: X("fSWK", s, s + 1), "fRBW")
-    red(X("fCBN", me, me + 1), compare("fCB", "fRBW", me))
+    total(X("fCBN", me, me + 1), compare("fCB", "fRBW", me))
     tt(X("fCF", me, me + 1), X("fCN", me, me + 1), X("fCBN", me, me + 1), O.add)
     tt(X("fVO", 1, 2), X("fVO", 0, 1), X("fSD", 4 * me + 1, 4 * me + 2), O.add)
     ts(X("fH2"), CT(192, 384), X("fCF", me, me + 1), O.is_equal, X("fVO", 1, 2), O.mult)
     tr(X("fH2t"), X("fH2"))
     for c in range(6):
-        (accum if c % 2 else red)(X("fOX", c, c + 1), X("fH2t", 32 * c, 32 * c + 32))
-    pick("MG1", 16, "LD1", 0, 32, ("Mo", 0))
-    send2(1)
+        total(X("fOX", c, c + 1), X("fH2t", 32 * c, 32 * c + 32))
     for a in range(4):
         to_all(X("fXO", 6 * a, 6 * a + 6), X("fOX"), a)
     tt(X("fXP", 0, 12), X("fXO", 0, 12), X("fXO", 12, 24), O.add)
@@ -523,8 +595,9 @@ def rank_program(g, core, T, topo):
     ts(X("fOW", 1, 2), L1g, 128.0 * me + 128, O.is_lt)
     tt(X("fOW", 2, 3), X("fOW", 0, 1), X("fOW", 1, 2), O.mult)
     for s in others:
-        accum(X("fCBN", s, s + 1), compare("fCB", "fRBW", s))
-    tt(X("fCF"), X("fCN"), X("fCBN"), O.add)
+        total(X("fCBN", s, s + 1), compare("fCB", "fRBW", s))
+    for s in others:
+        tt(X("fCF", s, s + 1), X("fCN", s, s + 1), X("fCBN", s, s + 1), O.add)
     listed(1, CT(128, 160), "fCF", gid, X("fLB", 0, 1))
     listed(2, CT(128, 160), "fCF", key, X("fLB", 1, 2))
     listed(3, CT(64, 96), "fCF", lambda s: X("fSD", 4 * s + 2, 4 * s + 3), X("fLB", 2, 3))
@@ -538,11 +611,7 @@ def rank_program(g, core, T, topo):
 
     def new(nt, q0):
         for b in range(4):
-            o = X(nt, b, 512, 0, 128, 4)
-            if b < 2:
-                cp(o, X("p%d" % (2 + b), 0, 128))
-            else:
-                act(o, X("p%d" % (2 + b), 0, 128))
+            cp(X(nt, b, 512, 0, 128, 4), X("p%d" % (2 + b), 0, 128))
         quant("QT", q0, q0 + 128, nt, 0, 512)
 
     for b in range(4):
@@ -552,8 +621,7 @@ def rank_program(g, core, T, topo):
     tr(X("fSC"), X("p6", 0, 32))
     red(X("fNS", 0, 1), X("fSC", 0, 1), O.add, True, True)
     tt(X("fNK", 4 * me, 4 * me + 1), X("fNS", 0, 1), X("fOW", 2, 3), O.mult)
-    send_scores(2, "fNK", 4 * me, 1)
-    send1(3, "QT", 288)
+    send1(3, "QT", 288, lambda: send_scores(2, "fNK", 4 * me, 1))
     pick("MG2", 16, "LD2", 0, 96, ("Mo", 4))
     send2(2)
 
@@ -563,7 +631,7 @@ def rank_program(g, core, T, topo):
     def prep(w, ak, ag, bg):
         e, r, k, gl = tiles[w][:4]
         for i, c in enumerate((ak, ag, bg)):
-            ts(X(e, 32 * i, 32 * i + 32), X("fON"), c, O.mult)
+            times(X(e, 32 * i, 32 * i + 32), X("fON"), c)
         tr(X(k, 0, 32), X(e, 0, 32))
         tr(X(r, 0, 64), X(e, 32, 96))
         ts(X(gl, 0, 32), X(r, 32, 64), ag, O.is_lt)
@@ -579,8 +647,8 @@ def rank_program(g, core, T, topo):
         ts(X(t, 64, 128), X(k, 0, 64), bk, O.is_gt)
         tt(X(t, 32, 64), X(t, 256, 288), X(gl, 0, 32), O.mult)
         tt(X(t, 128, 192), X(t, 288, 352), X(gl, 32, 96), O.mult)
-        red(X(ml, 0, 1), X(t, 0, 64))
-        red(X(ml, 1, 2), X(t, 64, 192))
+        total(X(ml, 0, 1), X(t, 0, 64))
+        total(X(ml, 1, 2), X(t, 64, 192))
         ts(X(ml, 2, 3), X(ml, 0, 1), P32, O.add)
 
     def hot(w, at, row, n, va, vb, outs):
@@ -590,7 +658,7 @@ def rank_program(g, core, T, topo):
         tt(X(h, at + 2 * n, at + 3 * n), X(h, at, at + n), X(h, at + n, at + 2 * n), O.add)
         tr(X(h, at + 3 * n, at + 4 * n), X(h, at + 2 * n, at + 3 * n))
         for i, o in enumerate(outs):
-            red(o, X(h, at + 3 * n + 32 * i, at + 3 * n + 32 * i + 32))
+            total(o, X(h, at + 3 * n + 32 * i, at + 3 * n + 32 * i + 32))
 
     def pc(i, v):
         ts(X("fFM", i, i + 1), P32, float(v), O.add)
@@ -600,7 +668,7 @@ def rank_program(g, core, T, topo):
         ts(X("fFH", 192 * i, 192 * i + 192), X("fPT"), gcol, O.is_equal, acol, O.mult)
         tr(X("fFT%d" % i), X("fFH", 192 * i, 192 * i + 192))
         for c in range(6):
-            (red if i > 1 and c % 2 else accum)(X("fFR", 6 * i + c, 6 * i + c + 1), X("fFT%d" % i, 32 * c, 32 * c + 32))
+            total(X("fFR", 6 * i + c, 6 * i + c + 1), X("fFT%d" % i, 32 * c, 32 * c + 32))
         tt(out, X("fFR", 6 * i, 6 * i + 6), out, O.max)
 
     prep("", c2k, c2g, D1g)
@@ -637,7 +705,7 @@ def rank_program(g, core, T, topo):
     dma("y", T.oc[:, 0:384], _codes(T, "LF", 0, 96), [X("LF", 0, 96)], [])
     for k in range(4):
         dma("y", T.osc[4 * k:4 * k + 4, 0:96], T.LFs[32 * k:32 * k + 4, 0:96], [X("LFs", 0, 96)], [])
-    act(X("fY"), X("p7", 0, 96))
+    cp(X("fY"), X("p7", 0, 96))
     dma("a", T.y[:], T.fY[:], [X("fY")], [])
 
     hot("b", 384, X("fR96", 0, 32), 32, a128, a192, [X("fMLb", 6, 7)])
@@ -648,13 +716,14 @@ def rank_program(g, core, T, topo):
     for k in range(4):
         dma("a" if k % 2 else "y", T.osc[4 * k:4 * k + 4, 96:192], T.DFs[32 * k:32 * k + 4, 0:96], [X("DFs", 0, 96)], [])
     cp(X("GI"), X("fG4", 0, 4))
-    op("v", lambda: g.vector.tensor_scalar(T.GJ[:], T.GI[:], 7, None, O.arith_shift_right), [X("GI")], [X("GJ")])
+    op("v", lambda: g.vector.tensor_scalar(T.GJ[:], T.GI[:], 7, None, O.arith_shift_right), [X("GI")], [X("GJ")], el(1))
     ts(X("GK"), X("GJ"), -32, O.mult)
     ms(X("fG4t", 0, 32), 0.0)
     tt(X("fG4t", 0, 4), X("GI"), X("GK"), O.add)
     tr(X("fG4t", 32, 64), X("fG4t", 0, 32))
     dma("a", T.lw[:], T.fG4t[0:2, 32:64], [X("fG4t", 32, 64)], [])
     dma("a", T.sw[:], T.fG4t[2:4, 32:64], [X("fG4t", 32, 64)], [])
+    schedule()
     cnt["ls"] = ls[0]
     for s in sorted(cnt):
         if waited["g"].get(s, 0) < cnt[s]:

@@ -28,6 +28,7 @@ for _x, _n in ((1, 4), (2, 12), (3, 4)):
     SCRATCH["RW%ds" % _x] = ("sbuf", [128, _n], "uint8")
 _F = {"RS1": 3, "RS2": 1, "SD": 32, "NK": 32, "ON": 32, "ROW": 192, "R96": 96, "PC": 8, "LC": 1, "TL": 32, "CT": 416, "UZ": 8,
       "FT": 96, "FK": 96, "S8": 8, "JB": 6, "PT": 192, "K0": 192, "KK": 192, "TT": 192, "KF": 96, "TF": 96, "CL": 288, "RB": 4,
+      "EO": 32, "RO": 32, "CW": 256, "CV": 256, "NF": 2, "CTO": 64, "IDW": 32, "RP": 96,
       "HL": 288, "HT": 288, "EA": 256, "RA": 256, "CA": 1792, "CN": 8, "H1": 64, "H1t": 64, "OL": 2,
       "SWK": 8, "EB": 256, "RBW": 256, "CB": 1792, "CBN": 8, "CF": 8, "VO": 2, "H2": 192, "H2t": 192, "OX": 6, "XO": 24, "XP": 18,
       "GID": 8, "OW": 4, "HB": 1024, "SB": 1024, "LB": 4, "XB": 16, "SX": 8, "MM": 96, "MW": 384, "MV": 384, "OM": 6,
@@ -45,11 +46,12 @@ for _n, _w in _F.items():
 SCRATCH["fW"] = ("sbuf", [128, _o], F32)
 for _i in range(8):
     SCRATCH["p%d" % _i] = ("psum", [128, 512], F32)
-SEMAPHORES = ["vs", "ac", "te", "gp", "ls", "sa1", "sa2", "sr1", "sr2"]
+SEMAPHORES = ["vs", "ac", "te", "gp", "ls", "sa1", "sa2", "sn1", "sn2", "sr1", "sr2"]
 for _x in (1, 2, 3):
     SEMAPHORES += ["a%d" % _x, "b%d" % _x, "qc%d" % _x, "qs%d" % _x, "wc%d" % _x, "ws%d" % _x]
 SEMAPHORES += ["d%d" % _i for _i in range(60)]
-WAKE, PIPE, CYCLE, SLACK, FLIGHT = 0.1, 0.06, 0.00083, 0.03, 6.2
+WAKE, PIPE, CYCLE, SLACK = 0.1, 0.06, 0.00083, 0.03
+LATE = {"n1": 2.74, "s1": 4.34, "a1": 2.36, "b1": 1.74, "n2": 3.83, "s2": 4.82, "a2": 2.39, "b2": 4.04, "a3": 4.5, "b3": 3.94}
 NX = {1: 4, 2: 12, 3: 4}
 LAND = {1: ("UD", 0), 2: ("DW", 96), 3: ("DW", 192)}
 
@@ -99,7 +101,8 @@ def _hand_on(g, core, T, topo, rank, far):
     def scores(k, w):
         g.wait_ge(T.sem["sr%d" % k], n_on)
         dst = "fSD" if k == 1 else "fNK"
-        return _remote(g, T, topo, core, [(T["fRS%d" % k][:], [(T.cores[r], T[dst][:, 4 * rank:4 * rank + w]) for r in far], eng)], "sa%d" % k)
+        to = far[:len(far) // 2] if me < 2 else far[len(far) // 2:]
+        return _remote(g, T, topo, core, [(T["fRS%d" % k][:], [(T.cores[r], T[dst][:, 4 * rank:4 * rank + w]) for r in to], eng)], "sa%d" % k)
 
     def first(x, codes):
         n = NX[x]
@@ -124,16 +127,15 @@ def _hand_on(g, core, T, topo, rank, far):
             mv = [(T["RW%ds" % x][:], [(T.cores[r], T[nm + "s"][:, base:base + n]) for r in far], eng)]
         return _remote(g, T, topo, core, mv, "b%d" % x)
 
-    if me == 0:
-        ls += scores(1, 3) + scores(2, 1)
-    elif me in (1, 2):
+    if me in (1, 2):
+        ls += scores(1, 3)
         for x in (1, 3):
             ls += first(x, me == 1)
             ls += second(x, me == 1)
-    else:
-        for f in (first, second):
-            ls += f(2, True)
-            ls += f(2, False)
+    elif me in (0, 3):
+        ls += first(2, me == 0)
+        ls += scores(2, 1)
+        ls += second(2, me == 0)
     g.wait_ge(T.sem.ls, ls)
 
 
@@ -364,7 +366,7 @@ def rank_program(g, core, T, topo):
     def send1(x, src, s0, between=lambda: None):
         n = NX[x]
         p, ps = s0 + n * m0, src + "s"
-        send([(_codes(T, src, p, p + 4 * n), [(hs[3 if x == 2 else 1], _codes(T, "RC%d" % x, 0, 4 * n))], e_on)], "qc%d" % x, [X(src, p, p + 4 * n)])
+        send([(_codes(T, src, p, p + 4 * n), [(hs[0 if x == 2 else 1], _codes(T, "RC%d" % x, 0, 4 * n))], e_on)], "qc%d" % x, [X(src, p, p + 4 * n)])
         send([(T[ps][:, p:p + 4 * n], [(hs[3 if x == 2 else 2], T["RC%ds" % x][:])], e_on)], "qs%d" % x, [X(ps, p, p + 4 * n)])
         mc, mp, rd, rp = [], [], [], []
         for i, r in enumerate(near):
@@ -379,7 +381,7 @@ def rank_program(g, core, T, topo):
         send(mp, "a%d" % x, rp)
         dcol("y", "LD%d" % x, n * me, src, s0 + n * m, n)
         oth = [X(k, n * r, n * r + n) for k in ("LD%d" % x, "LD%ds" % x) for r in range(8) if r != me]
-        arrive(oth, "a%d" % x, 4 * 7, FLIGHT)
+        arrive(oth, "a%d" % x, 4 * 7, LATE["a%d" % x])
 
     def send2(x):
         n = NX[x]
@@ -387,7 +389,7 @@ def rank_program(g, core, T, topo):
         c = base + n * m
         src = "MG%d" % x
         two = []
-        for s, hc, h, k in ((src, "RW%d" % x, hs[3 if x == 2 else 1], "wc%d"), (src + "s", "RW%ds" % x, hs[3 if x == 2 else 2], "ws%d")):
+        for s, hc, h, k in ((src, "RW%d" % x, hs[0 if x == 2 else 1], "wc%d"), (src + "s", "RW%ds" % x, hs[3 if x == 2 else 2], "ws%d")):
             code = s == src
             sap = _codes(T, s, 0, n) if code else T[s][:, 0:n]
             dap = _codes(T, nm, c, c + n) if code else T[nm + "s"][:, c:c + n]
@@ -398,14 +400,15 @@ def rank_program(g, core, T, topo):
             send(*mv)
         dcol("y", nm, c, src, 0, n)
         oth = [X(k, base + n * order.index(r), base + n * order.index(r) + n) for k in (nm, nm + "s") for r in range(8) if r != me]
-        arrive(oth, "b%d" % x, 7 * 2 * len(e_off), FLIGHT)
+        arrive(oth, "b%d" % x, 7 * 2 * len(e_off), LATE["b%d" % x])
 
     def send_scores(k, src, c0, w):
         sap = T[src][:, c0:c0 + w]
         rd = [X(src, c0, c0 + w)]
-        send([(sap, [(hs[0], T["fRS%d" % k][:])], e_on)], "sr%d" % k, rd)
-        send([(sap, [(T.cores[r], T[src][:, c0:c0 + w]) for r in near], e_off)], "sa%d" % k, rd)
-        arrive([X(src, 4 * r, 4 * r + w) for r in range(8) if r != me], "sa%d" % k, 7 * len(e_off), FLIGHT)
+        send([(sap, [(h, T["fRS%d" % k][:]) for h in (hs[1:3] if k == 1 else (hs[0], hs[3]))], e_on)], "sr%d" % k, rd)
+        send([(sap, [(T.cores[r], T[src][:, c0:c0 + w]) for r in near], e_off)], "sn%d" % k, rd)
+        arrive([X(src, 4 * r, 4 * r + w) for r in near], "sn%d" % k, len(near) * len(e_off), LATE["n%d" % k])
+        arrive([X(src, 4 * r, 4 * r + w) for r in far], "sa%d" % k, len(far) * len(e_off), LATE["s%d" % k])
 
     def load(q, buf, c0, c1, ext):
         dma(q, T[buf][:, c0:c1], ext, [], [X(buf, c0, c1)])
@@ -475,9 +478,8 @@ def rank_program(g, core, T, topo):
     for i, val in enumerate((lambda b: X("fTT", 32 * b, 32 * b + 1), lambda b: X("fPC", 3 + b, 4 + b), lambda b: X("fTT", 96 + 32 * b, 97 + 32 * b))):
         for b in range(3):
             ts(X("fHL", 96 * i + 32 * b, 96 * i + 32 * b + 32), X("fTL"), X("fRB", b, b + 1), O.is_equal, val(b), O.mult)
-    tr(X("fHT"), X("fHL"))
-    for i in range(3):
-        red(X("fSD", 4 * me + i, 4 * me + i + 1), X("fHT", 96 * i, 96 * i + 96))
+        tr(X("fHT", 96 * i, 96 * i + 96), X("fHL", 96 * i, 96 * i + 96))
+        total(X("fSD", 4 * me + i, 4 * me + i + 1), X("fHT", 96 * i, 96 * i + 96))
     send_scores(1, "fSD", 4 * me, 3)
 
     LCv = X("fLC")
@@ -493,6 +495,8 @@ def rank_program(g, core, T, topo):
     ts(CT(320, 384, 0, 64), X("fROW", 0, 64, 0, 64), X("fLC", 0, 1, 0, 64), O.subtract, 32.0, O.add)
     ts(X("fPT"), X("fROW"), 128.0 * me, O.add)
     ts(X("fJB"), X("fJB"), P16, O.add)
+    ts(X("fRP", 0, 64), X("fROW", 0, 64), P32, O.subtract)
+    ts(X("fRP", 64, 96), X("fR96", 0, 32), P32, O.subtract)
     ms(X("fVO", 0, 1, 0, 64), 96.0)
     ms(X("fVO", 0, 1, 64, 128), 0.0)
     for b in range(8):
@@ -529,9 +533,17 @@ def rank_program(g, core, T, topo):
         for d in range(4):
             cp(rows4(out, d), rows4(src, a))
 
-    expand("fEA", key, "fRA")
-    total(X("fCN", me, me + 1), compare("fCA", "fRA", me))
-    ts(X("fH1"), CT(0, 64), X("fCN", me, me + 1), O.is_equal, X("fSD", 4 * me + 1, 4 * me + 2), O.mult)
+    times(X("fEO"), X("fON"), key(me))
+    tr(X("fRO"), X("fEO"))
+    for i, grp in enumerate((near, far)):
+        n = 32 * len(grp)
+        for j, s in enumerate(grp):
+            ts(X("fCW", 128 * i + 32 * j, 128 * i + 32 * j + 32), X("fRO"), key(s), O.is_le if s < me else O.is_lt)
+        tr(X("fCV", 128 * i, 128 * i + n), X("fCW", 128 * i, 128 * i + n))
+        total(X("fNF", i, i + 1), X("fCV", 128 * i, 128 * i + n))
+        if i == 0:
+            ts(X("fCTO"), CT(0, 64), X("fNF", 0, 1), O.subtract)
+    ts(X("fH1"), X("fCTO"), X("fNF", 1, 2), O.is_equal, X("fSD", 4 * me + 1, 4 * me + 2), O.mult)
     tr(X("fH1t"), X("fH1"))
     total(X("fOL", 0, 1), X("fH1t", 0, 32))
     total(X("fOL", 1, 2), X("fH1t", 32, 64))
@@ -539,6 +551,8 @@ def rank_program(g, core, T, topo):
     pick("SL1", 32, "QT", 96, 192, ("DPo", 0))
     send1(1, "SL1", 0)
 
+    expand("fEA", key, "fRA")
+    tt(X("fCN", me, me + 1), X("fNF", 0, 1), X("fNF", 1, 2), O.add)
     others = [s for s in range(8) if s != me]
     for s in others:
         total(X("fCN", s, s + 1), compare("fCA", "fRA", s))
@@ -594,6 +608,7 @@ def rank_program(g, core, T, topo):
     ts(X("fOW", 0, 1), L1g, 128.0 * me, O.is_ge)
     ts(X("fOW", 1, 2), L1g, 128.0 * me + 128, O.is_lt)
     tt(X("fOW", 2, 3), X("fOW", 0, 1), X("fOW", 1, 2), O.mult)
+    ts(X("fIDW"), X("fR96", 0, 32), P32, O.is_equal, X("fOW", 2, 3), O.mult)
     for s in others:
         total(X("fCBN", s, s + 1), compare("fCB", "fRBW", s))
     for s in others:
@@ -618,9 +633,8 @@ def rank_program(g, core, T, topo):
         mm("p%d" % (2 + b), 128, "EQ", 128 * b, "UD", 0, False, True)
     new("NT0", 288)
     mm("p6", 128, "UQ", 0, "QT", 288)
-    tr(X("fSC"), X("p6", 0, 32))
-    red(X("fNS", 0, 1), X("fSC", 0, 1), O.add, True, True)
-    tt(X("fNK", 4 * me, 4 * me + 1), X("fNS", 0, 1), X("fOW", 2, 3), O.mult)
+    tt(X("fSC"), X("p6", 0, 32), X("fIDW"), O.mult)
+    red(X("fNK", 4 * me, 4 * me + 1), X("fSC"), O.add, True, True)
     send1(3, "QT", 288, lambda: send_scores(2, "fNK", 4 * me, 1))
     pick("MG2", 16, "LD2", 0, 96, ("Mo", 4))
     send2(2)
@@ -632,33 +646,40 @@ def rank_program(g, core, T, topo):
         e, r, k, gl = tiles[w][:4]
         for i, c in enumerate((ak, ag, bg)):
             times(X(e, 32 * i, 32 * i + 32), X("fON"), c)
-        tr(X(k, 0, 32), X(e, 0, 32))
+        tr(X(k, 32, 64), X(e, 0, 32))
         tr(X(r, 0, 64), X(e, 32, 96))
-        ts(X(gl, 0, 32), X(r, 32, 64), ag, O.is_lt)
-        ts(X(gl, 32, 96), X(r, 0, 64), bg, O.is_lt)
+        o = O.is_lt if w else O.is_ge
+        ts(X(gl, 0, 32), X(r, 32, 64), ag, o, -step, O.mult)
+        ts(X(gl, 32, 96), X(r, 0, 64), bg, o, -step, O.mult)
+        ts(X(gl, 0, 96), X(gl, 0, 96), 1.0, O.add)
 
-    def ranks(w, ak, bk):
+    def ranks(w, ak, bk, raw, cut):
         e, r, k, gl, t, h, ml = tiles[w]
-        ts(X(e, 96, 128), X("fON"), bk, O.mult)
-        tr(X(k, 32, 64), X(e, 96, 128))
-        ts(X(t, 256, 288), X(k, 32, 64), ak, O.is_equal)
-        ts(X(t, 288, 352), X(k, 0, 64), bk, O.is_equal)
-        ts(X(t, 0, 32), X(k, 32, 64), ak, O.is_gt)
-        ts(X(t, 64, 128), X(k, 0, 64), bk, O.is_gt)
-        tt(X(t, 32, 64), X(t, 256, 288), X(gl, 0, 32), O.mult)
-        tt(X(t, 128, 192), X(t, 288, 352), X(gl, 32, 96), O.mult)
-        total(X(ml, 0, 1), X(t, 0, 64))
-        total(X(ml, 1, 2), X(t, 64, 192))
-        ts(X(ml, 2, 3), X(ml, 0, 1), P32, O.add)
+        if cut is None:
+            ts(X(e, 96, 128), X("fON"), raw, O.mult)
+        else:
+            ts(X(e, 96, 128), X("fON"), raw, O.mult, cut, O.min)
+        tr(X(k, 64, 96), X(e, 96, 128))
+        tt(X(t, 0, 32), X(k, 64, 96), X(gl, 0, 32), O.mult)
+        tt(X(t, 32, 96), X(k, 32, 96), X(gl, 32, 96), O.mult)
+        o = O.is_gt if w else O.is_ge
+        ts(X(t, 96, 128), X(t, 0, 32), ak, o)
+        ts(X(t, 128, 192), X(t, 32, 96), bk, o)
+        total(X(ml, 0, 1), X(t, 96, 128))
+        total(X(ml, 1, 2), X(t, 128, 192))
 
-    def hot(w, at, row, n, va, vb, outs):
+    def hot(w, at, wide, va, vb, outs):
         e, r, k, gl, t, h, ml = tiles[w]
-        ts(X(h, at, at + n), row, X(ml, 2, 3), O.is_equal, va, O.mult)
-        ts(X(h, at + n, at + 2 * n), row, X(ml, 1, 2), O.is_equal, vb, O.mult)
-        tt(X(h, at + 2 * n, at + 3 * n), X(h, at, at + n), X(h, at + n, at + 2 * n), O.add)
-        tr(X(h, at + 3 * n, at + 4 * n), X(h, at + 2 * n, at + 3 * n))
+        n = 64 if wide else 32
+        for i in range(n // 32):
+            ra = X("fRP", 32 * i, 32 * i + 32) if wide else X("fRP", 64, 96)
+            rb = X("fROW", 32 * i, 32 * i + 32) if wide else X("fR96", 0, 32)
+            o = at + 64 * i
+            ts(X(h, o, o + 32), ra, X(ml, 0, 1), O.is_equal, va, O.mult)
+            ts(X(h, o + 32, o + 64), rb, X(ml, 1, 2), O.is_equal, vb, O.mult)
+        tr(X(h, at + 2 * n, at + 4 * n), X(h, at, at + 2 * n))
         for i, o in enumerate(outs):
-            total(o, X(h, at + 3 * n + 32 * i, at + 3 * n + 32 * i + 32))
+            total(o, X(h, at + 2 * n + 64 * i, at + 2 * n + 64 * i + 64))
 
     def pc(i, v):
         ts(X("fFM", i, i + 1), P32, float(v), O.add)
@@ -672,11 +693,11 @@ def rank_program(g, core, T, topo):
         tt(out, X("fFR", 6 * i, 6 * i + 6), out, O.max)
 
     prep("", c2k, c2g, D1g)
-    ranks("", c2k, z1)
-    hot("", 0, X("fROW", 0, 64), 64, pc(0, 64), P32, [X("fML", 4, 5), X("fML", 5, 6)])
+    ranks("", c2k, z1, z1, None)
+    hot("", 0, True, pc(0, 64), P32, [X("fML", 4, 5), X("fML", 5, 6)])
     cp(X("B2o"), X("fML", 4, 6))
     prep("b", o2k, o2g, L1g)
-    hot("", 256, X("fR96", 0, 32), 32, c2g, D1g, [H2g])
+    hot("", 256, False, c2g, D1g, [H2g])
     cp(X("fFL"), X("fJB"))
     cp(X("fFD"), X("fJB"))
     final(0, L1g, pc(1, 288), X("fFL"))
@@ -685,18 +706,18 @@ def rank_program(g, core, T, topo):
 
     red(X("fNB"), ("fNK", 0, 32, 0, 128, 4))
     ts(X("fNS", 1, 2), X("fNB"), -low, O.min)
-    ranks("b", o2k, X("fNS", 1, 2))
-    hot("b", 0, X("fROW", 0, 64), 64, o2g, L1g, [X("fMLb", 4, 5), X("fMLb", 5, 6)])
+    ranks("b", o2k, X("fNS", 1, 2), X("fNB"), -low)
+    hot("b", 0, True, o2g, L1g, [X("fMLb", 4, 5), X("fMLb", 5, 6)])
     ts(X("N2o"), X("fMLb", 4, 6), 128.0 * me, O.subtract, 95.0, O.min)
-    pick("NP2", 32, "QT", 192, 288, ("N2o", 0))
-    for b in range(4):
-        mm("p%d" % (2 + b), 128, "EQ", 128 * b, "NP2", 0, True, False)
     pick("BP2", 32, "DW", 96, 192, ("B2o", 0))
     for b in range(4):
-        mm("p%d" % (2 + b), 128, "EQ", 128 * b, "BP2", 0, False, True)
+        mm("p%d" % (2 + b), 128, "EQ", 128 * b, "BP2", 0, True, False)
+    pick("NP2", 32, "QT", 192, 288, ("N2o", 0))
+    for b in range(4):
+        mm("p%d" % (2 + b), 128, "EQ", 128 * b, "NP2", 0, False, True)
     pick("MG3", 16, "LD3", 0, 32, ("Mo", 2))
     send2(3)
-    hot("b", 256, X("fR96", 0, 32), 32, o2g, L1g, [L2g])
+    hot("b", 256, False, o2g, L1g, [L2g])
     final(2, L2g, a416, X("fFL"))
     cp(X("FLo", 0, 6), X("fFL"))
     new("NT1", 416)
@@ -708,7 +729,7 @@ def rank_program(g, core, T, topo):
     cp(X("fY"), X("p7", 0, 96))
     dma("a", T.y[:], T.fY[:], [X("fY")], [])
 
-    hot("b", 384, X("fR96", 0, 32), 32, a128, a192, [X("fMLb", 6, 7)])
+    hot("b", 384, False, a128, a192, [X("fMLb", 6, 7)])
     final(3, H2g, X("fMLb", 6, 7), X("fFD"))
     cp(X("FDo"), X("fFD"))
     pick("DF", 96, "DW", 0, 224, ("FDo", 0))

@@ -11,34 +11,38 @@ SCRATCH = {
     "UT": ("sbuf", [128, 512], BF), "ZT": ("sbuf", [128, 512], BF), "ONB": ("sbuf", [128, 128], BF),
     "HAF": ("sbuf", [128, 128], BF), "DG": ("sbuf", [128, 128], BF), "ET": ("sbuf", [128, 2048], BF),
     "NT0": ("sbuf", [128, 512], BF), "NT1": ("sbuf", [128, 512], BF),
-    "PI": ("sbuf", [128, 1], I32), "PJ": ("sbuf", [128, 3], I32), "MI": ("sbuf", [128, 3], I32),
+    "PI": ("sbuf", [128, 1], I32), "PJ": ("sbuf", [128, 4], I32), "MI": ("sbuf", [128, 3], I32),
     "DPo": ("sbuf", [128, 2], U16), "LPo": ("sbuf", [128, 2], U16), "Mo": ("sbuf", [128, 6], U16),
-    "X2o": ("sbuf", [128, 6], U16), "B2o": ("sbuf", [128, 2], U16), "N2o": ("sbuf", [128, 2], U16),
+    "O1o": ("sbuf", [128, 2], U16), "UOo": ("sbuf", [128, 2], U16), "X2o": ("sbuf", [128, 6], U16), "B2o": ("sbuf", [128, 2], U16), "N2o": ("sbuf", [128, 2], U16),
     "FLo": ("sbuf", [128, 8], U16), "FDo": ("sbuf", [128, 6], U16), "GI": ("sbuf", [128, 4], I32), "GJ": ("sbuf", [128, 4], I32),
     "GK": ("sbuf", [128, 4], I32),
 }
-for _n, _w in {"QT": 544, "UQ": 128, "ZQ": 128, "EQ": 512, "WQ": 128, "SL1": 32, "LD1": 32, "MG1": 16, "UD": 128, "SL2": 96,
-               "LD2": 96, "MG2": 16, "LD3": 32, "MG3": 16, "DW": 224, "NP1": 128, "BP2": 128, "NP2": 128, "LF": 128, "DF": 96}.items():
+for _n, _w in {"QT": 544, "UQ": 128, "ZQ": 128, "EQ": 512, "WQ": 128, "SL1": 32, "LD1": 128, "MG1": 32, "UO": 36, "UD": 128, "SL2": 96,
+               "LD2": 128, "MG2": 16, "LD3": 32, "MG3": 16, "DW": 224, "NP1": 128, "BP2": 128, "NP2": 128, "LF": 128, "DF": 96}.items():
     SCRATCH[_n] = ("sbuf", [128, _w], "float8_e4m3fn_x4")
     SCRATCH[_n + "s"] = ("sbuf", [128, _w], "uint8")
-for _x, _n in ((1, 4), (2, 12), (3, 4)):
-    SCRATCH["RC%d" % _x] = ("sbuf", [128, 4 * _n], "float8_e4m3fn_x4")
-    SCRATCH["RC%ds" % _x] = ("sbuf", [128, 4 * _n], "uint8")
-    SCRATCH["RW%d" % _x] = ("sbuf", [128, _n], "float8_e4m3fn_x4")
-    SCRATCH["RW%ds" % _x] = ("sbuf", [128, _n], "uint8")
-_F = {"RS1": 3, "RS2": 1, "SD": 32, "NK": 32, "ON": 32, "ROW": 192, "R96": 96, "PC": 8, "LC": 1, "TL": 32, "CT": 416, "UZ": 8,
-      "FT": 96, "FK": 96, "S8": 8, "JB": 6, "PT": 192, "K0": 192, "KK": 192, "TT": 192, "KF": 96, "TF": 96, "CL": 288, "RB": 4,
-      "EO": 32, "RO": 32, "CW": 256, "CV": 256, "NF": 2, "CTO": 64, "IDW": 32, "RP": 96,
-      "HL": 288, "HT": 288, "EA": 256, "RA": 256, "CA": 1792, "CN": 8, "H1": 64, "H1t": 64, "OL": 2,
-      "SWK": 8, "EB": 256, "RBW": 256, "CB": 1792, "CBN": 8, "CF": 8, "VO": 2, "H2": 192, "H2t": 192, "OX": 6, "XO": 24, "XP": 18,
-      "GID": 8, "OW": 4, "HB": 1024, "SB": 1024, "LB": 4, "XB": 16, "SX": 8, "MM": 96, "MW": 384, "MV": 384, "OM": 6,
+for _x, _n, _w in ((1, 16, 18), (2, 48, 16), (3, 16, 4)):
+    SCRATCH["RC%d" % _x] = ("sbuf", [128, _n], "float8_e4m3fn_x4")
+    SCRATCH["RC%ds" % _x] = ("sbuf", [128, _n], "uint8")
+    SCRATCH["RW%d" % _x] = ("sbuf", [128, _w], "float8_e4m3fn_x4")
+    SCRATCH["RW%ds" % _x] = ("sbuf", [128, _w], "uint8")
+_F = {"RS1": 1, "RS2": 1, "RS3": 1, "RS4": 1, "SD": 32, "NL": 32, "NM": 32, "DQ": 1, "GV": 2, "CX": 256, "CY": 256, "SWA": 8, "HN": 128, "HM": 128,
+      "T4": 4, "TS": 2, "G2": 2, "GA": 8, "NS2": 1, "NK": 32, "ON": 32, "ROW": 192, "R96": 96, "PC": 8, "LC": 1, "TL": 32, "CT": 416, "UZ": 8,
+      "FT": 96, "FK": 96, "JB": 6, "PT": 192, "K0": 192, "KK": 192, "TT": 192, "KF": 96, "TF": 96, "CL": 288, "RB": 4,
+      "EO": 32, "RO": 32, "CW": 256, "CV": 256, "NF": 4, "CN": 1, "CF": 1, "CTO": 64, "IDW": 32, "RP": 96,
+      "HL": 288, "HT": 288, "H1": 64, "H1t": 64, "OL": 2,
+      "VO": 2, "H2": 192, "H2t": 192, "OX": 6, "XO": 24, "XP": 18,
+      "OW": 4, "MM": 32, "MW": 384, "MV": 384, "OM": 6,
       "SC": 32, "NS": 4, "FM": 12, "FH": 768, "FR": 24, "FL": 6, "FD": 6, "Y": 96, "G4": 8, "G4t": 64, "NB": 1,
+      "PR": 64, "PM": 64, "HP": 64, "HPt": 64, "DL": 2, "OE": 32, "OR": 32, "KM": 64, "OT": 64, "Q1": 2, "KC": 2, "QA": 2, "PA": 4,
+      "K4": 4, "KT": 4, "KE": 128, "KR": 128, "GR": 128, "GP": 4, "FF": 512, "WW": 512, "CC": 512, "N1": 4, "RB2": 4, "CO": 128, "AD": 4,
+      "HO": 256, "HQ": 256, "MO": 2,
       "FT0": 192, "FT1": 192, "FT2": 192, "FT3": 192}
 for _n, _w in (("EP", 128), ("EQr", 128), ("MK", 128), ("MG", 192), ("MT", 512), ("MH", 640), ("ML", 16)):
     _F[_n] = _F[_n + "b"] = _w
 _AT, _o = {}, 0
 for _n, _w in _F.items():
-    if _n in ("RS1", "RS2", "SD", "NK", "Y", "G4t"):
+    if _n in ("RS1", "RS2", "RS3", "RS4", "SD", "NL", "NM", "NK", "Y", "G4t"):
         SCRATCH["f" + _n] = ("sbuf", [128, _w], F32)
     else:
         _AT["f" + _n] = (_o, _w)
@@ -46,14 +50,16 @@ for _n, _w in _F.items():
 SCRATCH["fW"] = ("sbuf", [128, _o], F32)
 for _i in range(8):
     SCRATCH["p%d" % _i] = ("psum", [128, 512], F32)
-SEMAPHORES = ["vs", "ac", "te", "gp", "ls", "sa1", "sa2", "sn1", "sn2", "sr1", "sr2"]
+SEMAPHORES = ["vs", "ac", "te", "gp", "ls"] + [_s + str(_k) for _k in (1, 2, 3, 4) for _s in ("sa", "sn", "sr")]
 for _x in (1, 2, 3):
     SEMAPHORES += ["a%d" % _x, "b%d" % _x, "qc%d" % _x, "qs%d" % _x, "wc%d" % _x, "ws%d" % _x]
 SEMAPHORES += ["d%d" % _i for _i in range(60)]
 WAKE, PIPE, CYCLE, SLACK = 0.1, 0.06, 0.00083, 0.03
-LATE = {"n1": 2.74, "s1": 4.34, "a1": 2.36, "b1": 1.74, "n2": 3.83, "s2": 4.82, "a2": 2.39, "b2": 4.04, "a3": 4.5, "b3": 3.94}
-NX = {1: 4, 2: 12, 3: 4}
-LAND = {1: ("UD", 0), 2: ("DW", 96), 3: ("DW", 192)}
+LATE = {"n1": 2.53, "s1": 3.9, "a1": 4.9, "b1": 2.63, "n3": 1.9, "s3": 2.97, "n4": 1.9, "s4": 3.09, "n2": 2.14, "s2": 5.03, "a2": 4.51, "b2": 5.0,
+        "a3": 3.82, "b3": 2.45}
+NX = {1: 16, 2: 16, 3: 4}
+NY = {1: 18, 2: 16, 3: 4}
+LAND = {1: ("UO", 0), 2: ("DW", 96), 3: ("DW", 192)}
 
 
 def _layout(T, topo):
@@ -63,6 +69,10 @@ def _layout(T, topo):
     return a, b
 
 
+def _owners(x, order):
+    return {1: [order[0], order[4]], 2: order[1:4] + order[5:8], 3: order}[x]
+
+
 def _helpers(home, far, topo):
     h = [c for c in topo.cores_of(home) if c != home and topo.may_write(c, far)]
     return sorted(h, key=lambda c: (topo.die(c) != topo.die(home), c))
@@ -70,7 +80,7 @@ def _helpers(home, far, topo):
 
 def _remote(g, T, topo, core, moves, sem):
     tr = []
-    for src, dsts, eng in moves:
+    for src, dsts, eng, *own in moves:
         ids = []
         for c, _ in dsts:
             rid, pid = topo.addr(c, core)
@@ -78,9 +88,9 @@ def _remote(g, T, topo, core, moves, sem):
         m = 0
         for e in eng:
             m |= 1 << e
-        tr.append(RemoteDMATransfer(dst_ids=ids, dma_engine_mask=m, remote_sem=T.sem[sem], srcs=[src], dsts=[d for _, d in dsts]))
+        tr.append(RemoteDMATransfer(dst_ids=ids, dma_engine_mask=m, remote_sem=T.sem[own[0] if own else sem], srcs=[src], dsts=[d for _, d in dsts]))
     g.remote_dma_fused(tr, local_sem=T.sem.ls)
-    return sum(len(e) for _, _, e in moves)
+    return sum(len(mv[2]) for mv in moves)
 
 
 def _codes(T, name, a, b):
@@ -96,11 +106,10 @@ def _hand_on(g, core, T, topo, rank, far):
     eng = topo.engines(core, T.cores[far[0]])
     n_on = len(topo.engines(home, core)) - len(eng)
     a, b = _layout(T, topo)
-    pos = (a + b).index(rank)
 
     def scores(k, w):
         g.wait_ge(T.sem["sr%d" % k], n_on)
-        dst = "fSD" if k == 1 else "fNK"
+        dst = ("fSD", "fNK", "fNL", "fNM")[k - 1]
         to = far[:len(far) // 2] if me < 2 else far[len(far) // 2:]
         return _remote(g, T, topo, core, [(T["fRS%d" % k][:], [(T.cores[r], T[dst][:, 4 * rank:4 * rank + w]) for r in to], eng)], "sa%d" % k)
 
@@ -108,8 +117,9 @@ def _hand_on(g, core, T, topo, rank, far):
         n = NX[x]
         g.wait_ge(T.sem[("qc%d" if codes else "qs%d") % x], n_on)
         mv = []
-        for i, r in enumerate(far):
-            e = eng[2 * i:2 * i + 2]
+        to = [r for r in _owners(x, a + b) if r in far]
+        for i, r in enumerate(to):
+            e = eng if x == 1 else eng[2 * i:2 * i + 2]
             if codes:
                 mv.append((_codes(T, "RC%d" % x, n * i, n * i + n), [(T.cores[r], _codes(T, "LD%d" % x, n * rank, n * rank + n))], e))
             else:
@@ -117,9 +127,12 @@ def _hand_on(g, core, T, topo, rank, far):
         return _remote(g, T, topo, core, mv, "a%d" % x)
 
     def second(x, codes):
-        n = NX[x]
+        own = _owners(x, a + b)
+        if rank not in own:
+            return 0
+        n = NY[x]
         nm, base = LAND[x]
-        base += n * pos
+        base += n * own.index(rank)
         g.wait_ge(T.sem[("wc%d" if codes else "ws%d") % x], n_on)
         if codes:
             mv = [(_codes(T, "RW%d" % x, 0, n), [(T.cores[r], _codes(T, nm, base, base + n)) for r in far], eng)]
@@ -128,11 +141,13 @@ def _hand_on(g, core, T, topo, rank, far):
         return _remote(g, T, topo, core, mv, "b%d" % x)
 
     if me in (1, 2):
-        ls += scores(1, 3)
+        ls += scores(1, 1)
         for x in (1, 3):
             ls += first(x, me == 1)
             ls += second(x, me == 1)
     elif me in (0, 3):
+        ls += scores(3, 1)
+        ls += scores(4, 1)
         ls += first(2, me == 0)
         ls += scores(2, 1)
         ls += second(2, me == 0)
@@ -151,7 +166,6 @@ def rank_program(g, core, T, topo):
     near = [r for r in (pa if rank in pa else pb) if r != rank]
     order = pa + pb
     m = order.index(rank)
-    m0 = order.index(far[0])
     hs = _helpers(core, T.cores[far[0]], topo)
     e_off = topo.engines(core, T.cores[near[0]])
     e_on = [e for e in topo.engines(core, hs[0]) if e not in e_off]
@@ -364,49 +378,51 @@ def rank_program(g, core, T, topo):
         op("v", lambda: g.vector.tensor_copy(T[dst][:, 0:n].bitcast(dt.uint32), T[win][:, a:b].bitcast(dt.uint32).indirect(ap(ov))), [X(win, a, b), ov], [X(dst, 0, n)], el(n, 1.5))
 
     def send1(x, src, s0, between=lambda: None):
-        n = NX[x]
-        p, ps = s0 + n * m0, src + "s"
-        send([(_codes(T, src, p, p + 4 * n), [(hs[0 if x == 2 else 1], _codes(T, "RC%d" % x, 0, 4 * n))], e_on)], "qc%d" % x, [X(src, p, p + 4 * n)])
-        send([(T[ps][:, p:p + 4 * n], [(hs[3 if x == 2 else 2], T["RC%ds" % x][:])], e_on)], "qs%d" % x, [X(ps, p, p + 4 * n)])
+        n, own, ps = NX[x], _owners(x, order), src + "s"
+        fo = [r for r in own if r in far]
+        p, w = s0 + n * own.index(fo[0]), n * len(fo)
+        send([(_codes(T, src, p, p + w), [(hs[0 if x == 2 else 1], _codes(T, "RC%d" % x, 0, w))], e_on)], "qc%d" % x, [X(src, p, p + w)])
+        send([(T[ps][:, p:p + w], [(hs[3 if x == 2 else 2], T["RC%ds" % x][:])], e_on)], "qs%d" % x, [X(ps, p, p + w)])
         mc, mp, rd, rp = [], [], [], []
-        for i, r in enumerate(near):
-            c = s0 + n * order.index(r)
-            e = e_off[2 * i:2 * i + 2]
+        for i, r in enumerate([r for r in near if r in own]):
+            c = s0 + n * own.index(r)
+            e = e_off if x == 1 else e_off[2 * i:2 * i + 2]
             mc.append((_codes(T, src, c, c + n), [(T.cores[r], _codes(T, "LD%d" % x, n * me, n * me + n))], e))
             mp.append((T[ps][:, c:c + n], [(T.cores[r], T["LD%ds" % x][:, n * me:n * me + n])], e))
             rd.append(X(src, c, c + n))
             rp.append(X(ps, c, c + n))
         between()
-        send(mc, "a%d" % x, rd)
-        send(mp, "a%d" % x, rp)
-        dcol("y", "LD%d" % x, n * me, src, s0 + n * m, n)
-        oth = [X(k, n * r, n * r + n) for k in ("LD%d" % x, "LD%ds" % x) for r in range(8) if r != me]
-        arrive(oth, "a%d" % x, 4 * 7, LATE["a%d" % x])
+        if mc:
+            send(mc, "a%d" % x, rd)
+            send(mp, "a%d" % x, rp)
+        if me in own:
+            dcol("y", "LD%d" % x, n * me, src, s0 + n * own.index(me), n)
+            oth = [X(k, n * r, n * r + n) for k in ("LD%d" % x, "LD%ds" % x) for r in range(8) if r != me]
+            arrive(oth, "a%d" % x, 7 * 2 * (len(e_off) if x == 1 else 2), LATE["a%d" % x])
 
     def send2(x):
-        n = NX[x]
+        n, own = NY[x], _owners(x, order)
         nm, base = LAND[x]
-        c = base + n * m
         src = "MG%d" % x
-        two = []
-        for s, hc, h, k in ((src, "RW%d" % x, hs[0 if x == 2 else 1], "wc%d"), (src + "s", "RW%ds" % x, hs[3 if x == 2 else 2], "ws%d")):
-            code = s == src
-            sap = _codes(T, s, 0, n) if code else T[s][:, 0:n]
-            dap = _codes(T, nm, c, c + n) if code else T[nm + "s"][:, c:c + n]
-            hap = _codes(T, hc, 0, n) if code else T[hc][:]
-            send([(sap, [(h, hap)], e_on)], k % x, [X(s, 0, n)])
-            two.append(([(sap, [(T.cores[r], dap) for r in near], e_off)], "b%d" % x, [X(s, 0, n)]))
-        for mv in two:
-            send(*mv)
-        dcol("y", nm, c, src, 0, n)
-        oth = [X(k, base + n * order.index(r), base + n * order.index(r) + n) for k in (nm, nm + "s") for r in range(8) if r != me]
-        arrive(oth, "b%d" % x, 7 * 2 * len(e_off), LATE["b%d" % x])
+        if me in own:
+            c = base + n * own.index(me)
+            for s, hc, h, k in ((src, "RW%d" % x, hs[0 if x == 2 else 1], "wc%d"), (src + "s", "RW%ds" % x, hs[3 if x == 2 else 2], "ws%d")):
+                code = s == src
+                sap = _codes(T, s, 0, n) if code else T[s][:, 0:n]
+                dap = _codes(T, nm, c, c + n) if code else T[nm + "s"][:, c:c + n]
+                hap = _codes(T, hc, 0, n) if code else T[hc][:]
+                send([(sap, [(h, hap)], e_on, k % x), (sap, [(T.cores[r], dap) for r in near], e_off, "b%d" % x)], None, [X(s, 0, n)])
+            dcol("y", nm, c, src, 0, n)
+        oth = [(base + n * i, r) for i, r in enumerate(own) if r != me]
+        arrive([X(k, c, c + n) for k in (nm, nm + "s") for c, r in oth], "b%d" % x, len(oth) * 2 * len(e_off), LATE["b%d" % x])
 
     def send_scores(k, src, c0, w):
         sap = T[src][:, c0:c0 + w]
         rd = [X(src, c0, c0 + w)]
-        send([(sap, [(h, T["fRS%d" % k][:]) for h in (hs[1:3] if k == 1 else (hs[0], hs[3]))], e_on)], "sr%d" % k, rd)
-        send([(sap, [(T.cores[r], T[src][:, c0:c0 + w]) for r in near], e_off)], "sn%d" % k, rd)
+        fm = (sap, [(h, T["fRS%d" % k][:]) for h in (hs[1:3] if k == 1 else (hs[0], hs[3]))], e_on, "sr%d" % k)
+        nm = (sap, [(T.cores[r], T[src][:, c0:c0 + w]) for r in near], e_off, "sn%d" % k)
+        for mv in ([fm], [nm]) if k == 1 else ([fm, nm],):
+            send(mv, None, rd)
         arrive([X(src, 4 * r, 4 * r + w) for r in near], "sn%d" % k, len(near) * len(e_off), LATE["n%d" % k])
         arrive([X(src, 4 * r, 4 * r + w) for r in far], "sa%d" % k, len(far) * len(e_off), LATE["s%d" % k])
 
@@ -424,17 +440,26 @@ def rank_program(g, core, T, topo):
     iota(X("fROW"), [[16, 6], [0, 2], [1, 16]], 0)
     CT = lambda a, b, r0=0, r1=128: X("fCT", a, b, r0, r1)
     iota(CT(96, 128), [[0, 8], [1, 4]], 4 * m)
-    iota(X("fS8"), [[128, 8]], 0)
     iota(X("fJB"), [[16, 6]], 0)
+    e1 = _owners(1, order)
+    cl = [order.index(s) % 2 for s in range(8)]
+    a0, a1 = -cl[me] % 2, (1 - cl[me]) % 2
+    iota(X("fPR"), [[a1 - a0, 2], [0, 2], [2, 16]], a0)
+    if me in e1:
+        ow = e1.index(me)
+        pairs = [(order[2 * q + ow], order[2 * q + 1 - ow]) for q in range(4)]
+        for q, (s0, s1) in enumerate(pairs):
+            iota(X("fGR", 32 * q, 32 * q + 32), [[2, 16], [1 + 32 * (s1 - s0), 2]], 32 * s0)
     ms(X("ONB"), 1.0)
     ms(X("fON"), 1.0)
     ms(X("HAF"), 0.5)
     ms(CT(192, 320, 0, 64), -1000.0)
     ms(CT(320, 384, 64, 128), -1000.0)
     op("g", lambda: g.affine_select(T.DG[:], T.HAF[:], [[-1, 128]], O.is_equal, 0.0, 0, 1), [X("HAF")], [X("DG")], 0.4)
-    for i, k in enumerate((31, 15, 3)):
+    for i, k in enumerate((31, 15, 3, 1)):
         op("v", lambda k=k, i=i: g.vector.tensor_scalar(T.PJ[:, i:i + 1], T.PI[:], k, None, O.bitwise_and), [X("PI")], [X("PJ", i, i + 1)], el(1))
-    cp(X("fPC", 0, 3), X("PJ"))
+    cp(X("fPC", 0, 3), X("PJ", 0, 3))
+    cp(X("fPA", 0, 1), X("PJ", 3, 4))
     P32, P16, P4 = X("fPC", 0, 1), X("fPC", 1, 2), X("fPC", 2, 3)
     for a in range(4):
         ts(X("fLC", 0, 1, 32 * a, 32 * a + 32), X("fPC", 0, 1, 32 * a, 32 * a + 32), 32.0 * (a % 2), O.add)
@@ -480,17 +505,50 @@ def rank_program(g, core, T, topo):
             ts(X("fHL", 96 * i + 32 * b, 96 * i + 32 * b + 32), X("fTL"), X("fRB", b, b + 1), O.is_equal, val(b), O.mult)
         tr(X("fHT", 96 * i, 96 * i + 96), X("fHL", 96 * i, 96 * i + 96))
         total(X("fSD", 4 * me + i, 4 * me + i + 1), X("fHT", 96 * i, 96 * i + 96))
-    send_scores(1, "fSD", 4 * me, 3)
+    send_scores(1, "fSD", 4 * me, 1)
+
+    B0 = lambda n, c0=0, c1=None: X(n, c0, c1, 0, 32)
+    ts(B0("fPM"), B0("fPR"), B0("fPC", 0, 1), O.is_equal)
+    times(B0("fHP"), B0("fPM"), B0("fSD", 4 * me + 1, 4 * me + 2))
+    tr(B0("fHPt"), B0("fHP"))
+    total(B0("fDL", 0, 1), B0("fHPt", 0, 32))
+    total(B0("fDL", 1, 2), B0("fHPt", 32, 64))
+    for d in range(4):
+        cp(("DPo", 0, 2, 32 * d, 32 * d + 32, 1), ("fW",) + X("fDL")[1:3] + (0, 32, 1))
+    pick("SL1", 32, "QT", 96, 192, ("DPo", 0))
+    send1(1, "SL1", 0)
 
     LCv = X("fLC")
     ts(CT(0, 64), X("fROW", 0, 64), LCv, O.subtract)
     ts(CT(64, 96), X("fR96", 0, 32), LCv, O.subtract)
     ts(CT(128, 160), X("fR96", 0, 32), LCv, O.subtract, 32.0, O.add)
     ts(CT(96, 128), CT(96, 128), P32, O.is_equal)
-    ts(CT(384, 416), X("fROW", 0, 32), 12.0, O.is_ge, -1000.0, O.mult)
-    tt(CT(160, 192), CT(384, 416), X("fROW", 0, 32), O.add)
-    for i in range(3):
-        ts(X("fMM", 32 * i, 32 * i + 32), CT(160, 192), 12.0 * m - 32.0 * i, O.add, P32, O.is_equal)
+    x2 = _owners(2, order)
+    if me in x2:
+        ts(X("fMM", 0, 32), X("fROW", 0, 32), 16.0 * (x2.index(me) % 2), O.add, P32, O.is_equal)
+    ts(X("fGV", 0, 1), X("fSD", 4 * me + 1, 4 * me + 2), 128.0 * me, O.add)
+    cp(X("fGV", 1, 2, 32, 64), X("fGV", 0, 1, 32, 64))
+    cp(X("fGV", 1, 2, 64, 128), X("fGV", 0, 1, 64, 128))
+    ts(B0("fNS2"), B0("fPA", 0, 1), float(cl[me]), O.not_equal, 1024.0, O.mult)
+    tt(B0("fGV", 1, 2), B0("fGV", 0, 1), B0("fNS2"), O.add)
+    ms(X("fNL", 4 * me, 4 * me + 1, 96, 128), 0.0)
+    for h in range(2):
+        ts(X("fKC", h, h + 1), P16, 16.0 * h, O.add)
+        ts(X("fKM", 32 * h, 32 * h + 32), X("fR96", 0, 32), X("fKC", h, h + 1), O.is_equal, 64.0, O.mult)
+        ts(X("fOT", 32 * h, 32 * h + 32), X("fR96", 0, 32), X("fKC", h, h + 1), O.is_lt)
+    tt(X("fKM"), X("fKM"), X("fOT"), O.add)
+    if me in e1:
+        par, npar = B0("fPA", 0, 1), B0("fPA", 1, 2)
+        ts(npar, par, -1.0, O.mult, 1.0, O.add)
+        ts(B0("fPA", 2, 3), B0("fPC", 0, 1), 0.5, O.mult)
+        for q, (s0, s1) in enumerate(pairs):
+            ts(B0("fAD", q, q + 1), par, 16.0 * (s1 - s0) - 0.5, O.mult, 16.0 * s0, O.add)
+            tt(B0("fAD", q, q + 1), B0("fAD", q, q + 1), B0("fPA", 2, 3), O.add)
+            ts(B0("fGP", q, q + 1), par, 32.0 * (s1 - s0), O.mult, B0("fPC", 0, 1), O.add)
+            ts(B0("fGP", q, q + 1), B0("fGP", q, q + 1), 32.0 * s0, O.add)
+            ff = B0("fFF", 128 * q, 128 * q + 128)
+            ts(ff, B0("fGR"), B0("fGP", q, q + 1), O.is_ge, -step, O.mult)
+            ts(ff, ff, 1.0, O.add)
     ts(CT(192, 320, 64, 128), X("fROW", 0, 128, 64, 128), X("fLC", 0, 1, 64, 128), O.subtract)
     ts(CT(320, 384, 0, 64), X("fROW", 0, 64, 0, 64), X("fLC", 0, 1, 0, 64), O.subtract, 32.0, O.add)
     ts(X("fPT"), X("fROW"), 128.0 * me, O.add)
@@ -514,18 +572,6 @@ def rank_program(g, core, T, topo):
     def key(s):
         return X("fSD", 4 * s, 4 * s + 1)
 
-    def expand(e, col, rows):
-        for s in range(8):
-            times(X(e, 32 * s, 32 * s + 32), X("fON"), col(s))
-        tr(X(rows), X(e))
-
-    def compare(buf, rows, s):
-        if s:
-            ts(X(buf, 224 * s, 224 * s + 32 * s), X(rows, 0, 32 * s), key(s), O.is_ge)
-        if s < 7:
-            ts(X(buf, 224 * s + 32 * s, 224 * s + 224), X(rows, 32 * s + 32, 256), key(s), O.is_gt)
-        return X(buf, 224 * s, 224 * s + 224)
-
     def rows4(v, a):
         return (v[0], v[1], v[2], 32 * a, 32 * a + 32, v[5])
 
@@ -535,33 +581,88 @@ def rank_program(g, core, T, topo):
 
     times(X("fEO"), X("fON"), key(me))
     tr(X("fRO"), X("fEO"))
+    planes = (pa, pb) if rank in pa else (pb, pa)
     for i, grp in enumerate((near, far)):
-        n = 32 * len(grp)
+        n, pl = 32 * len(grp), planes[i]
+        for a in range(4):
+            cp(X("fSWA", 4 * i, 4 * i + 4, 32 * a, 32 * a + 32), ("fSD", 4 * pl[0], 4 * pl[-1] + 1, 32 * (a ^ 1), 32 * (a ^ 1) + 32, 4 * (pl[1] - pl[0])))
         for j, s in enumerate(grp):
-            ts(X("fCW", 128 * i + 32 * j, 128 * i + 32 * j + 32), X("fRO"), key(s), O.is_le if s < me else O.is_lt)
-        tr(X("fCV", 128 * i, 128 * i + n), X("fCW", 128 * i, 128 * i + n))
-        total(X("fNF", i, i + 1), X("fCV", 128 * i, 128 * i + n))
+            o = O.is_le if s < me else O.is_lt
+            w = 4 * i + pl.index(s)
+            ts(X("fCW", 128 * i + 32 * j, 128 * i + 32 * j + 32), X("fRO"), key(s), o)
+            ts(X("fCX", 128 * i + 32 * j, 128 * i + 32 * j + 32), X("fRO"), X("fSWA", w, w + 1), o)
+        for k, (w, v) in enumerate((("fCW", "fCV"), ("fCX", "fCY"))):
+            tr(X(v, 128 * i, 128 * i + n), X(w, 128 * i, 128 * i + n))
+            total(X("fNF", 2 * k + i, 2 * k + i + 1), X(v, 128 * i, 128 * i + n))
         if i == 0:
             ts(X("fCTO"), CT(0, 64), X("fNF", 0, 1), O.subtract)
+            tt(X("fNF", 2, 3), X("fNF", 0, 1), X("fNF", 2, 3), O.add)
+    ts(X("fCN"), X("fNF", 0, 1), X("fNF", 1, 2), O.add)
+    ts(X("fCF"), X("fNF", 2, 3), X("fNF", 1, 2), O.add, X("fNF", 3, 4), O.add)
+    NL = lambda a, n="fNL": X(n, 4 * me, 4 * me + 1, 32 * a, 32 * a + 32)
+    T4 = lambda a, c: X("fT4", c, c + 1, 32 * a, 32 * a + 32)
+    TS = lambda a, c: X("fTS", c, c + 1, 32 * a, 32 * a + 32)
+    entries = lambda i, t, n, v: ts(X("fHN", 32 * i, 32 * i + 32), t, X(n), O.is_equal, v, O.mult)
+    entries(0, CT(64, 96), "fCN", X("fGV", 1, 2))
+    entries(1, CT(64, 96), "fCN", X("fSD", 4 * me + 2, 4 * me + 3))
+    tr(X("fHM", 0, 64), X("fHN", 0, 64))
+    for a in (0, 2):
+        total(NL(a), X("fHM", 0, 32, 32 * a, 32 * a + 32))
+    total(T4(2, 0), X("fHM", 32, 64, 64, 96))
+    cp(NL(1), T4(2, 0))
+    send_scores(3, "fNL", 4 * me, 1)
+
+    if me in e1:
+        nq = [2 * ow, 2 * ow + 1]
+        n0, f0 = 64 * ow, 64 - 64 * ow
+        for q in nq + [q for q in range(4) if q not in nq]:
+            k4 = B0("fK4", q, q + 1)
+            times(B0("fKT", q, q + 1), par, B0("fSD", 4 * pairs[q][1], 4 * pairs[q][1] + 1))
+            ts(k4, npar, B0("fSD", 4 * pairs[q][0], 4 * pairs[q][0] + 1), O.mult, B0("fKT", q, q + 1), O.add)
+            times(B0("fKE", 32 * q, 32 * q + 32), B0("fON"), k4)
+            if q % 2:
+                tr(B0("fKR", 32 * q - 32, 32 * q + 32), B0("fKE", 32 * q - 32, 32 * q + 32))
+
+        def ahead(q, c0, c1, out):
+            w, c = B0("fWW", 128 * q + c0, 128 * q + c1), B0("fCC", 128 * q + c0, 128 * q + c1)
+            tt(w, B0("fKR", c0, c1), B0("fFF", 128 * q + c0, 128 * q + c1), O.mult)
+            ts(c, w, B0("fK4", q, q + 1), O.is_ge)
+            total(out, c)
+
+        for i, q in enumerate(nq):
+            ahead(q, n0, n0 + 64, B0("fN1", q, q + 1))
+            ts(B0("fCO", 64 * i, 64 * i + 64), B0("fROW", 0, 64), B0("fN1", q, q + 1), O.subtract)
+        for q in range(4):
+            if q in nq:
+                ahead(q, f0, f0 + 64, B0("fRB2", q, q + 1))
+            else:
+                ahead(q, 0, 128, B0("fRB2", q, q + 1))
+            for h in range(2):
+                t = B0("fCO", 64 * nq.index(q) + 32 * h, 64 * nq.index(q) + 32 * h + 32) if q in nq else B0("fROW", 32 * h, 32 * h + 32)
+                ts(B0("fHO", 128 * h + 32 * q, 128 * h + 32 * q + 32), t, B0("fRB2", q, q + 1), O.is_equal, B0("fAD", q, q + 1), O.mult)
+        for h in range(2):
+            tr(B0("fHQ", 128 * h, 128 * h + 128), B0("fHO", 128 * h, 128 * h + 128))
+            total(B0("fMO", h, h + 1), B0("fHQ", 128 * h, 128 * h + 128))
+        for d in range(4):
+            cp(("O1o", 0, 2, 32 * d, 32 * d + 32, 1), B0("fMO"))
+        pick("MG1", 32, "LD1", 0, 128, ("O1o", 0))
+    send2(1)
+
+    entries(2, CT(128, 160), "fCF", X("fGV", 0, 1))
+    entries(3, CT(128, 160), "fCF", key(me))
+    tr(X("fHM", 64, 128), X("fHN", 64, 128))
+    for i in (2, 3):
+        total(X("fT4", i, i + 1), X("fHM", 32 * i, 32 * i + 32))
+    for a in range(4):
+        c = 2 if a % 2 else 3
+        cp(TS(a, c - 2), T4(a ^ 1, c))
+        tt(NL(a, "fNM"), T4(a, c), TS(a, c - 2), O.add)
+    send_scores(4, "fNM", 4 * me, 1)
+
     ts(X("fH1"), X("fCTO"), X("fNF", 1, 2), O.is_equal, X("fSD", 4 * me + 1, 4 * me + 2), O.mult)
     tr(X("fH1t"), X("fH1"))
     total(X("fOL", 0, 1), X("fH1t", 0, 32))
     total(X("fOL", 1, 2), X("fH1t", 32, 64))
-    to_all(X("DPo"), X("fOL"), 0)
-    pick("SL1", 32, "QT", 96, 192, ("DPo", 0))
-    send1(1, "SL1", 0)
-
-    expand("fEA", key, "fRA")
-    tt(X("fCN", me, me + 1), X("fNF", 0, 1), X("fNF", 1, 2), O.add)
-    others = [s for s in range(8) if s != me]
-    for s in others:
-        total(X("fCN", s, s + 1), compare("fCA", "fRA", s))
-
-    def listed(k, tgt, cn, val, out):
-        for s in range(8):
-            ts(X("fHB", 256 * k + 32 * s, 256 * k + 32 * s + 32), tgt, X(cn, s, s + 1), O.is_equal, val(s), O.mult)
-        tr(X("fSB", 256 * k, 256 * k + 256), X("fHB", 256 * k, 256 * k + 256))
-        total(out, X("fSB", 256 * k, 256 * k + 256))
 
     def owners(parts, mul, add, i):
         n = len(parts)
@@ -573,22 +674,8 @@ def rank_program(g, core, T, topo):
         cp(X("MI", i, i + 1), X("fOM", 2 * i + 1, 2 * i + 2))
         ts(X("Mo", 2 * i, 2 * i + 1), X("MI", i, i + 1), float(mul), O.mult, add, O.add)
 
-    tt(X("fGID"), ("fSD", 1, 32, 0, 128, 4), X("fS8"), O.add)
-    gid = lambda s: X("fGID", s, s + 1)
-    listed(0, CT(64, 96), "fCN", gid, X("fG4", 4, 5))
-    L1g, L2g, D1g, H2g = (X("fG4", i, i + 1) for i in range(4))
-    to_all(D1g, X("fG4", 4, 5), 0)
-    owners([(CT(96, 128), D1g)], 4, P4, 0)
-    pick("MG1", 16, "LD1", 0, 32, ("Mo", 0))
-    send2(1)
-
-    for a in range(4):
-        cp(X("fSWK", 0, 8, 32 * a, 32 * a + 32), ("fSD", 0, 32, 32 * (a ^ 1), 32 * (a ^ 1) + 32, 4))
-    expand("fEB", lambda s: X("fSWK", s, s + 1), "fRBW")
-    total(X("fCBN", me, me + 1), compare("fCB", "fRBW", me))
-    tt(X("fCF", me, me + 1), X("fCN", me, me + 1), X("fCBN", me, me + 1), O.add)
     tt(X("fVO", 1, 2), X("fVO", 0, 1), X("fSD", 4 * me + 1, 4 * me + 2), O.add)
-    ts(X("fH2"), CT(192, 384), X("fCF", me, me + 1), O.is_equal, X("fVO", 1, 2), O.mult)
+    ts(X("fH2"), CT(192, 384), X("fCF"), O.is_equal, X("fVO", 1, 2), O.mult)
     tr(X("fH2t"), X("fH2"))
     for c in range(6):
         total(X("fOX", c, c + 1), X("fH2t", 32 * c, 32 * c + 32))
@@ -600,28 +687,36 @@ def rank_program(g, core, T, topo):
     pick("SL2", 96, "QT", 0, 192, ("X2o", 0))
     send1(2, "SL2", 0)
 
+    L1q, L2g, D1g, H2g = (X("fG4", i, i + 1) for i in range(4))
+    red(X("fG2", 0, 1), ("fNL", 0, 32, 0, 128, 4))
+    DQ = X("fDQ")
+    to_all(DQ, X("fG2", 0, 1), 0)
+    ts(X("fOE"), X("fON"), DQ, O.mult, 1024.0, O.is_ge)
+    tr(X("fOR"), X("fOE"))
+    for h in range(2):
+        tt(X("fOT", 32 * h, 32 * h + 32), X("fOR"), X("fKM", 32 * h, 32 * h + 32), O.mult)
+        total(X("fQ1", h, h + 1), X("fOT", 32 * h, 32 * h + 32))
+    tt(X("fQA"), X("fKC"), X("fQ1"), O.subtract)
+    for h in range(2):
+        ts(X("UOo", h, h + 1), X("fQ1", h, h + 1), 46.0, O.subtract, X("fQA", h, h + 1), O.max)
+    pick("UD", 32, "UO", 0, 36, ("UOo", 0))
+    red(X("fG2", 1, 2), ("fNM", 0, 32, 0, 128, 4))
+    for a in range(4):
+        to_all(X("fGA", 2 * a, 2 * a + 2), X("fG2"), a)
+    _, c2k, z1, c2g, L1g, o2k, _, o2g = (X("fGA", i, i + 1) for i in range(8))
+    ts(D1g, DQ, 1024.0, O.is_ge, -1024.0, O.mult)
+    tt(D1g, D1g, DQ, O.add)
+
     to_all(X("LPo"), X("fOL"), 2)
     pick("NP1", 32, "QT", 192, 288, ("LPo", 0))
     for b in range(4):
         mm("p%d" % (2 + b), 128, "EQ", 128 * b, "NP1", 0, True, False)
-    to_all(L1g, X("fG4", 4, 5), 2)
     ts(X("fOW", 0, 1), L1g, 128.0 * me, O.is_ge)
     ts(X("fOW", 1, 2), L1g, 128.0 * me + 128, O.is_lt)
     tt(X("fOW", 2, 3), X("fOW", 0, 1), X("fOW", 1, 2), O.mult)
     ts(X("fIDW"), X("fR96", 0, 32), P32, O.is_equal, X("fOW", 2, 3), O.mult)
-    for s in others:
-        total(X("fCBN", s, s + 1), compare("fCB", "fRBW", s))
-    for s in others:
-        tt(X("fCF", s, s + 1), X("fCN", s, s + 1), X("fCBN", s, s + 1), O.add)
-    listed(1, CT(128, 160), "fCF", gid, X("fLB", 0, 1))
-    listed(2, CT(128, 160), "fCF", key, X("fLB", 1, 2))
-    listed(3, CT(64, 96), "fCF", lambda s: X("fSD", 4 * s + 2, 4 * s + 3), X("fLB", 2, 3))
-    for a in range(4):
-        to_all(X("fXB", 4 * a, 4 * a + 3), X("fLB", 0, 3), a)
-    tt(X("fSX", 0, 3), X("fXB", 0, 3), X("fXB", 4, 7), O.add)
-    tt(X("fSX", 4, 7), X("fXB", 8, 11), X("fXB", 12, 15), O.add)
-    c2g, c2k, o2g, o2k, z1 = X("fSX", 0, 1), X("fSX", 1, 2), X("fSX", 4, 5), X("fSX", 5, 6), X("fSX", 6, 7)
-    owners([(X("fMM", 32 * i, 32 * i + 32), c) for i, c in enumerate((L1g, o2g, c2g)) if 12 * m < 32 * i + 32 and 12 * m + 12 > 32 * i], 12, P16, 2)
+    if me in x2:
+        owners([(X("fMM", 0, 32), (L1g, o2g, c2g)[x2.index(me) // 2])], 16, P16, 2)
     owners([(CT(96, 128), L1g)], 4, P4, 1)
 
     def new(nt, q0):
@@ -636,7 +731,8 @@ def rank_program(g, core, T, topo):
     tt(X("fSC"), X("p6", 0, 32), X("fIDW"), O.mult)
     red(X("fNK", 4 * me, 4 * me + 1), X("fSC"), O.add, True, True)
     send1(3, "QT", 288, lambda: send_scores(2, "fNK", 4 * me, 1))
-    pick("MG2", 16, "LD2", 0, 96, ("Mo", 4))
+    if me in x2:
+        pick("MG2", 16, "LD2", 0, 128, ("Mo", 4))
     send2(2)
 
     tiles = {"": ("fEP", "fEQr", "fMK", "fMG", "fMT", "fMH", "fML")}
@@ -736,6 +832,7 @@ def rank_program(g, core, T, topo):
     dma("y", T.oc[:, 384:768], _codes(T, "DF", 0, 96), [X("DF", 0, 96)], [])
     for k in range(4):
         dma("a" if k % 2 else "y", T.osc[4 * k:4 * k + 4, 96:192], T.DFs[32 * k:32 * k + 4, 0:96], [X("DFs", 0, 96)], [])
+    cp(L1q, L1g)
     cp(X("GI"), X("fG4", 0, 4))
     op("v", lambda: g.vector.tensor_scalar(T.GJ[:], T.GI[:], 7, None, O.arith_shift_right), [X("GI")], [X("GJ")], el(1))
     ts(X("GK"), X("GJ"), -32, O.mult)

import numpy as np
from concourse.bass import DstId, RemoteDMATransfer
from concourse.mybir import dt, AluOpType, AxisListType, ActivationFunctionType

O = AluOpType
AF = ActivationFunctionType
P = 96
F32, BF, I32, U16 = "float32", "bfloat16", "int32", "uint16"
SCRATCH = {
    "BT": ("sbuf", [128, 1152], BF), "WT": ("sbuf", [128, 512], BF), "UZ": ("sbuf", [128, 8], BF),
    "UT": ("sbuf", [128, 512], BF), "ZT": ("sbuf", [128, 512], BF), "ONB": ("sbuf", [128, 128], BF),
    "HAF": ("sbuf", [128, 128], BF), "DG": ("sbuf", [128, 128], BF), "ET": ("sbuf", [128, 2048], BF),
    "NT0": ("sbuf", [128, 512], BF), "NT1": ("sbuf", [128, 512], BF),
    "PI": ("sbuf", [128, 1], I32), "PJ": ("sbuf", [128, 4], I32), "MI": ("sbuf", [128, 3], I32),
    "DPo": ("sbuf", [128, 2], U16), "LPo": ("sbuf", [128, 2], U16), "Mo": ("sbuf", [128, 6], U16),
    "O1o": ("sbuf", [128, 2], U16), "UOo": ("sbuf", [128, 2], U16), "X2o": ("sbuf", [128, 6], U16), "B2o": ("sbuf", [128, 2], U16), "N2o": ("sbuf", [128, 2], U16),
    "FLo": ("sbuf", [128, 8], U16), "FDo": ("sbuf", [128, 6], U16), "GI": ("sbuf", [128, 4], I32), "GJ": ("sbuf", [128, 4], I32),
    "GK": ("sbuf", [128, 4], I32),
}
for _n, _w in {"QT": 544, "UQ": 128, "ZQ": 128, "EQ": 512, "WQ": 128, "SL1": 32, "LD1": 128, "MG1": 32, "UO": 36, "UD": 128, "SL2": 96,
               "LD2": 128, "MG2": 16, "LD3": 32, "MG3": 16, "DW": 224, "NP1": 128, "BP2": 128, "NP2": 128, "LF": 128, "DF": 96}.items():
    SCRATCH[_n] = ("sbuf", [128, _w], "float8_e4m3fn_x4")
    SCRATCH[_n + "s"] = ("sbuf", [128, _w], "uint8")
for _x, _n, _w in ((1, 16, 18), (2, 48, 16), (3, 16, 4)):
    SCRATCH["RC%d" % _x] = ("sbuf", [128, _n], "float8_e4m3fn_x4")
    SCRATCH["RC%ds" % _x] = ("sbuf", [128, _n], "uint8")
    SCRATCH["RW%d" % _x] = ("sbuf", [128, _w], "float8_e4m3fn_x4")
    SCRATCH["RW%ds" % _x] = ("sbuf", [128, _w], "uint8")
_F = {"RS1": 1, "RS2": 1, "RS3": 1, "RS4": 1, "SD": 32, "NL": 32, "NM": 32, "DQ": 1, "GV": 2, "CX": 256, "CY": 256, "SWA": 8, "HN": 128, "HM": 128,
      "T4": 4, "TS": 2, "G2": 2, "GA": 8, "NS2": 1, "NK": 32, "ON": 32, "ROW": 192, "R96": 96, "PC": 8, "LC": 1, "TL": 32, "CT": 416, "UZ": 8,
      "FT": 96, "FK": 96, "JB": 6, "PT": 192, "K0": 192, "KK": 192, "TT": 192, "KF": 96, "TF": 96, "CL": 288, "RB": 4,
      "EO": 32, "RO": 32, "CW": 256, "CV": 256, "NF": 4, "CN": 1, "CF": 1, "CTO": 64, "IDW": 32, "RP": 96,
      "HL": 288, "HT": 288, "H1": 64, "H1t": 64, "OL": 2,
      "VO": 2, "H2": 192, "H2t": 192, "OX": 6, "XO": 24, "XP": 18,
      "OW": 4, "MM": 32, "MW": 384, "MV": 384, "OM": 6,
      "SC": 32, "NS": 4, "FM": 12, "FH": 768, "FR": 24, "FL": 6, "FD": 6, "Y": 96, "G4": 8, "G4t": 64, "NB": 1,
      "PR": 64, "PM": 64, "HP": 64, "HPt": 64, "DL": 2, "OE": 32, "OR": 32, "KM": 64, "OT": 64, "Q1": 2, "KC": 2, "QA": 2, "PA": 4,
      "K4": 4, "KT": 4, "KE": 128, "KR": 128, "GR": 128, "GP": 4, "FF": 512, "WW": 512, "CC": 512, "N1": 4, "RB2": 4, "CO": 128, "AD": 4,
      "HO": 256, "HQ": 256, "MO": 2,
      "FT0": 192, "FT1": 192, "FT2": 192, "FT3": 192}
for _n, _w in (("EP", 128), ("EQr", 128), ("MK", 128), ("MG", 192), ("MT", 512), ("MH", 640), ("ML", 16)):
    _F[_n] = _F[_n + "b"] = _w
_AT, _o = {}, 0
for _n, _w in _F.items():
    if _n in ("RS1", "RS2", "RS3", "RS4", "SD", "NL", "NM", "NK", "Y", "G4t"):
        SCRATCH["f" + _n] = ("sbuf", [128, _w], F32)
    else:
        _AT["f" + _n] = (_o, _w)
        _o += -(-_w // 32) * 32
SCRATCH["fW"] = ("sbuf", [128, _o], F32)
for _i in range(8):
    SCRATCH["p%d" % _i] = ("psum", [128, 512], F32)
SEMAPHORES = ["vs", "ac", "te", "gp", "ls"] + [_s + str(_k) for _k in (1, 2, 3, 4) for _s in ("sa", "sn", "sr")]
for _x in (1, 2, 3):
    SEMAPHORES += ["a%d" % _x, "b%d" % _x, "qc%d" % _x, "qs%d" % _x, "wc%d" % _x, "ws%d" % _x]
SEMAPHORES += ["d%d" % _i for _i in range(60)]
WAKE, PIPE, CYCLE, SLACK = 0.1, 0.06, 0.00083, 0.03
LATE = {"n1": 2.53, "s1": 3.9, "a1": 4.9, "b1": 2.63, "n3": 1.9, "s3": 2.97, "n4": 1.9, "s4": 3.09, "n2": 2.14, "s2": 5.03, "a2": 4.51, "b2": 5.0,
        "a3": 3.82, "b3": 2.45}
NX = {1: 16, 2: 16, 3: 4}
NY = {1: 18, 2: 16, 3: 4}
LAND = {1: ("UO", 0), 2: ("DW", 96), 3: ("DW", 192)}


def _layout(T, topo):
    ranks = T.cores
    a = [r for r in range(8) if r == 0 or topo.same_plane(ranks[0], ranks[r])]
    b = [r for r in range(8) if r not in a]
    return a, b


def _owners(x, order):
    return {1: [order[0], order[4]], 2: order[1:4] + order[5:8], 3: order}[x]


def _helpers(home, far, topo):
    h = [c for c in topo.cores_of(home) if c != home and topo.may_write(c, far)]
    return sorted(h, key=lambda c: (topo.die(c) != topo.die(home), c))


def _remote(g, T, topo, core, moves, sem):
    tr = []
    for src, dsts, eng, *own in moves:
        ids = []
        for c, _ in dsts:
            rid, pid = topo.addr(c, core)
            ids.append(DstId(rid=rid, pnc=pid))
        m = 0
        for e in eng:
            m |= 1 << e
        tr.append(RemoteDMATransfer(dst_ids=ids, dma_engine_mask=m, remote_sem=T.sem[own[0] if own else sem], srcs=[src], dsts=[d for _, d in dsts]))
    g.remote_dma_fused(tr, local_sem=T.sem.ls)
    return sum(len(mv[2]) for mv in moves)


def _codes(T, name, a, b):
    return T[name][:, a:b].bitcast(dt.uint8)


def _hand_on(g, core, T, topo, rank, far):
    home = T.cores[rank]
    hs = _helpers(home, T.cores[far[0]], topo)
    if core not in hs:
        return
    me, ls = hs.index(core), 0
    eng = topo.engines(core, T.cores[far[0]])
    n_on = len(topo.engines(home, core)) - len(eng)
    a, b = _layout(T, topo)

    def scores(k, w):
        g.wait_ge(T.sem["sr%d" % k], n_on)
        dst = ("fSD", "fNK", "fNL", "fNM")[k - 1]
        to = far[:len(far) // 2] if me < 2 else far[len(far) // 2:]
        return _remote(g, T, topo, core, [(T["fRS%d" % k][:], [(T.cores[r], T[dst][:, 4 * rank:4 * rank + w]) for r in to], eng)], "sa%d" % k)

    def first(x, codes):
        n = NX[x]
        g.wait_ge(T.sem[("qc%d" if codes else "qs%d") % x], n_on)
        mv = []
        to = [r for r in _owners(x, a + b) if r in far]
        for i, r in enumerate(to):
            e = eng if x == 1 else eng[2 * i:2 * i + 2]
            if codes:
                mv.append((_codes(T, "RC%d" % x, n * i, n * i + n), [(T.cores[r], _codes(T, "LD%d" % x, n * rank, n * rank + n))], e))
            else:
                mv.append((T["RC%ds" % x][:, n * i:n * i + n], [(T.cores[r], T["LD%ds" % x][:, n * rank:n * rank + n])], e))
        return _remote(g, T, topo, core, mv, "a%d" % x)

    def second(x, codes):
        own = _owners(x, a + b)
        if rank not in own:
            return 0
        n = NY[x]
        nm, base = LAND[x]
        base += n * own.index(rank)
        g.wait_ge(T.sem[("wc%d" if codes else "ws%d") % x], n_on)
        if codes:
            mv = [(_codes(T, "RW%d" % x, 0, n), [(T.cores[r], _codes(T, nm, base, base + n)) for r in far], eng)]
        else:
            mv = [(T["RW%ds" % x][:], [(T.cores[r], T[nm + "s"][:, base:base + n]) for r in far], eng)]
        return _remote(g, T, topo, core, mv, "b%d" % x)

    if me in (1, 2):
        ls += scores(1, 1)
        for x in (1, 3):
            ls += first(x, me == 1)
            ls += second(x, me == 1)
    elif me in (0, 3):
        ls += scores(3, 1)
        ls += scores(4, 1)
        ls += first(2, me == 0)
        ls += scores(2, 1)
        ls += second(2, me == 0)
    g.wait_ge(T.sem.ls, ls)


def rank_program(g, core, T, topo):
    rank = T.rank_of(core)
    pa, pb = _layout(T, topo)
    if rank is None:
        for r in range(8):
            if core in topo.cores_of(T.cores[r]):
                _hand_on(g, core, T, topo, r, pb if r in pa else pa)
        return
    far = pb if rank in pa else pa
    near = [r for r in (pa if rank in pa else pb) if r != rank]
    order = pa + pb
    m = order.index(rank)
    hs = _helpers(core, T.cores[far[0]], topo)
    e_off = topo.engines(core, T.cores[near[0]])
    e_on = [e for e in topo.engines(core, hs[0]) if e not in e_off]
    me = rank

    Q = {"v": g.vector, "a": g.scalar, "t": g.tensor, "g": g, "y": g.sync}
    SEM = {"v": "vs", "a": "ac", "t": "te", "g": "gp"}
    acc, waited, know, cnt = {}, {q: {} for q in Q}, {}, {}
    nd, ls, sent = [0], [0], []

    def X(name, c0=0, c1=None, r0=0, r1=128, st=1):
        o, w = _AT[name] if name in _AT else (0, SCRATCH[name][1][1])
        return ("fW" if name in _AT else name, o + c0, o + (w if c1 is None else c1), r0, r1, st)

    def ap(v):
        n, c0, c1, r0, r1, st = v
        if (r0, r1) == (0, 128):
            return T[n][:, c0:c1] if st == 1 else T[n][:, c0:c1:st]
        return T[n][r0:r1, c0:c1] if st == 1 else T[n][r0:r1, c0:c1:st]

    def width(v):
        return -(-(v[2] - v[1]) // v[5])

    def hit(a, b):
        if a[4] <= b[3] or b[4] <= a[3] or a[2] <= b[1] or b[2] <= a[1]:
            return False
        return not (a[5] == b[5] > 1 and (a[1] - b[1]) % a[5])

    def norm(v):
        return (v[0], 0, 512, 0, 128, 1) if SCRATCH[v[0]][0] == "psum" else v

    def enter(book, reads, writes, tag, q):
        for v in writes:
            nv = norm(v)
            book[v[0]] = [e for e in book.get(v[0], []) if not (nv[1] <= e[0][1] and e[0][2] <= nv[2] and nv[3] <= e[0][3] and e[0][4] <= nv[4] and nv[5] == 1)]
            book[v[0]].append((nv, True, tag, q))
        for v in reads:
            book.setdefault(v[0], []).append((norm(v), False, tag, q))

    def pre(q, reads, writes):
        need = {}
        for vs, w in ((reads, False), (writes, True)):
            for v in vs:
                ps = SCRATCH[v[0]][0] == "psum"
                for r, iw, ev, eq in acc.get(v[0], []):
                    if (iw or w or (ps and eq != q)) and hit(r, norm(v)):
                        if ps and q == "t" and eq == "t" and w:
                            continue
                        need[ev[0]] = max(need.get(ev[0], 0), ev[1])
        for s in sorted(need, key=lambda s: (s in ("vs", "ac", "te"), s)):
            if waited[q].get(s, 0) < need[s]:
                Q[q].wait_ge(T.sem[s], need[s])
                for s2, n2 in know.get((s, need[s]), {}).items():
                    waited[q][s2] = max(waited[q].get(s2, 0), n2)
                waited[q][s] = need[s]

    def post(q, reads, writes, ev):
        know[ev] = dict(waited[q])
        enter(acc, reads, writes, ev, q)

    nodes, seen = [], {}

    def note(ways, reads, writes, after=(), late=0.0):
        k = len(nodes)
        pr = set(after)
        q0 = list(ways)[0] if len(ways) == 1 else ""
        for vs, w in ((reads, False), (writes, True)):
            for v in vs:
                ps = SCRATCH[v[0]][0] == "psum"
                for r, iw, i, q in seen.get(v[0], []):
                    if i != k and (iw or w or (ps and (q != q0 or not q))) and hit(r, norm(v)):
                        pr.add(i)
        enter(seen, reads, writes, k, q0)
        nodes.append((ways, pr, late))
        return k

    def schedule():
        n = len(nodes)
        succ = [[] for _ in range(n)]
        for k, (_, pr, _) in enumerate(nodes):
            for p in pr:
                succ[p].append(k)
        dur = [min(c for _, c in w.values()) + late for w, _, late in nodes]
        path = [0.0] * n
        for k in range(n - 1, -1, -1):
            path[k] = dur[k] + max([path[x] + WAKE for x in succ[k]], default=0.0)
        left = [len(pr) for _, pr, _ in nodes]
        at = [0.0] * n
        free = {q: 0.0 for q in Q}
        ready = {k for k in range(n) if not left[k]}
        while ready:
            opt = []
            for k in ready:
                q, t = min(((q, max(free.get(q, 0.0), at[k])) for q in nodes[k][0]), key=lambda x: x[1] + nodes[k][0][x[0]][1])
                opt.append((t, k, q))
            first = min(opt)[0]
            t, k, q = max((o for o in opt if o[0] <= first + SLACK), key=lambda o: (path[o[1]], -o[1]))
            ready.discard(k)
            issue, c = nodes[k][0][q]
            issue()
            if q in free:
                free[q] = t + c - (PIPE if q in SEM else 0.0)
            for x in succ[k]:
                at[x] = max(at[x], t + c + nodes[k][2] + WAKE)
                left[x] -= 1
                if not left[x]:
                    ready.add(x)

    def issue_op(q, call, reads, writes):
        pre(q, reads, writes)
        s = SEM[q]
        if q == "g" and waited[q].get(s, 0) < cnt.get(s, 0):
            g.wait_ge(T.sem[s], cnt[s])
            waited[q][s] = cnt[s]
        i = call()
        cnt[s] = cnt.get(s, 0) + 1
        i.then_inc(T.sem[s], 1)
        post(q, reads, writes, (s, cnt[s]))

    def el(n, f=1.0):
        return PIPE + max(64, n * f) * CYCLE

    def op(q, call, reads, writes, cost):
        note({q: (lambda: issue_op(q, call, reads, writes), cost)}, reads, writes)

    def either(v, a, reads, writes, n):
        note({"v": (lambda: issue_op("v", v, reads, writes), el(n)), "a": (lambda: issue_op("a", a, reads, writes), el(n) + 0.02)}, reads, writes)

    def dma(q, out, in_, reads=(), writes=()):
        def issue():
            pre(q, reads, writes)
            s = "d%d" % nd[0]
            nd[0] += 1
            Q[q].dma_start(out, in_).then_inc(T.sem[s], 16)
            cnt[s] = 16
            post(q, reads, writes, (s, 16))
        note({q: (issue, 0.06)}, reads, writes, (), 2.0)

    def send(moves, sem, reads):
        def issue():
            pre("g", reads, [])
            ls[0] += _remote(g, T, topo, core, moves, sem)
        sent.append(note({"g": (issue, 0.4)}, reads, [], sent[-1:]))

    def arrive(views, sem, total, late):
        def issue():
            cnt[sem] = total
            for v in views:
                acc.setdefault(v[0], []).append((v, True, (sem, total), "r"))
        note({"r": (issue, 0.0)}, [], views, sent[-1:], late)

    def dcol(q, dst, d0, src, s0, n):
        dma(q, _codes(T, dst, d0, d0 + n), _codes(T, src, s0, s0 + n), [X(src, s0, s0 + n)], [X(dst, d0, d0 + n)])
        dma(q, T[dst + "s"][:, d0:d0 + n], T[src + "s"][:, s0:s0 + n], [X(src + "s", s0, s0 + n)], [X(dst + "s", d0, d0 + n)])

    def sc(s):
        return (ap(s), [s]) if isinstance(s, tuple) else (s, [])

    def ts(out, a, s1, op0, s2=None, op1=None):
        p1, r1 = sc(s1)
        p2, r2 = sc(s2)
        if op1 is None:
            op("v", lambda: g.vector.tensor_scalar(ap(out), ap(a), p1, None, op0), [a] + r1, [out], el(width(out)))
        else:
            op("v", lambda: g.vector.tensor_scalar(ap(out), ap(a), p1, p2, op0, op1), [a] + r1 + r2, [out], el(width(out)))

    def tt(out, a, b, o):
        op("v", lambda: g.vector.tensor_tensor(ap(out), ap(a), ap(b), o), [a, b], [out], el(width(out), 2.0))

    def cp(out, a):
        v = lambda: g.vector.tensor_copy(ap(out), ap(a))
        if SCRATCH[out[0]][2] in (F32, BF) and SCRATCH[a[0]][2] in (F32, BF):
            either(v, lambda: g.scalar.activation(ap(out), ap(a), AF.Copy), [a], [out], width(out))
        else:
            op("v", v, [a], [out], el(width(out)))

    def times(out, a, col):
        either(lambda: g.vector.tensor_scalar(ap(out), ap(a), ap(col), None, O.mult), lambda: g.scalar.activation(ap(out), ap(a), AF.Copy, scale=ap(col)), [a, col], [out], width(out))

    def red(out, a, o=O.add, neg=False, ab=False):
        op("v", lambda: g.vector.tensor_reduce(ap(out), ap(a), AxisListType.X, o, negate=neg, apply_absolute_value=ab), [a], [out], el(width(a)))

    def total(out, a):
        either(lambda: g.vector.tensor_reduce(ap(out), ap(a), AxisListType.X, O.add),
               lambda: g.scalar.activation(ap(a), ap(a), AF.Copy, accum_out=ap(out)), [a], [a, out], width(a))

    def tr(out, a):
        op("v", lambda: g.vector.transpose(ap(out), ap(a)), [a], [out], el(width(a)))

    def ms(out, c):
        op("v", lambda: g.vector.memset(ap(out), c), [], [out], el(width(out)))

    def act(out, a, func):
        op("a", lambda: g.scalar.activation(ap(out), ap(a), func), [a], [out], el(width(out)) + 0.02)

    def iota(out, pat, base, cm=0):
        kw = {} if SCRATCH[out[0]][2] == I32 else {"allow_small_or_imprecise_dtypes": True}
        op("g", lambda: g.iota(ap(out), pat, base, cm, **kw), [], [out], 0.13 + 2 * CYCLE * width(out))

    def quant(dst, d0, d1, src, s0, s1):
        op("v", lambda: g.vector.quantize_mx(T[dst][:, d0:d1], T[dst + "s"][:, d0:d1], T[src][:, s0:s1]), [X(src, s0, s1)], [X(dst, d0, d1), X(dst + "s", d0, d1)], 0.07 + 0.00022 * (s1 - s0))

    def mm(bank, n, l, l0, r, r0, start=True, stop=True):
        op("t", lambda: g.tensor.matmul_mx(T[bank][:, 0:n], T[l][:, l0:l0 + 128], T[l + "s"][:, l0:l0 + 128], T[r][:, r0:r0 + n], T[r + "s"][:, r0:r0 + n], start, stop),
           [X(l, l0, l0 + 128), X(l + "s", l0, l0 + 128), X(r, r0, r0 + n), X(r + "s", r0, r0 + n)], [X(bank, 0, n)], PIPE + 0.001 * (n + 16))

    def pick(dst, n, win, a, b, off):
        ov = X(off[0], off[1], off[1] + n // 16)
        op("a", lambda: g.scalar.activation(T[dst + "s"][:, 0:n], T[win + "s"][:, a:b].indirect(ap(ov)), AF.Copy), [X(win + "s", a, b), ov], [X(dst + "s", 0, n)], el(n, 1.5) + 0.02)
        op("v", lambda: g.vector.tensor_copy(T[dst][:, 0:n].bitcast(dt.uint32), T[win][:, a:b].bitcast(dt.uint32).indirect(ap(ov))), [X(win, a, b), ov], [X(dst, 0, n)], el(n, 1.5))

    def send1(x, src, s0, between=lambda: None):
        n, own, ps = NX[x], _owners(x, order), src + "s"
        fo = [r for r in own if r in far]
        p, w = s0 + n * own.index(fo[0]), n * len(fo)
        send([(_codes(T, src, p, p + w), [(hs[0 if x == 2 else 1], _codes(T, "RC%d" % x, 0, w))], e_on)], "qc%d" % x, [X(src, p, p + w)])
        send([(T[ps][:, p:p + w], [(hs[3 if x == 2 else 2], T["RC%ds" % x][:])], e_on)], "qs%d" % x, [X(ps, p, p + w)])
        mc, mp, rd, rp = [], [], [], []
        for i, r in enumerate([r for r in near if r in own]):
            c = s0 + n * own.index(r)
            e = e_off if x == 1 else e_off[2 * i:2 * i + 2]
            mc.append((_codes(T, src, c, c + n), [(T.cores[r], _codes(T, "LD%d" % x, n * me, n * me + n))], e))
            mp.append((T[ps][:, c:c + n], [(T.cores[r], T["LD%ds" % x][:, n * me:n * me + n])], e))
            rd.append(X(src, c, c + n))
            rp.append(X(ps, c, c + n))
        between()
        if mc:
            send(mc, "a%d" % x, rd)
            send(mp, "a%d" % x, rp)
        if me in own:
            dcol("y", "LD%d" % x, n * me, src, s0 + n * own.index(me), n)
            oth = [X(k, n * r, n * r + n) for k in ("LD%d" % x, "LD%ds" % x) for r in range(8) if r != me]
            arrive(oth, "a%d" % x, 7 * 2 * (len(e_off) if x == 1 else 2), LATE["a%d" % x])

    def send2(x):
        n, own = NY[x], _owners(x, order)
        nm, base = LAND[x]
        src = "MG%d" % x
        if me in own:
            c = base + n * own.index(me)
            for s, hc, h, k in ((src, "RW%d" % x, hs[0 if x == 2 else 1], "wc%d"), (src + "s", "RW%ds" % x, hs[3 if x == 2 else 2], "ws%d")):
                code = s == src
                sap = _codes(T, s, 0, n) if code else T[s][:, 0:n]
                dap = _codes(T, nm, c, c + n) if code else T[nm + "s"][:, c:c + n]
                hap = _codes(T, hc, 0, n) if code else T[hc][:]
                send([(sap, [(h, hap)], e_on, k % x), (sap, [(T.cores[r], dap) for r in near], e_off, "b%d" % x)], None, [X(s, 0, n)])
            dcol("y", nm, c, src, 0, n)
        oth = [(base + n * i, r) for i, r in enumerate(own) if r != me]
        arrive([X(k, c, c + n) for k in (nm, nm + "s") for c, r in oth], "b%d" % x, len(oth) * 2 * len(e_off), LATE["b%d" % x])

    def send_scores(k, src, c0, w):
        sap = T[src][:, c0:c0 + w]
        rd = [X(src, c0, c0 + w)]
        fm = (sap, [(h, T["fRS%d" % k][:]) for h in (hs[1:3] if k == 1 else (hs[0], hs[3]))], e_on, "sr%d" % k)
        nm = (sap, [(T.cores[r], T[src][:, c0:c0 + w]) for r in near], e_off, "sn%d" % k)
        for mv in ([fm], [nm]) if k == 1 else ([fm, nm],):
            send(mv, None, rd)
        arrive([X(src, 4 * r, 4 * r + w) for r in near], "sn%d" % k, len(near) * len(e_off), LATE["n%d" % k])
        arrive([X(src, 4 * r, 4 * r + w) for r in far], "sa%d" % k, len(far) * len(e_off), LATE["s%d" % k])

    def load(q, buf, c0, c1, ext):
        dma(q, T[buf][:, c0:c1], ext, [], [X(buf, c0, c1)])

    load("y", "UZ", 4, 8, T.z[:, 0:4])
    load("a", "UZ", 0, 4, T.u[:, 0:4])
    load("y", "BT", 384, 768, T.dm[:])
    load("a", "BT", 0, 384, T.lv[:])
    load("y", "BT", 768, 1152, T.nz[:])
    load("a", "WT", 0, 512, T.w[:])
    iota(X("PI"), [[1, 1]], 0, 1)
    iota(X("fR96"), [[0, 3], [1, 32]], 0)
    iota(X("fROW"), [[16, 6], [0, 2], [1, 16]], 0)
    CT = lambda a, b, r0=0, r1=128: X("fCT", a, b, r0, r1)
    iota(CT(96, 128), [[0, 8], [1, 4]], 4 * m)
    iota(X("fJB"), [[16, 6]], 0)
    e1 = _owners(1, order)
    cl = [order.index(s) % 2 for s in range(8)]
    a0, a1 = -cl[me] % 2, (1 - cl[me]) % 2
    iota(X("fPR"), [[a1 - a0, 2], [0, 2], [2, 16]], a0)
    if me in e1:
        ow = e1.index(me)
        pairs = [(order[2 * q + ow], order[2 * q + 1 - ow]) for q in range(4)]
        for q, (s0, s1) in enumerate(pairs):
            iota(X("fGR", 32 * q, 32 * q + 32), [[2, 16], [1 + 32 * (s1 - s0), 2]], 32 * s0)
    ms(X("ONB"), 1.0)
    ms(X("fON"), 1.0)
    ms(X("HAF"), 0.5)
    ms(CT(192, 320, 0, 64), -1000.0)
    ms(CT(320, 384, 64, 128), -1000.0)
    op("g", lambda: g.affine_select(T.DG[:], T.HAF[:], [[-1, 128]], O.is_equal, 0.0, 0, 1), [X("HAF")], [X("DG")], 0.4)
    for i, k in enumerate((31, 15, 3, 1)):
        op("v", lambda k=k, i=i: g.vector.tensor_scalar(T.PJ[:, i:i + 1], T.PI[:], k, None, O.bitwise_and), [X("PI")], [X("PJ", i, i + 1)], el(1))
    cp(X("fPC", 0, 3), X("PJ", 0, 3))
    cp(X("fPA", 0, 1), X("PJ", 3, 4))
    P32, P16, P4 = X("fPC", 0, 1), X("fPC", 1, 2), X("fPC", 2, 3)
    for a in range(4):
        ts(X("fLC", 0, 1, 32 * a, 32 * a + 32), X("fPC", 0, 1, 32 * a, 32 * a + 32), 32.0 * (a % 2), O.add)
    ts(X("fTL"), X("fR96", 0, 32), X("fLC"), O.add, P32, O.subtract)
    step = 2.0 ** -24
    ms(X("fFT", 0, 96, 64, 128), 1.0)
    ms(X("fFK", 0, 96, 0, 64), 1.0)
    for n, r0 in (("fFT", 0), ("fFK", 64)):
        v = X(n, 0, 96, r0, r0 + 64)
        ts(v, X("fR96", 0, 96, r0, r0 + 64), X("fPC", 0, 1, r0, r0 + 64), O.is_lt, -step, O.mult)
        ts(v, v, 1.0, O.add)
    for b in range(3):
        ts(X("fPC", 3 + b, 4 + b), P32, 32.0 * b, O.add)
    cp(X("fUZ"), X("UZ"))
    for nm, c, q in (("ZT", 4, "ZQ"), ("UT", 0, "UQ")):
        for t in range(4):
            times(X(nm, t, 512, 0, 128, 4), X("ONB"), X("fUZ", c + t, c + t + 1))
        quant(q, 0, 128, nm, 0, 512)
    quant("QT", 0, 288, "BT", 0, 1152)
    mm("p0", 192, "ZQ", 0, "QT", 0)
    mm("p1", 128, "UQ", 0, "QT", 0)
    act(X("fK0", 0, 96, 0, 64), X("p0", 96, 192, 0, 64), AF.Abs)
    act(X("fK0", 0, 96, 64, 128), X("p1", 0, 96, 64, 128), AF.Abs)
    act(X("fK0", 96, 192), X("p0", 0, 96), AF.Abs)
    low = 2.0 ** -110
    ts(X("fKK", 0, 96, 0, 64), X("fK0", 0, 96, 0, 64), low, O.max)
    ts(X("fKK", 0, 96, 64, 128), X("fK0", 0, 96, 64, 128), -1.0, O.mult, -low, O.min)
    ts(X("fKK", 96, 192), X("fK0", 96, 192), low, O.max)
    tr(X("fTT"), X("fKK"))
    tt(X("fKF"), X("fKK", 0, 96), X("fFK"), O.mult)
    tt(X("fTF"), X("fTT", 0, 96), X("fFT"), O.mult)
    for b in range(3):
        s = X("fTT", 32 * b, 32 * b + 1)
        if b:
            ts(X("fCL", 96 * b, 96 * b + 32 * b), X("fKK", 0, 32 * b), s, O.is_ge)
        if b < 2:
            ts(X("fCL", 96 * b + 32 * b + 32, 96 * b + 96), X("fKK", 32 * b + 32, 96), s, O.is_gt)
        tt(X("fCL", 128 * b, 128 * b + 32), X("fKF", 32 * b, 32 * b + 32), X("fTF", 32 * b, 32 * b + 32), O.is_gt)
    for b in range(3):
        total(X("fRB", b, b + 1), X("fCL", 96 * b, 96 * b + 96))
    for i, val in enumerate((lambda b: X("fTT", 32 * b, 32 * b + 1), lambda b: X("fPC", 3 + b, 4 + b), lambda b: X("fTT", 96 + 32 * b, 97 + 32 * b))):
        for b in range(3):
            ts(X("fHL", 96 * i + 32 * b, 96 * i + 32 * b + 32), X("fTL"), X("fRB", b, b + 1), O.is_equal, val(b), O.mult)
        tr(X("fHT", 96 * i, 96 * i + 96), X("fHL", 96 * i, 96 * i + 96))
        total(X("fSD", 4 * me + i, 4 * me + i + 1), X("fHT", 96 * i, 96 * i + 96))
    send_scores(1, "fSD", 4 * me, 1)

    B0 = lambda n, c0=0, c1=None: X(n, c0, c1, 0, 32)
    ts(B0("fPM"), B0("fPR"), B0("fPC", 0, 1), O.is_equal)
    times(B0("fHP"), B0("fPM"), B0("fSD", 4 * me + 1, 4 * me + 2))
    tr(B0("fHPt"), B0("fHP"))
    total(B0("fDL", 0, 1), B0("fHPt", 0, 32))
    total(B0("fDL", 1, 2), B0("fHPt", 32, 64))
    for d in range(4):
        cp(("DPo", 0, 2, 32 * d, 32 * d + 32, 1), ("fW",) + X("fDL")[1:3] + (0, 32, 1))
    pick("SL1", 32, "QT", 96, 192, ("DPo", 0))
    send1(1, "SL1", 0)

    LCv = X("fLC")
    ts(CT(0, 64), X("fROW", 0, 64), LCv, O.subtract)
    ts(CT(64, 96), X("fR96", 0, 32), LCv, O.subtract)
    ts(CT(128, 160), X("fR96", 0, 32), LCv, O.subtract, 32.0, O.add)
    ts(CT(96, 128), CT(96, 128), P32, O.is_equal)
    x2 = _owners(2, order)
    if me in x2:
        ts(X("fMM", 0, 32), X("fROW", 0, 32), 16.0 * (x2.index(me) % 2), O.add, P32, O.is_equal)
    ts(X("fGV", 0, 1), X("fSD", 4 * me + 1, 4 * me + 2), 128.0 * me, O.add)
    cp(X("fGV", 1, 2, 32, 64), X("fGV", 0, 1, 32, 64))
    cp(X("fGV", 1, 2, 64, 128), X("fGV", 0, 1, 64, 128))
    ts(B0("fNS2"), B0("fPA", 0, 1), float(cl[me]), O.not_equal, 1024.0, O.mult)
    tt(B0("fGV", 1, 2), B0("fGV", 0, 1), B0("fNS2"), O.add)
    ms(X("fNL", 4 * me, 4 * me + 1, 96, 128), 0.0)
    for h in range(2):
        ts(X("fKC", h, h + 1), P16, 16.0 * h, O.add)
        ts(X("fKM", 32 * h, 32 * h + 32), X("fR96", 0, 32), X("fKC", h, h + 1), O.is_equal, 64.0, O.mult)
        ts(X("fOT", 32 * h, 32 * h + 32), X("fR96", 0, 32), X("fKC", h, h + 1), O.is_lt)
    tt(X("fKM"), X("fKM"), X("fOT"), O.add)
    if me in e1:
        par, npar = B0("fPA", 0, 1), B0("fPA", 1, 2)
        ts(npar, par, -1.0, O.mult, 1.0, O.add)
        ts(B0("fPA", 2, 3), B0("fPC", 0, 1), 0.5, O.mult)
        for q, (s0, s1) in enumerate(pairs):
            ts(B0("fAD", q, q + 1), par, 16.0 * (s1 - s0) - 0.5, O.mult, 16.0 * s0, O.add)
            tt(B0("fAD", q, q + 1), B0("fAD", q, q + 1), B0("fPA", 2, 3), O.add)
            ts(B0("fGP", q, q + 1), par, 32.0 * (s1 - s0), O.mult, B0("fPC", 0, 1), O.add)
            ts(B0("fGP", q, q + 1), B0("fGP", q, q + 1), 32.0 * s0, O.add)
            ff = B0("fFF", 128 * q, 128 * q + 128)
            ts(ff, B0("fGR"), B0("fGP", q, q + 1), O.is_ge, -step, O.mult)
            ts(ff, ff, 1.0, O.add)
    ts(CT(192, 320, 64, 128), X("fROW", 0, 128, 64, 128), X("fLC", 0, 1, 64, 128), O.subtract)
    ts(CT(320, 384, 0, 64), X("fROW", 0, 64, 0, 64), X("fLC", 0, 1, 0, 64), O.subtract, 32.0, O.add)
    ts(X("fPT"), X("fROW"), 128.0 * me, O.add)
    ts(X("fJB"), X("fJB"), P16, O.add)
    ts(X("fRP", 0, 64), X("fROW", 0, 64), P32, O.subtract)
    ts(X("fRP", 64, 96), X("fR96", 0, 32), P32, O.subtract)
    ms(X("fVO", 0, 1, 0, 64), 96.0)
    ms(X("fVO", 0, 1, 64, 128), 0.0)
    for b in range(8):
        ms(X("ET", 256 * b, 256 * b + 256), 0.0)
    for b in range(4):
        cp(X("ET", 513 * b, 512 * b + 512, 0, 128, 4), X("DG"))
    for b in range(4):
        quant("EQ", 128 * b, 128 * b + 128, "ET", 512 * b, 512 * b + 512)
    quant("WQ", 0, 128, "WT", 0, 512)
    ms(X("FLo", 6, 8), 0)
    for d in ("UD", "NP1", "BP2", "NP2"):
        dcol("y", d, 32, "QT", 0, 96)
    dcol("y", "DW", 0, "QT", 96, 96)

    def key(s):
        return X("fSD", 4 * s, 4 * s + 1)

    def rows4(v, a):
        return (v[0], v[1], v[2], 32 * a, 32 * a + 32, v[5])

    def to_all(out, src, a):
        for d in range(4):
            cp(rows4(out, d), rows4(src, a))

    times(X("fEO"), X("fON"), key(me))
    tr(X("fRO"), X("fEO"))
    planes = (pa, pb) if rank in pa else (pb, pa)
    for i, grp in enumerate((near, far)):
        n, pl = 32 * len(grp), planes[i]
        for a in range(4):
            cp(X("fSWA", 4 * i, 4 * i + 4, 32 * a, 32 * a + 32), ("fSD", 4 * pl[0], 4 * pl[-1] + 1, 32 * (a ^ 1), 32 * (a ^ 1) + 32, 4 * (pl[1] - pl[0])))
        for j, s in enumerate(grp):
            o = O.is_le if s < me else O.is_lt
            w = 4 * i + pl.index(s)
            ts(X("fCW", 128 * i + 32 * j, 128 * i + 32 * j + 32), X("fRO"), key(s), o)
            ts(X("fCX", 128 * i + 32 * j, 128 * i + 32 * j + 32), X("fRO"), X("fSWA", w, w + 1), o)
        for k, (w, v) in enumerate((("fCW", "fCV"), ("fCX", "fCY"))):
            tr(X(v, 128 * i, 128 * i + n), X(w, 128 * i, 128 * i + n))
            total(X("fNF", 2 * k + i, 2 * k + i + 1), X(v, 128 * i, 128 * i + n))
        if i == 0:
            ts(X("fCTO"), CT(0, 64), X("fNF", 0, 1), O.subtract)
            tt(X("fNF", 2, 3), X("fNF", 0, 1), X("fNF", 2, 3), O.add)
    ts(X("fCN"), X("fNF", 0, 1), X("fNF", 1, 2), O.add)
    ts(X("fCF"), X("fNF", 2, 3), X("fNF", 1, 2), O.add, X("fNF", 3, 4), O.add)
    NL = lambda a, n="fNL": X(n, 4 * me, 4 * me + 1, 32 * a, 32 * a + 32)
    T4 = lambda a, c: X("fT4", c, c + 1, 32 * a, 32 * a + 32)
    TS = lambda a, c: X("fTS", c, c + 1, 32 * a, 32 * a + 32)
    entries = lambda i, t, n, v: ts(X("fHN", 32 * i, 32 * i + 32), t, X(n), O.is_equal, v, O.mult)
    entries(0, CT(64, 96), "fCN", X("fGV", 1, 2))
    entries(1, CT(64, 96), "fCN", X("fSD", 4 * me + 2, 4 * me + 3))
    tr(X("fHM", 0, 64), X("fHN", 0, 64))
    for a in (0, 2):
        total(NL(a), X("fHM", 0, 32, 32 * a, 32 * a + 32))
    total(T4(2, 0), X("fHM", 32, 64, 64, 96))
    cp(NL(1), T4(2, 0))
    send_scores(3, "fNL", 4 * me, 1)

    if me in e1:
        nq = [2 * ow, 2 * ow + 1]
        n0, f0 = 64 * ow, 64 - 64 * ow
        for q in nq + [q for q in range(4) if q not in nq]:
            k4 = B0("fK4", q, q + 1)
            times(B0("fKT", q, q + 1), par, B0("fSD", 4 * pairs[q][1], 4 * pairs[q][1] + 1))
            ts(k4, npar, B0("fSD", 4 * pairs[q][0], 4 * pairs[q][0] + 1), O.mult, B0("fKT", q, q + 1), O.add)
            times(B0("fKE", 32 * q, 32 * q + 32), B0("fON"), k4)
            if q % 2:
                tr(B0("fKR", 32 * q - 32, 32 * q + 32), B0("fKE", 32 * q - 32, 32 * q + 32))

        def ahead(q, c0, c1, out):
            w, c = B0("fWW", 128 * q + c0, 128 * q + c1), B0("fCC", 128 * q + c0, 128 * q + c1)
            tt(w, B0("fKR", c0, c1), B0("fFF", 128 * q + c0, 128 * q + c1), O.mult)
            ts(c, w, B0("fK4", q, q + 1), O.is_ge)
            total(out, c)

        for i, q in enumerate(nq):
            ahead(q, n0, n0 + 64, B0("fN1", q, q + 1))
            ts(B0("fCO", 64 * i, 64 * i + 64), B0("fROW", 0, 64), B0("fN1", q, q + 1), O.subtract)
        for q in range(4):
            if q in nq:
                ahead(q, f0, f0 + 64, B0("fRB2", q, q + 1))
            else:
                ahead(q, 0, 128, B0("fRB2", q, q + 1))
            for h in range(2):
                t = B0("fCO", 64 * nq.index(q) + 32 * h, 64 * nq.index(q) + 32 * h + 32) if q in nq else B0("fROW", 32 * h, 32 * h + 32)
                ts(B0("fHO", 128 * h + 32 * q, 128 * h + 32 * q + 32), t, B0("fRB2", q, q + 1), O.is_equal, B0("fAD", q, q + 1), O.mult)
        for h in range(2):
            tr(B0("fHQ", 128 * h, 128 * h + 128), B0("fHO", 128 * h, 128 * h + 128))
            total(B0("fMO", h, h + 1), B0("fHQ", 128 * h, 128 * h + 128))
        for d in range(4):
            cp(("O1o", 0, 2, 32 * d, 32 * d + 32, 1), B0("fMO"))
        pick("MG1", 32, "LD1", 0, 128, ("O1o", 0))
    send2(1)

    entries(2, CT(128, 160), "fCF", X("fGV", 0, 1))
    entries(3, CT(128, 160), "fCF", key(me))
    tr(X("fHM", 64, 128), X("fHN", 64, 128))
    for i in (2, 3):
        total(X("fT4", i, i + 1), X("fHM", 32 * i, 32 * i + 32))
    for a in range(4):
        c = 2 if a % 2 else 3
        cp(TS(a, c - 2), T4(a ^ 1, c))
        tt(NL(a, "fNM"), T4(a, c), TS(a, c - 2), O.add)
    send_scores(4, "fNM", 4 * me, 1)

    ts(X("fH1"), X("fCTO"), X("fNF", 1, 2), O.is_equal, X("fSD", 4 * me + 1, 4 * me + 2), O.mult)
    tr(X("fH1t"), X("fH1"))
    total(X("fOL", 0, 1), X("fH1t", 0, 32))
    total(X("fOL", 1, 2), X("fH1t", 32, 64))

    def owners(parts, mul, add, i):
        n = len(parts)
        for j, (mask, col) in enumerate(parts):
            ts(X("fMW", 128 * i + 32 * j, 128 * i + 32 * j + 32), mask, col, O.mult)
        tr(X("fMV", 128 * i, 128 * i + 32 * n), X("fMW", 128 * i, 128 * i + 32 * n))
        red(X("fOM", 2 * i, 2 * i + 1), X("fMV", 128 * i, 128 * i + 32 * n))
        ts(X("fOM", 2 * i + 1, 2 * i + 2), X("fOM", 2 * i, 2 * i + 1), 63.5, O.subtract, 1.0 / 128, O.mult)
        cp(X("MI", i, i + 1), X("fOM", 2 * i + 1, 2 * i + 2))
        ts(X("Mo", 2 * i, 2 * i + 1), X("MI", i, i + 1), float(mul), O.mult, add, O.add)

    tt(X("fVO", 1, 2), X("fVO", 0, 1), X("fSD", 4 * me + 1, 4 * me + 2), O.add)
    ts(X("fH2"), CT(192, 384), X("fCF"), O.is_equal, X("fVO", 1, 2), O.mult)
    tr(X("fH2t"), X("fH2"))
    for c in range(6):
        total(X("fOX", c, c + 1), X("fH2t", 32 * c, 32 * c + 32))
    for a in range(4):
        to_all(X("fXO", 6 * a, 6 * a + 6), X("fOX"), a)
    tt(X("fXP", 0, 12), X("fXO", 0, 12), X("fXO", 12, 24), O.add)
    tt(X("fXP", 12, 18), X("fXP", 0, 6), X("fXP", 6, 12), O.add)
    cp(X("X2o"), X("fXP", 12, 18))
    pick("SL2", 96, "QT", 0, 192, ("X2o", 0))
    send1(2, "SL2", 0)

    L1q, L2g, D1g, H2g = (X("fG4", i, i + 1) for i in range(4))
    red(X("fG2", 0, 1), ("fNL", 0, 32, 0, 128, 4))
    DQ = X("fDQ")
    to_all(DQ, X("fG2", 0, 1), 0)
    ts(X("fOE"), X("fON"), DQ, O.mult, 1024.0, O.is_ge)
    tr(X("fOR"), X("fOE"))
    for h in range(2):
        tt(X("fOT", 32 * h, 32 * h + 32), X("fOR"), X("fKM", 32 * h, 32 * h + 32), O.mult)
        total(X("fQ1", h, h + 1), X("fOT", 32 * h, 32 * h + 32))
    tt(X("fQA"), X("fKC"), X("fQ1"), O.subtract)
    for h in range(2):
        ts(X("UOo", h, h + 1), X("fQ1", h, h + 1), 46.0, O.subtract, X("fQA", h, h + 1), O.max)
    pick("UD", 32, "UO", 0, 36, ("UOo", 0))
    red(X("fG2", 1, 2), ("fNM", 0, 32, 0, 128, 4))
    for a in range(4):
        to_all(X("fGA", 2 * a, 2 * a + 2), X("fG2"), a)
    _, c2k, z1, c2g, L1g, o2k, _, o2g = (X("fGA", i, i + 1) for i in range(8))
    ts(D1g, DQ, 1024.0, O.is_ge, -1024.0, O.mult)
    tt(D1g, D1g, DQ, O.add)

    to_all(X("LPo"), X("fOL"), 2)
    pick("NP1", 32, "QT", 192, 288, ("LPo", 0))
    for b in range(4):
        mm("p%d" % (2 + b), 128, "EQ", 128 * b, "NP1", 0, True, False)
    ts(X("fOW", 0, 1), L1g, 128.0 * me, O.is_ge)
    ts(X("fOW", 1, 2), L1g, 128.0 * me + 128, O.is_lt)
    tt(X("fOW", 2, 3), X("fOW", 0, 1), X("fOW", 1, 2), O.mult)
    ts(X("fIDW"), X("fR96", 0, 32), P32, O.is_equal, X("fOW", 2, 3), O.mult)
    if me in x2:
        owners([(X("fMM", 0, 32), (L1g, o2g, c2g)[x2.index(me) // 2])], 16, P16, 2)
    owners([(CT(96, 128), L1g)], 4, P4, 1)

    def new(nt, q0):
        for b in range(4):
            cp(X(nt, b, 512, 0, 128, 4), X("p%d" % (2 + b), 0, 128))
        quant("QT", q0, q0 + 128, nt, 0, 512)

    for b in range(4):
        mm("p%d" % (2 + b), 128, "EQ", 128 * b, "UD", 0, False, True)
    new("NT0", 288)
    mm("p6", 128, "UQ", 0, "QT", 288)
    tt(X("fSC"), X("p6", 0, 32), X("fIDW"), O.mult)
    red(X("fNK", 4 * me, 4 * me + 1), X("fSC"), O.add, True, True)
    send1(3, "QT", 288, lambda: send_scores(2, "fNK", 4 * me, 1))
    if me in x2:
        pick("MG2", 16, "LD2", 0, 128, ("Mo", 4))
    send2(2)

    tiles = {"": ("fEP", "fEQr", "fMK", "fMG", "fMT", "fMH", "fML")}
    tiles["b"] = tuple(n + "b" for n in tiles[""])

    def prep(w, ak, ag, bg):
        e, r, k, gl = tiles[w][:4]
        for i, c in enumerate((ak, ag, bg)):
            times(X(e, 32 * i, 32 * i + 32), X("fON"), c)
        tr(X(k, 32, 64), X(e, 0, 32))
        tr(X(r, 0, 64), X(e, 32, 96))
        o = O.is_lt if w else O.is_ge
        ts(X(gl, 0, 32), X(r, 32, 64), ag, o, -step, O.mult)
        ts(X(gl, 32, 96), X(r, 0, 64), bg, o, -step, O.mult)
        ts(X(gl, 0, 96), X(gl, 0, 96), 1.0, O.add)

    def ranks(w, ak, bk, raw, cut):
        e, r, k, gl, t, h, ml = tiles[w]
        if cut is None:
            ts(X(e, 96, 128), X("fON"), raw, O.mult)
        else:
            ts(X(e, 96, 128), X("fON"), raw, O.mult, cut, O.min)
        tr(X(k, 64, 96), X(e, 96, 128))
        tt(X(t, 0, 32), X(k, 64, 96), X(gl, 0, 32), O.mult)
        tt(X(t, 32, 96), X(k, 32, 96), X(gl, 32, 96), O.mult)
        o = O.is_gt if w else O.is_ge
        ts(X(t, 96, 128), X(t, 0, 32), ak, o)
        ts(X(t, 128, 192), X(t, 32, 96), bk, o)
        total(X(ml, 0, 1), X(t, 96, 128))
        total(X(ml, 1, 2), X(t, 128, 192))

    def hot(w, at, wide, va, vb, outs):
        e, r, k, gl, t, h, ml = tiles[w]
        n = 64 if wide else 32
        for i in range(n // 32):
            ra = X("fRP", 32 * i, 32 * i + 32) if wide else X("fRP", 64, 96)
            rb = X("fROW", 32 * i, 32 * i + 32) if wide else X("fR96", 0, 32)
            o = at + 64 * i
            ts(X(h, o, o + 32), ra, X(ml, 0, 1), O.is_equal, va, O.mult)
            ts(X(h, o + 32, o + 64), rb, X(ml, 1, 2), O.is_equal, vb, O.mult)
        tr(X(h, at + 2 * n, at + 4 * n), X(h, at, at + 2 * n))
        for i, o in enumerate(outs):
            total(o, X(h, at + 2 * n + 64 * i, at + 2 * n + 64 * i + 64))

    def pc(i, v):
        ts(X("fFM", i, i + 1), P32, float(v), O.add)
        return X("fFM", i, i + 1)

    def final(i, gcol, acol, out):
        ts(X("fFH", 192 * i, 192 * i + 192), X("fPT"), gcol, O.is_equal, acol, O.mult)
        tr(X("fFT%d" % i), X("fFH", 192 * i, 192 * i + 192))
        for c in range(6):
            total(X("fFR", 6 * i + c, 6 * i + c + 1), X("fFT%d" % i, 32 * c, 32 * c + 32))
        tt(out, X("fFR", 6 * i, 6 * i + 6), out, O.max)

    prep("", c2k, c2g, D1g)
    ranks("", c2k, z1, z1, None)
    hot("", 0, True, pc(0, 64), P32, [X("fML", 4, 5), X("fML", 5, 6)])
    cp(X("B2o"), X("fML", 4, 6))
    prep("b", o2k, o2g, L1g)
    hot("", 256, False, c2g, D1g, [H2g])
    cp(X("fFL"), X("fJB"))
    cp(X("fFD"), X("fJB"))
    final(0, L1g, pc(1, 288), X("fFL"))
    final(1, D1g, pc(2, 96), X("fFD"))
    a416, a128, a192 = pc(3, 416), pc(4, 128), pc(5, 192)

    red(X("fNB"), ("fNK", 0, 32, 0, 128, 4))
    ts(X("fNS", 1, 2), X("fNB"), -low, O.min)
    ranks("b", o2k, X("fNS", 1, 2), X("fNB"), -low)
    hot("b", 0, True, o2g, L1g, [X("fMLb", 4, 5), X("fMLb", 5, 6)])
    ts(X("N2o"), X("fMLb", 4, 6), 128.0 * me, O.subtract, 95.0, O.min)
    pick("BP2", 32, "DW", 96, 192, ("B2o", 0))
    for b in range(4):
        mm("p%d" % (2 + b), 128, "EQ", 128 * b, "BP2", 0, True, False)
    pick("NP2", 32, "QT", 192, 288, ("N2o", 0))
    for b in range(4):
        mm("p%d" % (2 + b), 128, "EQ", 128 * b, "NP2", 0, False, True)
    pick("MG3", 16, "LD3", 0, 32, ("Mo", 2))
    send2(3)
    hot("b", 256, False, o2g, L1g, [L2g])
    final(2, L2g, a416, X("fFL"))
    cp(X("FLo", 0, 6), X("fFL"))
    new("NT1", 416)
    pick("LF", 128, "QT", 0, 544, ("FLo", 0))
    mm("p7", 128, "WQ", 0, "LF", 0)
    dma("y", T.oc[:, 0:384], _codes(T, "LF", 0, 96), [X("LF", 0, 96)], [])
    for k in range(4):
        dma("y", T.osc[4 * k:4 * k + 4, 0:96], T.LFs[32 * k:32 * k + 4, 0:96], [X("LFs", 0, 96)], [])
    cp(X("fY"), X("p7", 0, 96))
    dma("a", T.y[:], T.fY[:], [X("fY")], [])

    hot("b", 384, False, a128, a192, [X("fMLb", 6, 7)])
    final(3, H2g, X("fMLb", 6, 7), X("fFD"))
    cp(X("FDo"), X("fFD"))
    pick("DF", 96, "DW", 0, 224, ("FDo", 0))
    dma("y", T.oc[:, 384:768], _codes(T, "DF", 0, 96), [X("DF", 0, 96)], [])
    for k in range(4):
        dma("a" if k % 2 else "y", T.osc[4 * k:4 * k + 4, 96:192], T.DFs[32 * k:32 * k + 4, 0:96], [X("DFs", 0, 96)], [])
    cp(L1q, L1g)
    cp(X("GI"), X("fG4", 0, 4))
    op("v", lambda: g.vector.tensor_scalar(T.GJ[:], T.GI[:], 7, None, O.arith_shift_right), [X("GI")], [X("GJ")], el(1))
    ts(X("GK"), X("GJ"), -32, O.mult)
    ms(X("fG4t", 0, 32), 0.0)
    tt(X("fG4t", 0, 4), X("GI"), X("GK"), O.add)
    tr(X("fG4t", 32, 64), X("fG4t", 0, 32))
    dma("a", T.lw[:], T.fG4t[0:2, 32:64], [X("fG4t", 32, 64)], [])
    dma("a", T.sw[:], T.fG4t[2:4, 32:64], [X("fG4t", 32, 64)], [])
    schedule()
    cnt["ls"] = ls[0]
    for s in sorted(cnt):
        if waited["g"].get(s, 0) < cnt[s]:
            g.wait_ge(T.sem[s], cnt[s])
